import numpy as np, ml_dtypes
CORES = [9,25,41,57]
N = 4
BF = ml_dtypes.bfloat16
def gentries(a):
    return np.ascontiguousarray(a.reshape(8, 16, -1).transpose(0, 2, 1)).reshape(8, -1)
def gtable(e):
    e = np.asarray(e); return np.ascontiguousarray(e.reshape(8, -1, 16).transpose(0, 2, 1)).reshape(128, -1).astype(np.int32)
W, K, TV, S, RO, QV = 3072, 768, 4, 1, 3, 17
CH = 16
def sgn(rng, *shape):
    return 2.0 * rng.integers(0, 2, shape) - 1.0
def pay(rng, *shape):
    return sgn(rng, *shape) * (0.5 + 0.5 * rng.random(shape))
def weights(rng, *shape):
    return (0.25 + 0.75 * rng.random(shape)) * (rng.random(shape) > 0.0625)
def names(rng):
    o = np.argsort(rng.random((N, 8, TV, W)), axis=-1)[..., :2 * K]
    return o[..., :K].copy(), o[..., K:].copy()
def plain(rng):
    th = pay(rng, N, 8, 16, W); va = 0.875 * th + pay(rng, N, 8, 16, W)
    a, b = names(rng)
    return th, va, pay(rng, N, 8, 16, K), weights(rng, N, 8, 16, K), a, b
def put(x):
    x = np.where(np.abs(x) < 2.0 ** -20, 0.0, x)
    return np.ascontiguousarray(x.reshape(N, 128, -1)).astype(np.float32).astype(BF)
def near(x):
    return np.where(np.abs(x) < 2.0 ** -20, 0.0, x).astype(np.float32).astype(BF).astype(np.float64)
def pack(th, va, yt, wt, a, b):
    return {"th": put(th), "va": put(va), "yt": put(yt), "wt": put(wt), "an": np.stack([gtable(v.reshape(8, TV * K)) for v in a]),
            "bn": np.ascontiguousarray(b.reshape(N, 8 * TV, K)).astype(np.int32)}
def residues(rng, x, g):
    th, va, yt, wt, a, b = x; n = 2 * (K // TV); top = TV * (TV - 1) // 2
    fac = np.concatenate([np.arange(1, TV), np.array([-top])])
    m = rng.integers(128, 192, (16, n)); k = rng.integers(1, 63 // top + 1, (16, n)) * (2 * rng.integers(0, 2, (16, n)) - 1); s = sgn(rng, 16, n) * 2.0 ** -8
    col = np.stack([rng.permutation(W)[:2 * K].reshape(TV, n) for q in range(N)])
    wt[:, g] = 0.0
    for q in range(N):
        for i in range(TV):
            th[q, g][:, col[q, i]] = s * m; va[q, g][:, col[q, i]] = s * (m - fac[i] * k)
    for r in range(N):
        js = rng.permutation(K).reshape(TV, K // TV)
        for i in range(TV):
            sl = rng.permutation(n)
            for t in range(TV):
                v = col[(r + S * t) % N, (i + t) % TV][sl]
                a[r, g, t, js[i]] = v[:K // TV]; b[r, g, t, js[i]] = v[K // TV:]
def first(tab, va, yt, wt, a, b):
    fa = np.zeros((TV, N, 16, K)); fb = np.zeros((TV, N, 16, K)); keep = []; tab = tab.copy()
    for t in range(TV):
        own = (np.arange(N) - S * t) % N; i1 = a[own, t][:, None, :]; i2 = b[own, t][:, None, :]
        p1 = np.take_along_axis(tab, i1, 2); p2 = np.take_along_axis(tab, i2, 2)
        er = p1 * p2 - yt[own]; w8 = 0.125 * wt[own]
        np.put_along_axis(tab, i1, p1 - w8 * er * p2, 2); np.put_along_axis(tab, i2, p2 - w8 * er * p1, 2)
        fa[t][own] = 0.125 * er * p2; fb[t][own] = 0.125 * er * p1
        keep.append((own, i1, i2, w8, p1, p2, er))
    dd = tab - va; hh = np.zeros((N, 16, K))
    for t in range(TV - 1, -1, -1):
        own, i1, i2, w8, p1, p2, er = keep[t]
        d1 = np.take_along_axis(dd, i1, 2); d2 = np.take_along_axis(dd, i2, 2); mm = p1 * p2 + er
        hh[own] = hh[own] - fa[t][own] * d1 - fb[t][own] * d2
        np.put_along_axis(dd, i1, d1 - w8 * (p2 * p2 * d1 + mm * d2), 2); np.put_along_axis(dd, i2, d2 - w8 * (mm * d1 + p1 * p1 * d2), 2)
    return hh, fa, fb
def knots(rng, x, g):
    th, va, yt, wt, a, b = x; M = min(K // 3, (W - 2 * K) // (2 * (TV - 1))); n = 2 * M * (TV - 1)
    cols = np.stack([rng.permutation(W) for q in range(N)]); prv = cols[:, :n].reshape(N, TV - 1, 2, M)
    js = np.stack([rng.permutation(K) for q in range(N)])
    for q in range(N):
        th[q, g][:, prv[q, :, 0].reshape(-1)] = sgn(rng, 16, n // 2) * (0.75 + 0.25 * rng.random((16, n // 2)))
        th[q, g][:, prv[q, :, 1].reshape(-1)] = 0.0625 * pay(rng, 16, n // 2)
        va[q, g][:, cols[q, :n]] = 0.0
    for r in range(N):
        for t in range(TV):
            q = (r + S * t) % N; v = rng.permutation(cols[q, n:]); k = 0 if t == 0 else M; i = js[r, k:]
            a[r, g, t, i] = v[:K - k]; b[r, g, t, i] = v[K - k:2 * (K - k)]
            if t > 0:
                a[r, g, t, js[r, :M]] = prv[q, t - 1, 0]; b[r, g, t, js[r, :M]] = prv[q, t - 1, 1]
    for z in (th, va, yt, wt): z[:, g] = near(z[:, g])
    hh, fa, fb = first(th[:, g], va[:, g], yt[:, g], wt[:, g], a[:, g], b[:, g])
    for r in range(N):
        o = js[r, :M]; rest = hh[r][:, o]
        for f, side in ((fb, 1), (fa, 0)):
            for t in range(1, TV):
                q = (r + S * t) % N; cf = f[t, r][:, o]
                v = near(np.clip(np.divide(-rest, cf), -2.0, 2.0))
                va[q, g][:, prv[q, t - 1, side]] = v; rest = rest + cf * v
def links(rng):
    n = 2 ** 19; one = np.float32; c = one(0.125)
    w0 = near(0.75 + 0.25 * rng.random(n)).astype(one); w1 = near(0.5 + 0.5 * rng.random(n)).astype(one)
    y0 = near(1.5 + 0.5 * rng.random(n)).astype(one); p = near(1.5 + 0.5 * rng.random(n)).astype(one)
    u1 = c * (w0 * (y0 * p)); pr = u1 * p; p64 = pr.astype(np.float64)
    y1 = near(np.minimum(1.0 + p64 + np.minimum(p64, 1.0 - p64) * rng.random(n), 2.0)).astype(one)
    er = pr - y1; u2 = u1 - c * (w1 * (er * p)); p2 = p - c * (w1 * (er * u1)); m = pr + er; wrong = one(2) * er + y1
    k = 0.125 * w1.astype(np.float64); s = 1.0 - k * p.astype(np.float64) * p.astype(np.float64); km = k * np.where(m == 0, one(1), m).astype(np.float64)
    vu = near(np.clip(u2 - np.divide(km * p2, s), -2.0, 2.0)).astype(one); d1 = u2 - vu
    vv = near(np.clip(p2 - np.divide(d1 * s, km), -2.0, 2.0)).astype(one); d2 = p2 - vv
    x1 = d1 - c * (w1 * ((p * p) * d1 + m * d2)); x2 = d1 - c * (w1 * ((p * p) * d1 + wrong * d2))
    hit = np.flatnonzero((x1 > 0) & (x2 <= 0))
    if len(hit) == 0: hit = np.array([int(np.argmin(np.abs(x1)))])
    i = hit[rng.integers(0, len(hit), (N, CH, 16))]; s1 = sgn(rng, N, CH, 16); s2 = sgn(rng, N, CH, 16)
    return s1 * y0[i], w0[i], s1 * y1[i], w1[i], s2 * p[i], s1 * s2 * vu[i], s2 * vv[i]
def halves(rng, x, g):
    th, va, yt, wt, a, b = x; y0, w0, y1, w1, p, vu, vv = links(rng); n = K - 2 * CH
    cols = np.stack([rng.permutation(W) for q in range(N)]); js = np.stack([rng.permutation(K) for q in range(N)])
    for q in range(N):
        u = cols[q, :CH]; v = cols[q, CH:2 * CH]; z = cols[q, 2 * CH:6 * CH]; r = (q - S) % N; j0 = js[q, :CH]; j1 = js[r, CH:2 * CH]
        th[q, g][:, z] = 0.0; va[q, g][:, z] = 0.0
        th[q, g][:, u] = 0.0; va[q, g][:, u] = vu[q].T
        th[q, g][:, v] = p[q].T; va[q, g][:, v] = vv[q].T
        yt[q, g][:, j0] = y0[q].T; wt[q, g][:, j0] = w0[q].T
        yt[r, g][:, j1] = y1[q].T; wt[r, g][:, j1] = w1[q].T
    for r in range(N):
        for t in range(TV):
            q = (r + S * t) % N; z = rng.permutation(cols[q, 2 * CH:6 * CH]); v = rng.permutation(cols[q, 6 * CH:])
            a[r, g, t, js[r, 2 * CH:]] = v[:n]; b[r, g, t, js[r, 2 * CH:]] = v[n:2 * n]
            for i in range(2):
                j = js[r, i * CH:(i + 1) * CH]; o = z[2 * CH * i:2 * CH * (i + 1)]
                if t == i: o = cols[q, :2 * CH]
                a[r, g, t, j] = o[:CH]; b[r, g, t, j] = o[CH:]
def setup_inputs(rng):
    return pack(*plain(rng))
def sized(rng, n):
    return sgn(rng, N, 8, 16, n) * (0.8 + 0.2 * rng.random((N, 8, 16, n))) * rng.choice(np.array([0.625, 0.8, 1.0]), (N, 8, 1, n))
def setup_inputs_spread(rng):
    u = rng.random((N, 8, 1, W))
    th = sized(rng, W)
    th = np.where(u < 0.03, 2.0 ** -20 * sgn(rng, N, 8, 16, W), np.where(u > 0.98, 0.0, th))
    va = 0.875 * th + sized(rng, W)
    va = np.where((u > 0.5) & (u < 0.53), 0.0, va)
    yt = sized(rng, K)
    yt = np.where((rng.random((N, 8, 1, K)) < 0.04) | (rng.random((N, 8, 16, K)) < 0.04), 0.0, yt)
    a, b = names(rng)
    return pack(th, va, yt, weights(rng, N, 8, 16, K), a, b)
def setup_inputs_ends(rng):
    o = np.concatenate([np.arange(K), np.arange(W - K, W)])[np.argsort(rng.random((N, 8, TV, 2 * K)), axis=-1)]
    for r in range(N):
        for g in range(8):
            for t in range(TV):
                v = o[r, g, t]; i, n1, n2 = (0, 0, W - 1) if g % 2 == 0 else (K - 1, W - 1, 0)
                for place, num in ((i, n1), (K + i, n2)):
                    s = int(np.flatnonzero(v == num)[0]); old = int(v[place]); v[place] = num; v[s] = old
    for r in range(N):
        for g in range(8):
            i, n1, n2 = (0, 0, W - 1) if g % 2 == 0 else (K - 1, W - 1, 0)
            o[r, g, :, i] = n1; o[r, g, :, K + i] = n2
    a, b = o[..., :K].copy(), o[..., K:].copy()
    th = 2.0 * sgn(rng, N, 8, 16, W); same = np.array([0.7, 0.75, 0.8, 0.85, 0.7, 0.75, 0.8, 0.85]).reshape(1, 8, 1, 1)
    va = th * np.where(rng.random(th.shape) < same, 1.0, -1.0)
    yt = 2.0 * sgn(rng, N, 8, 16, K); wt = 1.0 * rng.integers(0, 2, (N, 8, 16, K))
    s7 = sgn(rng, 16, 1); s0 = sgn(rng, 16, 1)
    for x in (th, va):
        one = x[:, 7, :1].copy(); x[:, 7] = one * s7; x[:, 0] = one[..., ::-1] * s0
    for x in (yt, wt):
        one = x[:, 7, :1].copy(); x[:, 7] = one; x[:, 0] = one
    a[:, 0] = W - 1 - a[:, 7]; b[:, 0] = W - 1 - b[:, 7]
    return pack(th, va, yt, wt, a, b)
def setup_inputs_corners(rng):
    th = sgn(rng, N, 8, 16, W); yt = sgn(rng, N, 8, 16, K); wt = rng.choice(np.array([0.0, 2.0 ** -20, 0.0625]), (N, 8, 16, K))
    a, b = names(rng); kap = np.zeros((N, 8, W)); kap[:, :2] = 2.0
    for r in range(N):
        todo = [(4, rng.permutation(K)[:1 + r % 3], 2.0), (6, np.array([0, 1, K // 2, K - 2, K - 1]), 2.0)]
        if r % 2 == 1: todo.append((0, rng.integers(0, K, 1), 0.0))
        for g0, js, val in todo:
            for g in (g0, g0 + 1):
                for t in range(TV):
                    q = (r + S * t) % N
                    kap[q, g, a[r, g, t, js]] = val; kap[q, g, b[r, g, t, js]] = val
                if val > 0: yt[r, g][:, js] = -th[r, g][:, a[r, g, 0, js]] * th[r, g][:, b[r, g, 0, js]]
    return pack(th, kap[:, :, None, :] * th, yt, wt, a, b)
def setup_inputs_crowd(rng):
    th0 = pay(rng, N, 2, W); va0 = 0.875 * th0 + pay(rng, N, 2, W); y0 = pay(rng, N, 2, K); w0 = weights(rng, N, 2, K)
    nm = np.argsort(rng.random((N, TV, W)), axis=-1)[..., :2 * K]; order = np.argsort(rng.random((N, 8, W)), axis=-1)
    cls = np.stack([rng.permutation((np.arange(16) >= n).astype(np.int64)) for n in (16, 16, 15, 1, 16, 0, 1, 15)]); sg = sgn(rng, 8, 16, 1)
    th = np.zeros((N, 8, 16, W)); va = np.zeros((N, 8, 16, W)); o = np.zeros((N, 8, TV, 2 * K), np.int64)
    for q in range(N):
        for g in range(8):
            th[q, g][:, order[q, g]] = sg[g] * th0[q][cls[g]]; va[q, g][:, order[q, g]] = sg[g] * va0[q][cls[g]]
            for t in range(TV): o[q, g, t] = order[(q + S * t) % N, g][nm[q, t]]
    return pack(th, va, y0[:, cls], w0[:, cls], o[..., :K].copy(), o[..., K:].copy())
def setup_inputs_calm(rng):
    th, va, yt, wt, a, b = plain(rng)
    th[:, :4] = sgn(rng, N, 4, 16, W); u = rng.random((N, 4, 16, W))
    va[:, :4] = th[:, :4] * np.where(u < 0.25, 0.0, np.where(u < 0.55, 1.0, 2.0))
    yt[:, :4] = sgn(rng, N, 4, 16, K); wt[:, :4] = 0.0
    th[:, 2] *= 2.0 ** -20; va[:, 2] *= 2.0 ** -20; yt[:, 2] *= 2.0 ** -12
    u = rng.random((N, 16, K))
    wt[:, 6] = np.where(u < 0.25, 2.0 ** -20, np.where(u < 0.5, np.exp2(-20 + 9 * rng.random((N, 16, K))), wt[:, 6]))
    for g in (5, 7): residues(rng, (th, va, yt, wt, a, b), g)
    for g in (4, 6): knots(rng, (th, va, yt, wt, a, b), g)
    halves(rng, (th, va, yt, wt, a, b), 0)
    return pack(th, va, yt, wt, a, b)
def check_ranges(d):
    bad = []
    for k, lo, hi, least in (("th", -2.0, 2.0, 2.0 ** -20), ("va", -2.0, 2.0, 2.0 ** -20), ("yt", -2.0, 2.0, 2.0 ** -12), ("wt", 0.0, 1.0, 2.0 ** -20)):
        v = np.asarray(d[k]).astype(np.float64); s = np.abs(v)
        if not np.all((v >= lo) & (v <= hi) & ((s == 0) | (s >= least))): bad.append("range of " + k)
    for k in ("an", "bn"):
        if np.min(d[k]) < 0 or np.max(d[k]) > W - 1: bad.append("range of " + k)
    a = np.stack([gentries(v) for v in np.asarray(d["an"])]).reshape(N, 8, TV, K); b = np.asarray(d["bn"]).reshape(N, 8, TV, K)
    o = np.sort(np.concatenate([a, b], axis=-1), axis=-1)
    if np.any(o[..., 1:] == o[..., :-1]): bad.append("names of a visit (an and bn) repeat")
    if not bad and rounds(d["th"], d["va"], d["yt"], d["wt"], d["an"], d["bn"], True)[2]: bad.append("a product under 2 ** -126")
    return bad
def tiny(A, B, e, w, da, db):
    m = A * B + e; one = np.float32(1)
    pairs = ((A, B), (B, B), (A, A), (e, B), (e, A), (w, e * B), (w, e * A), (e * B, da), (e * A, db), (B * B, da), (m, db), (m, da), (A * A, db),
             (one, (e * B) * da + (e * A) * db), (w, (B * B) * da + m * db), (w, m * da + (A * A) * db))
    return any(bool(np.any((u != 0) & (v != 0) & (np.abs(u * v) < 2.0 ** -123))) for u, v in pairs)
def rounds(th, va, yt, wt, an, bn, watch):
    a = np.stack([gentries(v) for v in an]).astype(np.int64).reshape(N, 8, TV, K); b = bn.astype(np.int64).reshape(N, 8, TV, K); low = False
    for rnd in range(RO):
        ft = np.float32 if rnd < RO - 1 else np.float64
        c = ft(0.125); tab = th.astype(ft).reshape(N, 8, 16, W)
        y = yt.astype(ft).reshape(N, 8, 16, K); w = wt.astype(ft).reshape(N, 8, 16, K); kept = []
        for t in range(TV):
            own = (np.arange(N) - S * t) % N
            ia = a[own, :, t][:, :, None, :]; ib = b[own, :, t][:, :, None, :]; ww = w[own]
            A = np.take_along_axis(tab, ia, 3); B = np.take_along_axis(tab, ib, 3)
            e = A * B - y[own]
            np.put_along_axis(tab, ia, A - c * (ww * (e * B)), 3)
            np.put_along_axis(tab, ib, B - c * (ww * (e * A)), 3)
            kept.append((own, ia, ib, ww, A, B, e))
        d = tab - va.astype(ft).reshape(N, 8, 16, W); h = np.zeros((N, 8, 16, K), ft)
        for t in range(TV - 1, -1, -1):
            own, ia, ib, ww, A, B, e = kept[t]
            da = np.take_along_axis(d, ia, 3); db = np.take_along_axis(d, ib, 3)
            if watch and rnd < RO - 1: low = low or tiny(A, B, e, ww, da, db)
            h[own] = h[own] - c * ((e * B) * da + (e * A) * db)
            m = A * B + e
            np.put_along_axis(d, ia, da - c * (ww * ((B * B) * da + m * db)), 3)
            np.put_along_axis(d, ib, db - c * (ww * (m * da + (A * A) * db)), 3)
        if rnd < RO - 1:
            up = np.sum((h > 0).astype(np.int64), axis=2)
            refused = up + np.roll(up, -1, axis=1) >= QV
            for r in range(N):
                for g in range(8):
                    p = np.flatnonzero(refused[r, g])
                    if len(p) > 1: b[r, g][:, p] = b[r, g][:, np.roll(p, 1)]
    return d, h, low
def reference(th, va, yt, wt, an, bn):
    d, h, low = rounds(th, va, yt, wt, an, bn, False)
    return {"yd": d.reshape(N, 128, W).astype(np.float32), "yh": h.reshape(N, 128, K).astype(np.float32)}

def check_inputs(d):
    bad = list(check_ranges(d))
    if not bad:
        for name, y in reference(**d).items():
            for q in range(N):
                v = np.abs(np.asarray(y[q], np.float64)); s = np.sqrt(np.mean(v * v))
                if v.max() > 12 * s or s < 2.0 ** -4: bad.append('%s of rank %d is uneven or too small' % (name, q))
    return bad

@@ -1,0 +1,649 @@
+from concourse.bass import DstId, RemoteDMATransfer
+from concourse.mybir import AluOpType, ActivationFunctionType
+
+W, K, NV_, RO = 3072, 768, 4, 3
+L2 = 2 * K
+H = K // 2
+IDX = "float16"
+OFF = 1536
+SAME_WAR = True
+BIG = 4096.0
+
+
+def FB(t):
+    return W + L2 * t
+
+
+def QB(t):
+    return W + 3 * L2 + L2 * (3 - t)
+
+
+SCRATCH = {
+    "PS": ("psum", [128, 4096], "float32"),
+    "Z": ("sbuf", [128, W + 7 * L2], "float32"),
+    "LOC": ("sbuf", [128, W], "float32"),
+    "GB": ("sbuf", [128, L2], "float32"),
+    "IO": ("sbuf", [128, L2], "float32"),
+    "KI": ("sbuf", [128, L2], "float32"),
+    "AB": ("sbuf", [128, 4 * K], "float32"),
+    "BB": ("sbuf", [128, 4 * K], "float32"),
+    "EA": ("sbuf", [128, 4 * K], "float32"),
+    "EB": ("sbuf", [128, 4 * K], "float32"),
+    "MM": ("sbuf", [128, 3 * K], "float32"),
+    "PR": ("sbuf", [128, K], "float32"),
+    "BS0": ("sbuf", [128, K], "float32"),
+    "DS": ("sbuf", [128, K], "float32"),
+    "DA": ("sbuf", [128, K], "float32"),
+    "DB": ("sbuf", [128, K], "float32"),
+    "T1": ("sbuf", [128, K], "float32"),
+    "T2": ("sbuf", [128, K], "float32"),
+    "T4": ("sbuf", [128, K], "float32"),
+    "T5": ("sbuf", [128, K], "float32"),
+    "C1": ("sbuf", [128, K], "float32"),
+    "C2": ("sbuf", [128, K], "float32"),
+    "C3": ("sbuf", [128, K], "float32"),
+    "YW": ("sbuf", [128, 4 * L2], "bfloat16"),
+    "NW": ("sbuf", [128, 4 * K], "bfloat16"),
+    "NVB": ("sbuf", [128, W + 4 * L2], "bfloat16"),
+    "POS": ("sbuf", [128, K], "bfloat16"),
+    "PN": ("sbuf", [128, K], "float32"),
+    "WO": ("sbuf", [128, 48], "float32"),
+    "BNI": ("sbuf", [128, K], "int32"),
+    "BNF": ("sbuf", [128, K + 8], IDX),
+    "ANI": ("sbuf", [128, 192], "int32"),
+    "LS": ("sbuf", [128, 4 * 96], "uint16"),
+    "LV": ("sbuf", [128, 4 * 96], "uint16"),
+    "FL": ("sbuf", [128, 4 * 96], "uint16"),
+    "NL": ("sbuf", [128, 3 * 96], "uint16"),
+    "FIN": ("sbuf", [128, 192], "uint16"),
+    "PP": ("sbuf", [128, 8 * 48], "uint16"),
+    "PI": ("sbuf", [128, 8 * 48], "uint16"),
+    "V1": ("sbuf", [128, 144], "float32"),
+    "V2": ("sbuf", [128, 144], "float32"),
+    "V0": ("sbuf", [128, 128], "float32"),
+    "MI": ("sbuf", [128, 128], "int32"),
+    "E1": ("sbuf", [128, 5 * 144], "float32"),
+    "E2": ("sbuf", [128, 4 * 144], IDX),
+    "EH": ("sbuf", [128, 288], IDX),
+    "ID": ("sbuf", [128, 128], "bfloat16"),
+    "IW": ("sbuf", [128, 128], "bfloat16"),
+    "MV": ("sbuf", [128, 128], "bfloat16"),
+    "RI": ("sbuf", [128, 4], "int32"),
+    "CS": ("sbuf", [128, 40], "float32"),
+}
+NPOOL = 70
+ARR = (["yw%d" % t for t in (1, 2, 3)] + ["lv%d" % t for t in (1, 2, 3)]
+       + ["c%d_%d" % (r, t) for r in range(RO) for t in (1, 2, 3)]
+       + ["pp%d_%d" % (r, t) for r in (1, 2) for t in (1, 2, 3)]
+       + ["pi%d_%d" % (r, t) for r in (1, 2) for t in (1, 2, 3)])
+SEMAPHORES = ["qv", "qa", "qp", "qg"] + ARR + ["s%d" % i for i in range(NPOOL)]
+
+
+def rank_program(g, core, T, topo):
+    rank = T.rank_of(core)
+    if rank is None:
+        return
+    cores = list(T.cores)
+    N = len(cores)
+    A_ = AluOpType
+    F_ = ActivationFunctionType
+    Q = {"g": g, "v": g.vector, "a": g.scalar, "p": g.tensor, "s": g.sync}
+    count = {"v": 0, "a": 0, "p": 0, "g": 0}
+    waited = {}
+    final = {}
+    acc = {}
+    banks = {}
+    pool = [0]
+
+    def newsem():
+        pool[0] += 1
+        return "s%d" % (pool[0] - 1)
+
+    def need(q, reads, writes):
+        want = {}
+
+        def add(tok):
+            want[tok[0]] = max(want.get(tok[0], 0), tok[1])
+        for regs, isw in ((reads, False), (writes, True)):
+            for (n, c0, c1) in regs:
+                for (a0, a1, tok, w) in acc.get(n, []):
+                    if a0 < c1 and c0 < a1 and (w or isw):
+                        if tok[2] == q and isw and not SAME_WAR and q != "g":
+                            continue
+                        add(tok)
+                if n == "PS":
+                    for b in range(c0 // 512, (c1 - 1) // 512 + 1):
+                        for e, tok in banks.get(b, {}).items():
+                            if e != q:
+                                add(tok)
+        for s, v in want.items():
+            if waited.get((q, s), 0) < v:
+                Q[q].wait_ge(T.sem[s], v)
+                waited[(q, s)] = v
+
+    def note(q, tok, reads, writes):
+        final[tok[0]] = max(final.get(tok[0], 0), tok[1])
+        for (n, c0, c1) in writes:
+            acc[n] = [x for x in acc.get(n, []) if not (c0 <= x[0] and x[1] <= c1 and (x[2][2] != q or q in "gsd" or SAME_WAR))]
+            acc[n].append((c0, c1, tok, True))
+        for (n, c0, c1) in reads:
+            acc[n] = [x for x in acc.get(n, []) if not (not x[3] and x[2][0] == tok[0] and c0 <= x[0] and x[1] <= c1)]
+            acc[n].append((c0, c1, tok, False))
+        for (n, c0, c1) in list(reads) + list(writes):
+            if n == "PS":
+                for b in range(c0 // 512, (c1 - 1) // 512 + 1):
+                    banks.setdefault(b, {})[q] = tok
+
+    def op(q, fn, reads, writes):
+        need(q, reads, writes)
+        count[q] += 1
+        fn().then_inc(T.sem["q" + q], 1)
+        note(q, ("q" + q, count[q], q), reads, writes)
+
+    def dma(q, out, in_, reads, writes, add=False):
+        need(q, reads, writes)
+        s = newsem()
+        if add:
+            Q[q].dma_start(out, in_, accum_op=A_.add).then_inc(T.sem[s], 16)
+        else:
+            Q[q].dma_start(out, in_).then_inc(T.sem[s], 16)
+        note("d", (s, 16, "d"), reads, writes)
+
+    def arrive(sem, n, reg):
+        note("d", (sem, n, "d"), [], [reg])
+
+    def ap(r):
+        return T[r[0]][:, r[1]:r[2]]
+
+    def ind(win, off):
+        return ap(win).indirect(ap(off))
+
+    def peer(d):
+        return cores[(rank + d) % N]
+
+    def dst(c):
+        a = topo.addr(c)
+        return DstId(rid=a[0], pnc=a[1])
+
+    def emask(c, i0, n):
+        m = 0
+        for e in topo.engines(core, c)[i0:i0 + n]:
+            m |= 1 << e
+        return m
+    NE = len(topo.engines(core, peer(1)))
+    NS_ = NE // 4
+
+    def send(items):
+        need("g", [r for it in items for r in it[1]], [])
+        s = newsem()
+        trs = []
+        tot = 0
+        for (c, srcs, land, sem, i0, n) in items:
+            if len(srcs) == 1:
+                trs.append(RemoteDMATransfer(dst_ids=[dst(c)], dma_engine_mask=emask(c, i0, n), remote_sem=T.sem[sem],
+                                             src=ap(srcs[0]), dst=ap(land)))
+            else:
+                trs.append(RemoteDMATransfer(dst_ids=[dst(c)], dma_engine_mask=emask(c, i0, n), remote_sem=T.sem[sem],
+                                             srcs=[ap(r) for r in srcs], dsts=[ap(land)], alu_op=1))
+            tot += n
+        g.remote_dma_fused(trs, local_sem=T.sem[s])
+        note("d", (s, tot, "d"), [r for it in items for r in it[1]], [])
+
+    def tt(out, a, b, o):
+        op("v", lambda: g.vector.tensor_tensor(ap(out), ap(a), ap(b), o), [a, b], [out])
+
+    def gtt(out, win, off, b, o):
+        op("v", lambda: g.vector.tensor_tensor(ap(out), ind(win, off), ap(b), o), [win, off, b], [out])
+
+    def ts(out, a, s1, s2, o0, o1=None):
+        rd = [a] + [s for s in (s1, s2) if isinstance(s, tuple)]
+        x1 = ap(s1) if isinstance(s1, tuple) else s1
+        x2 = ap(s2) if isinstance(s2, tuple) else s2
+        if o1 is None:
+            op("v", lambda: g.vector.tensor_scalar(ap(out), ap(a), x1, None, o0), rd, [out])
+        else:
+            op("v", lambda: g.vector.tensor_scalar(ap(out), ap(a), x1, x2, o0, o1), rd, [out])
+
+    def vcopy(out, a):
+        op("v", lambda: g.vector.tensor_copy(ap(out), ap(a)), [a], [out])
+
+    def vgat(out, win, off):
+        op("v", lambda: g.vector.tensor_copy(ap(out), ind(win, off)), [win, off], [out])
+
+    def agat(out, win, off, scale=1.0):
+        op("a", lambda: g.scalar.activation(ap(out), ind(win, off), F_.Copy, scale=scale), [win, off], [out])
+
+    def act(out, a, f, scale=1.0):
+        op("a", lambda: g.scalar.activation(ap(out), ap(a), f, scale=scale), [a], [out])
+
+    def scan(out, d0, d1, init, o0, o1):
+        rd = [d0, d1] + ([init] if isinstance(init, tuple) else [])
+        x = ap(init) if isinstance(init, tuple) else init
+        op("v", lambda: g.vector.tensor_tensor_scan(ap(out), ap(d0), ap(d1), x, o0, o1), rd, [out])
+
+    def iota(out, pat, base, cm, flt=True):
+        if flt:
+            op("g", lambda: g.iota(ap(out), pat, base, cm, allow_small_or_imprecise_dtypes=True), [], [out])
+        else:
+            op("g", lambda: g.iota(ap(out), pat, base, cm), [], [out])
+
+    def place(out, lhs, src):
+        need("p", [lhs, src], [out])
+        cuts = [out[1]] + [b for b in range(0, 4096, 512) if out[1] < b < out[2]] + [out[2]]
+        ins = None
+        for c0, c1 in zip(cuts[:-1], cuts[1:]):
+            s0 = src[1] + c0 - out[1]
+            ins = g.tensor.matmul(T.PS[:, c0:c1], ap(lhs), T[src[0]][:, s0:s0 + c1 - c0], True, True)
+        count["p"] += 1
+        ins.then_inc(T.sem.qp, 1)
+        note("p", ("qp", count["p"], "p"), [lhs, src], [out])
+
+    def wrap(c0, terms, parts=128):
+        n = (terms[0][0][2] - terms[0][0][1]) // 16
+        out = ("PS", c0, c0 + n)
+        rd = [x for tm in terms for x in tm]
+        need("p", rd, [out])
+        ins = None
+        for j, (src, em) in enumerate(terms):
+            for i in range(16):
+                e0 = em[1] + 15 - i
+                ins = g.tensor.matmul(ap(out), T[em[0]][0:parts, e0:e0 + 128],
+                                      T[src[0]][0:parts, src[1] + i:src[2]:16], i == 0 and j == 0,
+                                      i == 15 and j == len(terms) - 1)
+        count["p"] += 1
+        ins.then_inc(T.sem.qp, 1)
+        note("p", ("qp", count["p"], "p"), rd, [out])
+        return out
+
+    def U(n, t=0):
+        return (n, K * t, K * t + K)
+
+    def E1(r):
+        return ("E1", 144 * r, 144 * r + 144)
+    X = [("PS", K * i, K * i + K) for i in range(5)]
+    B6, B7 = 3072, 3840
+    CUT = ((0, 512), (512, K))
+
+    def names(t):
+        return ("LS" if t == 0 else "LV", 96 * t, 96 * t + 96)
+
+    def fwd(t):
+        return names(0) if t == 0 else ("FL", 96 * t, 96 * t + 96)
+
+    def half(r, i, n=2):
+        w = (r[2] - r[1]) // n
+        return (r[0], r[1] + i * w, r[1] + (i + 1) * w)
+
+    def pl(n, r, t):
+        c = 48 * (4 * (r - 1) + t)
+        return (n, c, c + 48)
+    LOCW = ("LOC", 0, W)
+    VA = ("NVB", 0, W)
+
+    def nva(t):
+        return ("NVB", W + L2 * t, W + L2 * (t + 1))
+
+    dma("s", T.BNI[0:32, :], T.bn[:], [], [U("BNI")])
+    dma("a", T.ANI[:], T.an[:], [], [("ANI", 0, 192)])
+    iota(("V2", 0, 144), [[16, 9], [1000, 16]], 0, -4)
+    iota(("RI", 0, 4), [[0, 4]], 0, 1, False)
+    iota(("CS", 0, 4), [[1, 4]], 0, 0)
+    iota(("V1", 0, 144), [[16, 9], [1000, 16]], 0, -1)
+    iota(("V0", 0, 128), [[1, 128]], 0, -1)
+    TH = ("NVB", W, 2 * W)
+    dma("s", ap(TH), T.th[:], [], [TH])
+    dma("g", T.Z[:, 0:W], T.th[:], [], [("Z", 0, W)])
+    iota(("KI", 0, L2), [[1, L2]], 0, 0)
+    iota(("MI", 0, 128), [[-16, 8], [0, 16]], 128, 1, False)
+    dma("s", T.YW[:, 0:K], T.yt[:], [], [("YW", 0, K)])
+    dma("s", T.YW[:, K:L2], T.wt[:], [], [("YW", K, L2)])
+    dma("s", T.NVB[:, 0:W], T.va[:], [], [VA])
+    op("v", lambda: g.vector.memset(T.POS[:], 1.0), [], [U("POS")])
+
+    def cols(t):
+        scan(U("LOC", t), U("POS"), U("POS"), float(K * t - 1), A_.mult, A_.add)
+
+    def ids(t, src, out):
+        op("a", lambda: g.scalar.activation(ap(out), ap(src), F_.Identity, bias=T.CS[:, 36 + t:37 + t],
+                                            scale=T.CS[:, 24 + t:25 + t]),
+           [src, ("CS", 24, 40)], [out])
+
+    def index(out, src):
+        ts(out, src, 0.25, None, A_.add)
+    cols(0)
+    ts(("RI", 0, 4), ("RI", 0, 4), 15, None, A_.bitwise_and)
+    ts(("CS", 8, 12), ("CS", 0, 4), -float(L2), float(QB(0)), A_.mult, A_.add)
+    vcopy(("CS", 4, 8), ("RI", 0, 4))
+    ts(("CS", 12, 16), ("CS", 0, 4), float(2 * L2), float(FB(0) - QB(0)), A_.mult, A_.add)
+    tt(("CS", 16, 20), ("CS", 0, 4), ("CS", 4, 8), A_.subtract)
+    ts(("CS", 20, 24), ("CS", 4, 8), 0.0, None, A_.is_equal)
+    ts(("CS", 24, 28), ("CS", 16, 20), -2.5, None, A_.is_gt)
+    ts(("CS", 28, 32), ("CS", 16, 20), -2.0, ("CS", 20, 21), A_.is_equal, A_.add)
+    tt(("CS", 32, 36), ("CS", 24, 28), ("CS", 8, 12), A_.mult)
+    tt(("CS", 28, 32), ("CS", 28, 32), ("CS", 12, 16), A_.mult)
+    ts(("E2", 0, 144), ("V2", 0, 144), 15000.0, None, A_.is_equal)
+    tt(("CS", 36, 40), ("CS", 32, 36), ("CS", 28, 32), A_.add)
+    cols(1)
+    ids(0, ("LOC", 0, L2), ("IO", 0, L2))
+    op("v", lambda: g.vector.tensor_scalar(T.BNF[0:32, 0:K], T.BNI[0:32, :], -float(OFF), None, A_.add),
+       [U("BNI")], [U("BNF")])
+    for u in range(1, 4):
+        ts(("E2", 144 * u, 144 * u + 144), ("V2", 0, 144), float(15000 - 4 * u), None, A_.is_equal)
+    wr = [wrap(512 * t, [(U("BNF"), ("E2", 144 * t, 144 * t + 144))], 32) for t in range(4)]
+    cols(2)
+    cols(3)
+    for t in range(4):
+        vcopy(("LS", 96 * t, 96 * t + 48), ("ANI", 48 * t, 48 * t + 48))
+        ts(("LS", 96 * t + 48, 96 * t + 96), wr[t], float(OFF), None, A_.add)
+    send([(peer(t), [("LS", 96 * t, 96 * t + 96)], ("LV", 96 * t, 96 * t + 96), "lv%d" % t, NS_ * (t - 1), NS_)
+          for t in (1, 2, 3)])
+    for t in (1, 2, 3):
+        send([(peer(t), [("YW", 0, L2)], ("YW", L2 * t, L2 * t + L2), "yw%d" % t, 0, NE)])
+        arrive("lv%d" % t, NS_, names(t))
+        arrive("yw%d" % t, NE, ("YW", L2 * t, L2 * t + L2))
+
+    def consts():
+        ts(("ID", 0, 128), ("V0", 0, 128), 0.0, None, A_.is_equal)
+        ts(("IW", 0, 128), ("V0", 0, 128), 0.0, -0.125, A_.is_equal, A_.mult)
+        ts(E1(0), ("V1", 0, 144), 15000.0, None, A_.is_equal)
+
+    def later():
+        ts(("MI", 0, 128), ("MI", 0, 128), 4, 7, A_.arith_shift_right, A_.bitwise_and)
+        for r in range(1, 5):
+            ts(E1(r), ("V1", 0, 144), float(15000 - r), None, A_.is_equal)
+        ts(("EH", 0, 144), ("V1", 0, 144), 15000.0, None, A_.is_equal)
+        ts(("EH", 144, 288), ("V1", 0, 144), 15000.0, -1.0, A_.is_equal, A_.mult)
+        op("v", lambda: g.vector.memset(T.CS[:, 8:12], -64.0), [], [("CS", 8, 12)])
+        ts(("WO", 0, 48), ("KI", 0, 48), 16.0, ("CS", 4, 5), A_.mult, A_.add)
+        ts(("MV", 0, 128), ("MI", 0, 128), 1.5, None, A_.is_lt)
+
+    def yw(t):
+        Xy, Xw = (X[0], X[1]) if t % 2 else (X[2], X[3])
+        place(Xy, ("ID", 0, 128), ("YW", L2 * t, L2 * t + K))
+        place(Xw, ("IW", 0, 128), ("YW", L2 * t + K, L2 * t + L2))
+
+    def squares(t):
+        Xa, Xb = (X[2], X[3]) if t % 2 else (X[0], X[1])
+        act(Xa, U("BB", t), F_.Square)
+        act(Xb, U("AB", t), F_.Square)
+
+    def inits(r):
+        for t in ((2, 1, 0) if r < RO - 1 else (2, 1, 0, -1, -2)):
+            z = ("Z", FB(t), FB(t) + L2)
+            s = ("NVB", z[1], z[2])
+            dma("g", ap(z), ap(s), [s, z], [z], add=True)
+
+    def errors(P, Xy, A, B, EA, EB):
+        for i in range(2):
+            tt(half(Xy, i), half(P, i), half(Xy, i), A_.subtract)
+        for i in range(2):
+            tt(half(EA, i), half(Xy, i), half(A, i), A_.mult)
+        tt(EB, Xy, B, A_.mult)
+
+    def forward(r, t):
+        Xy, Xw = (X[0], X[1]) if t % 2 else (X[2], X[3])
+        zw = ("Z", 0, FB(t))
+        fa, fb = half(fwd(t), 0), half(fwd(t), 1)
+        A, B, EA, EB = U("AB", t), U("BB", t), U("EA", t), U("EB", t)
+        oa, ob = ("Z", FB(t), FB(t) + K), ("Z", FB(t) + K, FB(t) + L2)
+        P = U("PR")
+        if r == 0:
+            GB, IO = ("GB", 0, L2), ("IO", 0, L2)
+            wf = ("PS", B6, B6 + 96)
+
+            def mark(i, n):
+                o, a, b = half(names(t), i, n), half(GB, i, n), half(IO, i, n)
+                op("v", lambda: g.vector.tensor_tensor(ind(LOCW, o), ap(a), ap(b), A_.max), [o, a, b], [LOCW])
+
+            def smark(src):
+                op("a", lambda: g.scalar.activation(ind(LOCW, names(t)), ap(src), F_.Silu), [names(t), src], [LOCW])
+            if t == 0:
+                zw = TH
+                agat(A, zw, fa)
+                smark(IO)
+                vgat(B, zw, fb)
+                consts()
+                yw(0)
+            elif t == 1:
+                yw(1)
+                mark(0, 2)
+                index(fwd(1), wf)
+                agat(B, zw, fb)
+                agat(A, zw, fa)
+                mark(1, 2)
+            elif t == 2:
+                yw(2)
+                agat(B, zw, fb)
+                agat(A, zw, fa)
+                mark(0, 1)
+            else:
+                yw(3)
+                agat(A, zw, fa)
+                vgat(B, zw, fb)
+                ids(3, ("KI", 0, L2), ("PS", X[2][1], X[3][2]))
+                agat(nva(3), VA, names(3), -1.0)
+            if t < 3:
+                agat(GB, LOCW, names(t + 1))
+                wrap(B6, [(GB, E1(0))])
+                if t < 2:
+                    ids(t + 1, ("KI", 0, L2), IO)
+                if t > 0:
+                    for u in ((1,) if t == 1 else (0, 2)):
+                        agat(nva(u), VA, names(u), -1.0)
+                    for u in ((0, 1) if t == 1 else (2,)):
+                        act(U("NW", u), ("YW", L2 * u + K, L2 * u + L2), F_.Copy, -0.125)
+                if t == 1:
+                    act(U("BS0"), U("BB", 0), F_.Copy)
+            for i in range(2):
+                gtt(half(P, i), zw, half(fa, i), half(B, i), A_.mult)
+            if t == 3:
+                inits(r)
+            errors(P, Xy, A, B, EA, EB)
+            if t < 3:
+                if t > 0:
+                    tt(U("MM", t), Xy, P, A_.add)
+                tt(Xy, EA, Xw, A_.mult)
+                tt(Xw, EB, Xw, A_.mult)
+                tt(ob, Xy, B, A_.add)
+                if t > 0:
+                    index(fwd(t + 1), wf)
+                tt(oa, Xw, A, A_.add)
+                if t == 0:
+                    later()
+            else:
+                tt(GB, ("PS", X[2][1], X[3][2]), GB, A_.max)
+                squares(3)
+                act(U("NW", t), ("YW", L2 * t + K, L2 * t + L2), F_.Copy, -0.125)
+                smark(GB)
+                agat(GB, LOCW, names(2))
+                agat(IO, LOCW, names(1))
+                tt(X[4], EA, Xw, A_.mult)
+                tt(Xy, Xy, P, A_.add)
+                tt(Xw, EB, Xw, A_.mult)
+                tt(X[4], X[4], B, A_.add)
+                tt(Xw, Xw, A, A_.add)
+                tt(U("DB"), X[4], half(nva(3), 1), A_.add)
+                tt(U("DA"), Xw, half(nva(3), 0), A_.add)
+            return
+        pp, pi = pl("PP", r, t), pl("PI", r, t)
+        Bs = U("BS0") if t == 0 else U("DS")
+        if t > 0:
+            arrive("pp%d_%d" % (r, t), NS_, pp)
+            arrive("pi%d_%d" % (r, t), NS_, pi)
+            agat(Bs, zw, fb)
+            if t > 1 or r == RO - 1:
+                Xp = X[2] if t % 2 else X[0]
+                tt(U("MM", t - 1), Xp, P, A_.add)
+                vgat(half(A, 0), zw, half(fa, 0))
+                agat(half(A, 1), zw, half(fa, 1))
+            else:
+                vgat(A, zw, fa)
+            if t == 3:
+                inits(r)
+        else:
+            yw(0)
+        agat(B, Bs, pp)
+        if t == 0:
+            op("a", lambda: g.scalar.activation(ind(U("T5"), pp), T.KI[:, 64:64 + K], F_.Silu),
+               [pp, ("KI", 64, 64 + K)], [U("T5")])
+            op("a", lambda: g.scalar.activation(ap(U("BNF")), ap(U("T5")), F_.Identity, bias=T.CS[:, 8:9]),
+               [U("T5"), ("CS", 8, 9)], [U("BNF")])
+            wi = wrap(B7, [(U("BNF"), ("EH", 0, 144))])
+            if r == 1:
+                agat(U("PN"), ("KI", 0, L2), pp)
+        if t < 3:
+            yw(t + 1)
+        else:
+            place(X[4], ("ID", 0, 128), half(nva(3), 1))
+            squares(3)
+        if r == 1 and t == 1:
+            wrap(B6, [(LOCW, E1(1))])
+        for i in range(2):
+            gtt(half(P, i), Bs, half(pp, i), half(A, i), A_.mult)
+        errors(P, Xy, A, B, EA, EB)
+        tt(U("T4"), EA, Xw, A_.mult)
+        if t == 3:
+            tt(Xy, Xy, P, A_.add)
+        if r == 1 and t == 2:
+            index(("FIN", 0, 192), ("PS", B6, B6 + 192))
+        tt(Xw, EB, Xw, A_.mult)
+        if t == 0:
+            tt(half(oa, 0), half(Xw, 0), half(A, 0), A_.add)
+            ts(pi, wi, 0.25, None, A_.add)
+            send([(peer(u), [pi], pl("PI", r, u), "pi%d_%d" % (r, u), NS_ * (u - 1), NS_) for u in (1, 2, 3)])
+            tt(half(oa, 1), half(Xw, 1), half(A, 1), A_.add)
+            gtt(ob, U("T4"), pi, Bs, A_.add)
+        elif t < 3:
+            gtt(ob, U("T4"), pi, Bs, A_.add)
+            tt(oa, Xw, A, A_.add)
+        else:
+            gtt(U("T5"), U("T4"), pi, Bs, A_.add)
+            tt(Xw, Xw, A, A_.add)
+            tt(U("DS"), X[4], U("T5"), A_.add)
+            tt(U("DA"), Xw, half(nva(3), 0), A_.add)
+
+    def backward(r, t):
+        last = r == RO - 1
+        Xa, Xb = (X[2], X[3]) if t % 2 else (X[0], X[1])
+        Xm = X[0] if t == 3 else X[4]
+        EA, EB, DA, DB, DS = U("EA", t), U("EB", t), U("DA"), U("DB"), U("DS")
+        T4, T5 = U("T4"), U("T5")
+        T1, T2 = (U("T1"), U("T2")) if t % 2 else (U("PR"), U("MM", 2))
+        full = last or t > 0
+        pp, pi = (pl("PP", r, t), pl("PI", r, t)) if r else (None, None)
+        wn = []
+        if t == 3:
+            if r == 0:
+                wn = wrap(B6, [(("GB", 0, L2), E1(4))])
+                tt(T2, EA, DB, A_.mult)
+                tt(T1, EB, DA, A_.mult)
+            else:
+                agat(DB, DS, pp)
+                act(X[4], EB, F_.Copy)
+                gtt(T2, DS, pp, EA, A_.mult)
+                tt(Xa, Xa, DA, A_.mult)
+                tt(T5, Xm, DA, A_.mult)
+                tt(T1, X[4], DA, A_.mult)
+        else:
+            zw = ("Z", 0, QB(t))
+            nl = ("NL", 96 * t, 96 * t + 96)
+            na, nb = half(nl, 0), half(nl, 1)
+            if r == 0:
+                if full:
+                    wn = wrap(X[2][1], [(("IO", 0, L2), E1(3))]) if t == 2 else wrap(0, [(("GB", 0, L2), E1(2))])
+                    agat(DA, zw, na)
+                    agat(DB, zw, nb)
+                gtt(T1, zw, na, EB, A_.mult)
+                gtt(T2, zw, nb, EA, A_.mult)
+            else:
+                agat(DS, zw, nb)
+                if full:
+                    agat(DA, zw, na)
+                    agat(DB, DS, pp)
+                gtt(T1, zw, na, EB, A_.mult)
+                gtt(T2, DS, pp, EA, A_.mult)
+        if t > 0:
+            send([(peer(-t), [T1, T2], U("C%d" % t), "c%d_%d" % (r, t), 0, NE)])
+            arrive("c%d_%d" % (r, t), NE, U("C%d" % t))
+            if t == 1:
+                dma("g", ap(U("C3")), ap(U("C2")), [U("C2"), U("C3")], [U("C3")], add=True)
+        elif last:
+            for s in (U("C1"), T1, T2):
+                dma("g", ap(U("C3")), ap(s), [s, U("C3")], [U("C3")], add=True)
+        if not full:
+            act(X[0], T1, F_.Copy)
+            tt(X[4], X[4], U("C1"), A_.subtract)
+            for (c0, c1) in CUT:
+                tt(("T4", c0, c1), ("PS", c0, c1), (T2[0], T2[1] + c0, T2[1] + c1), A_.add)
+            return
+        if t < 3 or r == 0:
+            tt(Xa, Xa, DA, A_.mult)
+            tt(T5, Xm, DA, A_.mult)
+        tt(T4, Xm, DB, A_.mult)
+        tt(Xb, Xb, DB, A_.mult)
+        if r == 0 and t < 3:
+            index(("NL", 96 * t - 96, 96 * t), wn)
+        if t > 1 or (t == 1 and last):
+            squares(t - 1)
+        if (r > 0 or t < 3) and (t > 1 or (t == 1 and last)):
+            act(X[4], U("MM", t - 1), F_.Copy)
+        if r == 0 and t == 2:
+            agat(("GB", 0, L2), LOCW, names(0))
+        if r == 1 and t == 2:
+            act(VA, VA, F_.Copy, -1.0)
+        tt(Xa, Xa, T4, A_.add)
+        tt(Xb, Xb, T5, A_.add)
+        qa, qb = ("Z", QB(t), QB(t) + K), ("Z", QB(t) + K, QB(t) + L2)
+        if r == 0:
+            tt(Xa, Xa, U("NW", t), A_.mult)
+            tt(Xb, Xb, U("NW", t), A_.mult)
+            if t == 3:
+                index(("NL", 192, 288), wn)
+                act(X[4], U("MM", t - 1), F_.Copy)
+            tt(qa, Xa, DA, A_.add)
+            tt(qb, Xb, DB, A_.add)
+        else:
+            tt(Xa, Xa, U("NW", t), A_.mult)
+            tt(T4, Xb, U("NW", t), A_.mult)
+            tt(qa, Xa, DA, A_.add)
+            gtt(qb, T4, pi, DS, A_.add)
+        if t == 1 and not last:
+            act(X[4], U("C3"), F_.Copy, -1.0)
+
+    def vote(r):
+        old = U("KI") if r == 0 else U("PN")
+        for (c0, c1) in CUT:
+            tt(("POS", c0, c1), ("T4", c0, c1), ("PS", B6 + c0, B6 + c1), A_.is_lt)
+            place(("PS", c0, c1), ("MV", 0, 128), ("POS", c0, c1))
+        for (c0, c1) in CUT:
+            ts(("PS", c0, c1), ("PS", c0, c1), 16.5, BIG, A_.is_lt, A_.mult)
+        for (c0, c1) in CUT:
+            tt(("T4", c0, c1), (old[0], c0, c1), ("PS", c0, c1), A_.subtract)
+        scan(U("T5"), X[0], U("T4"), 0.0, A_.min, A_.max)
+        scan(("BNF", 8, 8 + K), X[0], U("T4"), ("T5", K - 1, K), A_.min, A_.max)
+        vcopy(("BNF", 7, 8), ("T5", K - 1, K))
+        wp = wrap(B6, [(("BNF", 8, 8 + K), ("EH", 144, 288)), (("BNF", 7, 7 + K), ("EH", 0, 144))])
+        pp = pl("PP", r + 1, 0)
+        tt(("WO", 0, 48), wp, ("WO", 0, 48), A_.add)
+        vcopy(pp, ("WO", 0, 48))
+        send([(peer(u), [pp], pl("PP", r + 1, u), "pp%d_%d" % (r + 1, u), NS_ * (u - 1), NS_) for u in (1, 2, 3)])
+
+    for r in range(RO):
+        for t in range(4):
+            forward(r, t)
+        for t in (3, 2, 1, 0):
+            backward(r, t)
+        if r < RO - 1:
+            vote(r)
+
+    zw = ("Z", 0, W + 7 * L2)
+    for i in range(4):
+        o = U("LOC", i)
+        (agat if i % 2 else vgat)(o, zw, ("FIN", 48 * i, 48 * i + 48))
+        dma("s", T.yd[:, K * i:K * i + K], ap(o), [o], [])
+        if i == 1:
+            act(U("C2"), U("C3"), F_.Copy, -0.125)
+            dma("s", T.yh[:], ap(U("C2")), [U("C2")], [])
+    for s, v in final.items():
+        if max([waited.get((q, s), 0) for q in Q]) < v:
+            g.wait_ge(T.sem[s], v)

@@ -1,53 +1,67 @@
 from concourse.bass import DstId, RemoteDMATransfer
 from concourse.mybir import AluOpType, ActivationFunctionType
 
-W, K, NV_, RO = 3072, 768, 4, 3
-L2 = 2 * K
-H = K // 2
+W, K, RO = 3072, 768, 3
+L2, L3 = 2 * K, 3 * K
 IDX = "float16"
 OFF = 1536
-SAME_WAR = True
 BIG = 4096.0
+LIFT = 64
+NONE = -1024.0
+BS0 = W
+Q0B = W + K + 3 * L2 + 2 * W
+D0 = Q0B + K
+PE_E = True
+ACC = False
+EARLY = True
+GLANE = True
+START = False
+LOCA = 2
+IDV = ()
+VAORDER = (2, 1, 0)
+PASSES = 3
+LOG = []
+ORDER = []
+X0 = 128
+ONCE = {"remote": 2.0, "table": 1.3, "dma": 1.0}
+
+CYC, PCYC, GAT, SCA, FIX, SIG = 0.83e-3, 0.62e-3, 1.5, 3.0, 0.07, 0.1
+ISSUE, LAT, RATE = {"g": 1.0, "s": 0.1, "a": 0.1, "r": 0.6}, {"d": 2.5, "r": 3.0}, {"d": 500e3, "r": 8e3}
 
 
 def FB(t):
-    return W + L2 * t
+    return W + K + L2 * t
+
+
+def QV(t):
+    return FB(3) + W * (3 - t)
+
+
+def QA(t):
+    return {3: QV(3), 2: QV(2), 1: FB(1), 0: BS0}[t]
 
 
 def QB(t):
-    return W + 3 * L2 + L2 * (3 - t)
+    return Q0B if t == 0 else QA(t) + L3
 
+
+ROW_FIN, ROW_N, ROW_F = 1, (2, 3, 4), (None, 5, 6, 7)
 
 SCRATCH = {
     "PS": ("psum", [128, 4096], "float32"),
-    "Z": ("sbuf", [128, W + 7 * L2], "float32"),
-    "LOC": ("sbuf", [128, W], "float32"),
-    "GB": ("sbuf", [128, L2], "float32"),
-    "IO": ("sbuf", [128, L2], "float32"),
-    "KI": ("sbuf", [128, L2], "float32"),
-    "AB": ("sbuf", [128, 4 * K], "float32"),
-    "BB": ("sbuf", [128, 4 * K], "float32"),
-    "EA": ("sbuf", [128, 4 * K], "float32"),
-    "EB": ("sbuf", [128, 4 * K], "float32"),
-    "MM": ("sbuf", [128, 3 * K], "float32"),
-    "PR": ("sbuf", [128, K], "float32"),
-    "BS0": ("sbuf", [128, K], "float32"),
-    "DS": ("sbuf", [128, K], "float32"),
-    "DA": ("sbuf", [128, K], "float32"),
-    "DB": ("sbuf", [128, K], "float32"),
-    "T1": ("sbuf", [128, K], "float32"),
-    "T2": ("sbuf", [128, K], "float32"),
-    "T4": ("sbuf", [128, K], "float32"),
-    "T5": ("sbuf", [128, K], "float32"),
-    "C1": ("sbuf", [128, K], "float32"),
-    "C2": ("sbuf", [128, K], "float32"),
-    "C3": ("sbuf", [128, K], "float32"),
+    "Z": ("sbuf", [128, D0 + 4 * L3], "float32"),
+    "AB": ("sbuf", [128, 4 * L2], "float32"),
+    "EE": ("sbuf", [128, 4 * L2], "float32"),
+    "D1A": ("sbuf", [128, L3], "float32"),
+    "D1B": ("sbuf", [128, L3], "float32"),
+    "SB": ("sbuf", [128, L3], "float32"),
+    "C": ("sbuf", [128, L3], "float32"),
+    "KI": ("sbuf", [128, K + LIFT], "float32"),
     "YW": ("sbuf", [128, 4 * L2], "bfloat16"),
-    "NW": ("sbuf", [128, 4 * K], "bfloat16"),
-    "NVB": ("sbuf", [128, W + 4 * L2], "bfloat16"),
-    "POS": ("sbuf", [128, K], "bfloat16"),
-    "PN": ("sbuf", [128, K], "float32"),
-    "WO": ("sbuf", [128, 48], "float32"),
+    "NVB": ("sbuf", [128, 2 * W], "bfloat16"),
+    "NVD": ("dram", [3, 128, L2], "bfloat16"),
+    "G": ("sbuf", [128, 4 * K], "bfloat16"),
+    "GT": ("sbuf", [128, K], "bfloat16"),
     "BNI": ("sbuf", [128, K], "int32"),
     "BNF": ("sbuf", [128, K + 8], IDX),
     "ANI": ("sbuf", [128, 192], "int32"),
@@ -58,25 +72,98 @@ SCRATCH = {
     "FIN": ("sbuf", [128, 192], "uint16"),
     "PP": ("sbuf", [128, 8 * 48], "uint16"),
     "PI": ("sbuf", [128, 8 * 48], "uint16"),
-    "V1": ("sbuf", [128, 144], "float32"),
-    "V2": ("sbuf", [128, 144], "float32"),
-    "V0": ("sbuf", [128, 128], "float32"),
-    "MI": ("sbuf", [128, 128], "int32"),
     "E1": ("sbuf", [128, 5 * 144], "float32"),
     "E2": ("sbuf", [128, 4 * 144], IDX),
-    "EH": ("sbuf", [128, 288], IDX),
-    "ID": ("sbuf", [128, 128], "bfloat16"),
-    "IW": ("sbuf", [128, 128], "bfloat16"),
-    "MV": ("sbuf", [128, 128], "bfloat16"),
+    "EH": ("sbuf", [128, 3 * 144], IDX),
+    "EG": ("sbuf", [128, 6 * 144], "bfloat16"),
+    "MB": ("sbuf", [128, 10 * 128], "bfloat16"),
+    "MF": ("sbuf", [128, 2 * 128], "float32"),
+    "WO": ("sbuf", [128, 48], "float32"),
+    "WT": ("sbuf", [128, 2 * 192], "float32"),
     "RI": ("sbuf", [128, 4], "int32"),
-    "CS": ("sbuf", [128, 40], "float32"),
+    "CS": ("sbuf", [128, 72], "float32"),
 }
-NPOOL = 70
-ARR = (["yw%d" % t for t in (1, 2, 3)] + ["lv%d" % t for t in (1, 2, 3)]
+BYTES = {"float32": 4, "int32": 4, "bfloat16": 2, "float16": 2, "uint16": 2}
+NPOOL = 90
+ARR = (["yw%d" % t for t in (1, 2, 3)] + ["l%d_%d" % (s, t) for s in (0, 1) for t in (1, 2, 3)]
        + ["c%d_%d" % (r, t) for r in range(RO) for t in (1, 2, 3)]
        + ["pp%d_%d" % (r, t) for r in (1, 2) for t in (1, 2, 3)]
        + ["pi%d_%d" % (r, t) for r in (1, 2) for t in (1, 2, 3)])
 SEMAPHORES = ["qv", "qa", "qp", "qg"] + ARR + ["s%d" % i for i in range(NPOOL)]
+
+
+def step(r):
+    return r[3] if len(r) > 3 else 1
+
+
+def size(r):
+    return len(range(r[1], r[2], step(r)))
+
+
+def meet(x, y):
+    return x[1] < y[2] and y[1] < x[2] and (step(x) != step(y) or (x[1] - y[1]) % step(x) == 0)
+
+
+def covers(x, y):
+    return x[1] <= y[1] and y[2] <= x[2] and (step(x) == 1 or (step(y) == step(x) and (x[1] - y[1]) % step(x) == 0))
+
+
+def banks_of(regs):
+    return {b for r in regs if r[0] == "PS" for b in range(r[1] // 512, (r[2] - 1) // 512 + 1)}
+
+
+def issue_order(calls):
+    n = len(calls)
+    before, seen = [], {}
+    for i, c in enumerate(calls):
+        p = set(c["after"])
+        for regs, isw in ((c["reads"], False), (c["writes"], True)):
+            for r in regs:
+                p.update(j for (x, j, w) in seen.get(r[0], []) if (w or isw) and meet(x, r))
+        for r in c["writes"]:
+            seen[r[0]] = [x for x in seen.get(r[0], []) if not covers(r, x[0])] + [(r, i, True)]
+        for r in c["reads"]:
+            seen.setdefault(r[0], []).append((r, i, False))
+        p.discard(i)
+        before.append(p)
+    behind = [[] for _ in calls]
+    for i in range(n):
+        for j in before[i]:
+            behind[j].append(i)
+    span = [c["hold"] + c["lag"] + c["bytes"] for c in calls]
+    uses = [([(c["q"], 0.0, c["hold"])] if c["q"] != "x" else []) + ([(c["way"], c["hold"], c["bytes"])] if c["bytes"] else [])
+            + [(b, 0.0, c["hold"] + (SIG if c["q"] != "v" else 0.0)) for b in banks_of(c["reads"] + c["writes"])] for c in calls]
+
+    def lay(order, first, back):
+        busy, start = {}, [0.0] * n
+        for i in order:
+            s = max([start[j] + span[j] + (0.0 if calls[i]["q"] == calls[j]["q"] == "p" else SIG) for j in first[i]] + [0.0])
+            use = [(k, span[i] - a - d if back else a, d) for k, a, d in uses[i]]
+            moved = True
+            while moved:
+                moved = False
+                for k, a, d in use:
+                    for x, y in busy.get(k, ()):
+                        if x < s + a + d - 1e-9 and s + a < y - 1e-9:
+                            s, moved = y - a, True
+            for k, a, d in use:
+                busy.setdefault(k, []).append((s + a, s + a + d))
+                busy[k].sort()
+            start[i] = s
+        return start
+    order, kept = list(range(n)), None
+    if START:
+        late = lay(order[::-1], behind, True)
+        order = sorted(range(n), key=lambda i: (-late[i] - span[i], i))
+    for _ in range(PASSES):
+        start = lay(order, before, False)
+        t = max(start[i] + span[i] for i in range(n))
+        LOG.append(t)
+        if not kept or t < kept[0]:
+            kept = (t, sorted(range(n), key=lambda i: (start[i], i)))
+        late = lay(sorted(range(n), key=lambda i: (-start[i] - span[i], -i)), behind, True)
+        order = sorted(range(n), key=lambda i: (-late[i] - span[i], i))
+    return kept[1]
 
 
 def rank_program(g, core, T, topo):
@@ -88,75 +175,42 @@ def rank_program(g, core, T, topo):
     A_ = AluOpType
     F_ = ActivationFunctionType
     Q = {"g": g, "v": g.vector, "a": g.scalar, "p": g.tensor, "s": g.sync}
-    count = {"v": 0, "a": 0, "p": 0, "g": 0}
-    waited = {}
-    final = {}
-    acc = {}
-    banks = {}
+    calls = []
     pool = [0]
+    once = dict(ONCE)
 
     def newsem():
         pool[0] += 1
         return "s%d" % (pool[0] - 1)
 
-    def need(q, reads, writes):
-        want = {}
+    def call(q, fn, tok, reads, writes, hold, lag=0.0, nbytes=0.0, way=None, after=()):
+        calls.append(dict(q=q, fn=fn, tok=tok, reads=list(reads), writes=list(writes), hold=hold, lag=lag, bytes=nbytes,
+                          way=way, after=after))
 
-        def add(tok):
-            want[tok[0]] = max(want.get(tok[0], 0), tok[1])
-        for regs, isw in ((reads, False), (writes, True)):
-            for (n, c0, c1) in regs:
-                for (a0, a1, tok, w) in acc.get(n, []):
-                    if a0 < c1 and c0 < a1 and (w or isw):
-                        if tok[2] == q and isw and not SAME_WAR and q != "g":
-                            continue
-                        add(tok)
-                if n == "PS":
-                    for b in range(c0 // 512, (c1 - 1) // 512 + 1):
-                        for e, tok in banks.get(b, {}).items():
-                            if e != q:
-                                add(tok)
-        for s, v in want.items():
-            if waited.get((q, s), 0) < v:
-                Q[q].wait_ge(T.sem[s], v)
-                waited[(q, s)] = v
+    def op(q, fn, reads, writes, cycles):
+        call(q, fn, None, reads, writes, FIX + cycles * (PCYC if q == "p" else CYC))
 
-    def note(q, tok, reads, writes):
-        final[tok[0]] = max(final.get(tok[0], 0), tok[1])
-        for (n, c0, c1) in writes:
-            acc[n] = [x for x in acc.get(n, []) if not (c0 <= x[0] and x[1] <= c1 and (x[2][2] != q or q in "gsd" or SAME_WAR))]
-            acc[n].append((c0, c1, tok, True))
-        for (n, c0, c1) in reads:
-            acc[n] = [x for x in acc.get(n, []) if not (not x[3] and x[2][0] == tok[0] and c0 <= x[0] and x[1] <= c1)]
-            acc[n].append((c0, c1, tok, False))
-        for (n, c0, c1) in list(reads) + list(writes):
-            if n == "PS":
-                for b in range(c0 // 512, (c1 - 1) // 512 + 1):
-                    banks.setdefault(b, {})[q] = tok
-
-    def op(q, fn, reads, writes):
-        need(q, reads, writes)
-        count[q] += 1
-        fn().then_inc(T.sem["q" + q], 1)
-        note(q, ("q" + q, count[q], q), reads, writes)
-
-    def dma(q, out, in_, reads, writes, add=False):
-        need(q, reads, writes)
+    def dma(q, out, in_, reads, writes, nbytes, add=False):
         s = newsem()
-        if add:
-            Q[q].dma_start(out, in_, accum_op=A_.add).then_inc(T.sem[s], 16)
-        else:
-            Q[q].dma_start(out, in_).then_inc(T.sem[s], 16)
-        note("d", (s, 16, "d"), reads, writes)
 
-    def arrive(sem, n, reg):
-        note("d", (sem, n, "d"), [], [reg])
+        def fn():
+            ins = Q[q].dma_start(out, in_, accum_op=A_.add) if add else Q[q].dma_start(out, in_)
+            ins.then_inc(T.sem[s], 16)
+        call(q, fn, (s, 16, "d"), reads, writes, ISSUE[q], LAT["d"], nbytes * (2 if add else 1) / RATE["d"], "d")
+        if q == "g":
+            calls[-1]["hold"] += once.pop("dma", 0.0)
 
     def ap(r):
-        return T[r[0]][:, r[1]:r[2]]
+        return T[r[0]][:, r[1]:r[2]:r[3]] if len(r) > 3 else T[r[0]][:, r[1]:r[2]]
+
+    def nb(r):
+        return 128 * size(r) * BYTES[SCRATCH[r[0]][2]]
 
     def ind(win, off):
         return ap(win).indirect(ap(off))
+
+    def move(q, out, src, add=False):
+        dma(q, ap(out), ap(src), [src, out] if add else [src], [out], nb(out), add)
 
     def peer(d):
         return cores[(rank + d) % N]
@@ -173,11 +227,9 @@ def rank_program(g, core, T, topo):
     NE = len(topo.engines(core, peer(1)))
     NS_ = NE // 4
 
-    def send(items):
-        need("g", [r for it in items for r in it[1]], [])
+    def send(items, first=None):
         s = newsem()
         trs = []
-        tot = 0
         for (c, srcs, land, sem, i0, n) in items:
             if len(srcs) == 1:
                 trs.append(RemoteDMATransfer(dst_ids=[dst(c)], dma_engine_mask=emask(c, i0, n), remote_sem=T.sem[sem],
@@ -185,84 +237,174 @@ def rank_program(g, core, T, topo):
             else:
                 trs.append(RemoteDMATransfer(dst_ids=[dst(c)], dma_engine_mask=emask(c, i0, n), remote_sem=T.sem[sem],
                                              srcs=[ap(r) for r in srcs], dsts=[ap(land)], alu_op=1))
-            tot += n
-        g.remote_dma_fused(trs, local_sem=T.sem[s])
-        note("d", (s, tot, "d"), [r for it in items for r in it[1]], [])
+        call("g", lambda: g.remote_dma_fused(trs, local_sem=T.sem[s]), (s, sum(it[5] for it in items), "d"),
+             [r for it in items for r in it[1]] + cols(first), [], ISSUE["r"], LAT["r"] / 2, nb(items[0][2]) / items[0][5] / RATE["r"], "r")
+        calls[-1]["hold"] += once.pop("remote", 0.0)
+        me = len(calls) - 1
+        for it in items:
+            call("x", None, (it[3], it[5], "d"), [], [it[2]], 0.0, LAT["r"] / 2, after=(me,))
+
+    def issue():
+        count = {q: 0 for q in Q}
+        waited, final, acc, banks = {}, {}, {}, {}
+        if not ORDER:
+            ORDER.extend(issue_order(calls))
+        for i in ORDER:
+            c = calls[i]
+            q, tok = c["q"], c["tok"]
+            want = {}
+            for regs, isw in ((c["reads"], False), (c["writes"], True)):
+                for r in regs:
+                    for (x, k, w) in acc.get(r[0], []):
+                        if (w or isw) and meet(x, r) and not (q == "p" and k[2] == "p"):
+                            want[k[0]] = max(want.get(k[0], 0), k[1])
+            bs = banks_of(c["reads"] + c["writes"])
+            for b in bs:
+                for e, k in banks.get(b, {}).items():
+                    if e != q:
+                        want[k[0]] = max(want.get(k[0], 0), k[1])
+            if q != "x":
+                for s, v in want.items():
+                    if waited.get((q, s), 0) < v:
+                        Q[q].wait_ge(T.sem[s], v)
+                        waited[(q, s)] = v
+                if tok is None:
+                    count[q] += 1
+                    tok = ("q" + q, count[q], q)
+                    c["fn"]().then_inc(T.sem[tok[0]], 1)
+                else:
+                    c["fn"]()
+            final[tok[0]] = max(final.get(tok[0], 0), tok[1])
+            for r in c["writes"]:
+                acc[r[0]] = [x for x in acc.get(r[0], []) if not covers(r, x[0])] + [(r, tok, True)]
+            for r in c["reads"]:
+                acc[r[0]] = [x for x in acc.get(r[0], [])
+                             if not (not x[2] and x[1][0] == tok[0] and covers(r, x[0]))] + [(r, tok, False)]
+            for b in bs:
+                banks.setdefault(b, {})[q] = tok
+        for s, v in final.items():
+            if max([waited.get((q, s), 0) for q in Q]) < v:
+                g.wait_ge(T.sem[s], v)
+
+    def cols(*xs):
+        return [x for x in xs if isinstance(x, tuple)]
+
+    def val(x):
+        return ap(x) if isinstance(x, tuple) else x
 
     def tt(out, a, b, o):
-        op("v", lambda: g.vector.tensor_tensor(ap(out), ap(a), ap(b), o), [a, b], [out])
+        op("v", lambda: g.vector.tensor_tensor(ap(out), ap(a), ap(b), o), [a, b], [out],
+           size(out) * (1 if "PS" in (a[0], b[0]) else 2))
 
     def gtt(out, win, off, b, o):
-        op("v", lambda: g.vector.tensor_tensor(ap(out), ind(win, off), ap(b), o), [win, off, b], [out])
+        op("v", lambda: g.vector.tensor_tensor(ap(out), ind(win, off), ap(b), o), [win, off, b], [out], size(out) * GAT)
 
-    def ts(out, a, s1, s2, o0, o1=None):
-        rd = [a] + [s for s in (s1, s2) if isinstance(s, tuple)]
-        x1 = ap(s1) if isinstance(s1, tuple) else s1
-        x2 = ap(s2) if isinstance(s2, tuple) else s2
-        if o1 is None:
-            op("v", lambda: g.vector.tensor_scalar(ap(out), ap(a), x1, None, o0), rd, [out])
-        else:
-            op("v", lambda: g.vector.tensor_scalar(ap(out), ap(a), x1, x2, o0, o1), rd, [out])
+    def ts(out, a, s1, s2, o0, *o1):
+        op("v", lambda: g.vector.tensor_scalar(ap(out), ap(a), val(s1), val(s2), o0, *o1), cols(a, s1, s2), [out], size(out))
 
     def vcopy(out, a):
-        op("v", lambda: g.vector.tensor_copy(ap(out), ap(a)), [a], [out])
+        op("v", lambda: g.vector.tensor_copy(ap(out), ap(a)), [a], [out], size(out))
 
     def vgat(out, win, off):
-        op("v", lambda: g.vector.tensor_copy(ap(out), ind(win, off)), [win, off], [out])
+        op("v", lambda: g.vector.tensor_copy(ap(out), ind(win, off)), [win, off], [out], size(out) * GAT)
 
     def agat(out, win, off, scale=1.0):
-        op("a", lambda: g.scalar.activation(ap(out), ind(win, off), F_.Copy, scale=scale), [win, off], [out])
+        op("a", lambda: g.scalar.activation(ap(out), ind(win, off), F_.Copy, scale=scale), [win, off], [out],
+           size(out) * GAT)
 
-    def act(out, a, f, scale=1.0):
-        op("a", lambda: g.scalar.activation(ap(out), ap(a), f, scale=scale), [a], [out])
+    def act(out, a, f, scale=1.0, bias=None):
+        more = {} if bias is None else {"bias": ap(bias)}
+        op("a", lambda: g.scalar.activation(ap(out), ap(a), f, scale=val(scale), **more), cols(a, scale, bias), [out],
+           size(out))
+
+    def ascat(win, off, src):
+        op("a", lambda: g.scalar.activation(ind(win, off), ap(src), F_.Silu), [off, src], [win], size(src) * SCA)
+        calls[-1]["hold"] += once.pop("table", 0.0)
 
     def scan(out, d0, d1, init, o0, o1):
-        rd = [d0, d1] + ([init] if isinstance(init, tuple) else [])
-        x = ap(init) if isinstance(init, tuple) else init
-        op("v", lambda: g.vector.tensor_tensor_scan(ap(out), ap(d0), ap(d1), x, o0, o1), rd, [out])
+        op("v", lambda: g.vector.tensor_tensor_scan(ap(out), ap(d0), ap(d1), init, o0, o1), [d0, d1], [out], size(out))
 
     def iota(out, pat, base, cm, flt=True):
-        if flt:
-            op("g", lambda: g.iota(ap(out), pat, base, cm, allow_small_or_imprecise_dtypes=True), [], [out])
-        else:
-            op("g", lambda: g.iota(ap(out), pat, base, cm), [], [out])
+        more = {"allow_small_or_imprecise_dtypes": True} if flt else {}
+        op("g", lambda: g.iota(ap(out), pat, base, cm, **more), [], [out], 100 + 2 * size(out))
 
-    def place(out, lhs, src):
-        need("p", [lhs, src], [out])
+    def fill(out, v):
+        iota(out, [[0, size(out)]], v, 0)
+
+    def select(reg, pat, o, v, base, cm):
+        op("g", lambda: g.affine_select(ap(reg), ap(reg), pat, o, v, base, cm), [reg], [reg], 150 + 2 * size(reg))
+
+    def matmuls(out, rd, todo, start, stop):
+        grp = [("GRP", b, b + 1) for b in banks_of([out])]
+        shut = start and stop
+
+        def fn():
+            ins = None
+            for (o, lhs, rhs, st, sp) in todo:
+                ins = g.tensor.matmul(o, lhs, rhs, st, sp)
+            return ins
+        n = sum(max(64, o.shape[1]) for (o, lhs, rhs, st, sp) in todo)
+        op("p", fn, rd + (grp if shut else []), [out] + ([] if shut else grp), n * (4 if SCRATCH[rd[0][0]][2] == "float32" else 1))
+
+    def place(out, lhs, src, start=True, stop=True, parts=128):
         cuts = [out[1]] + [b for b in range(0, 4096, 512) if out[1] < b < out[2]] + [out[2]]
-        ins = None
+        k = step(src)
+        todo = []
         for c0, c1 in zip(cuts[:-1], cuts[1:]):
-            s0 = src[1] + c0 - out[1]
-            ins = g.tensor.matmul(T.PS[:, c0:c1], ap(lhs), T[src[0]][:, s0:s0 + c1 - c0], True, True)
-        count["p"] += 1
-        ins.then_inc(T.sem.qp, 1)
-        note("p", ("qp", count["p"], "p"), [lhs, src], [out])
+            s0 = src[1] + k * (c0 - out[1])
+            todo.append((T.PS[:, c0:c1], T[lhs[0]][0:parts, lhs[1]:lhs[2]],
+                         T[src[0]][0:parts, s0:s0 + k * (c1 - c0 - 1) + 1:k], start, stop))
+        matmuls(out, [lhs, src], todo, start, stop)
 
-    def wrap(c0, terms, parts=128):
-        n = (terms[0][0][2] - terms[0][0][1]) // 16
+    slot = [0]
+
+    def wrap(terms, parts=128, start=True, c0=None):
+        if c0 is None:
+            c0 = B7 + 96 * slot[0]
+            slot[0] = (slot[0] + 1) % 3
+        n = size(terms[0][0]) // 16
         out = ("PS", c0, c0 + n)
-        rd = [x for tm in terms for x in tm]
-        need("p", rd, [out])
-        ins = None
-        for j, (src, em) in enumerate(terms):
-            for i in range(16):
-                e0 = em[1] + 15 - i
-                ins = g.tensor.matmul(ap(out), T[em[0]][0:parts, e0:e0 + 128],
-                                      T[src[0]][0:parts, src[1] + i:src[2]:16], i == 0 and j == 0,
-                                      i == 15 and j == len(terms) - 1)
-        count["p"] += 1
-        ins.then_inc(T.sem.qp, 1)
-        note("p", ("qp", count["p"], "p"), rd, [out])
+        each = [(src, em, i) for src, em, which in terms for i in which]
+        todo = [(ap(out), T[em[0]][0:parts, em[1] + 15 - i:em[1] + 143 - i], T[src[0]][0:parts, src[1] + i:src[2]:16],
+                 start and j == 0, j == len(each) - 1) for j, (src, em, i) in enumerate(each)]
+        matmuls(out, [x for tm in terms for x in tm[:2]], todo, start, True)
         return out
+    ALL = range(16)
 
-    def U(n, t=0):
-        return (n, K * t, K * t + K)
+    def cut(r, c, n=K):
+        w = (3 * size(r) if len(r) > 3 else size(r))
+        return (r[0], r[1] + c[0] * w // n, min(r[2], r[1] + c[1] * w // n)) + tuple(r[3:])
+
+    def half(r, i, n=2):
+        return cut(r, (i, i + 1), n)
+
+    def lane(n, base, k):
+        return (n, base + k, base + L3, 3)
+
+    def U(n, i=0):
+        return (n, K * i, K * i + K)
+
+    def zr(c0, n=K):
+        return ("Z", c0, c0 + n)
+
+    def cs(c, n=1):
+        return ("CS", c, c + n)
 
     def E1(r):
-        return ("E1", 144 * r, 144 * r + 144)
-    X = [("PS", K * i, K * i + K) for i in range(5)]
-    B6, B7 = 3072, 3840
-    CUT = ((0, 512), (512, K))
+        i = (ROW_F[3], ROW_FIN) + ROW_N
+        return ("E1", 144 * i.index(r), 144 * i.index(r) + 144)
+
+    def EG(r):
+        return ("EG", 144 * (r - 2), 144 * (r - 2) + 144)
+    ID, IB, MVN, MVC, BN_, BC_ = [("MB", 128 * i, 128 * i + 128) for i in range(6)]
+    ONE = ("MB", 768, 1280)
+    IDF, NIF = ("MF", 0, 128), ("MF", 128, 256)
+    EX = [("PS", X0, X0 + K), ("PS", 1024 + X0, 1024 + X0 + K)]
+    XW, XU = ("PS", 2048, 2048 + K), ("PS", 2048 + K, 2048 + L2)
+    B7 = 3584
+    CUTU = ((0, 256), (256, K))
+    CUT = ((0, 512 - X0), (512 - X0, K))
+    CUTW = ((0, 512), (512, K))
 
     def names(t):
         return ("LS" if t == 0 else "LV", 96 * t, 96 * t + 96)
@@ -270,361 +412,393 @@ def rank_program(g, core, T, topo):
     def fwd(t):
         return names(0) if t == 0 else ("FL", 96 * t, 96 * t + 96)
 
-    def half(r, i, n=2):
-        w = (r[2] - r[1]) // n
-        return (r[0], r[1] + i * w, r[1] + (i + 1) * w)
+    def nxt(t):
+        return ("NL", 96 * t, 96 * t + 96)
 
     def pl(n, r, t):
         c = 48 * (4 * (r - 1) + t)
         return (n, c, c + 48)
-    LOCW = ("LOC", 0, W)
-    VA = ("NVB", 0, W)
+    LOC = zr(Q0B, W)
+    GB, IO = ("SB", 0, L2), ("D1A", 0, L2)
+    VA, TH, N3, TMP = ("NVB", 0, W), ("NVB", W, 2 * W), ("NVB", W, W + L2), ("NVB", W + L2, 2 * W)
+    POS, NV3 = half(TMP, 0), half(TMP, 1)
+    PN = zr(Q0B)
+    ST = ("BNF", 8, 8 + K)
+    V0, V1, V2 = ("D1B", 0, 128), ("D1B", 128, 272), ("D1B", 272, 416)
 
-    def nva(t):
-        return ("NVB", W + L2 * t, W + L2 * (t + 1))
+    def AA(t):
+        return U("AB", 2 * t)
 
-    dma("s", T.BNI[0:32, :], T.bn[:], [], [U("BNI")])
-    dma("a", T.ANI[:], T.an[:], [], [("ANI", 0, 192)])
-    iota(("V2", 0, 144), [[16, 9], [1000, 16]], 0, -4)
+    def BB(r, t):
+        return zr(BS0) if r == 0 and t == 0 else U("AB", 2 * t + 1)
+
+    def EA(t):
+        return U("EE", 2 * t)
+
+    def EB(t):
+        return U("EE", 2 * t + 1)
+
+    def CC(t):
+        return U("C", t - 1)
+
+    dma("s", T.BNI[0:32, :], T.bn[:], [], [U("BNI")], nb(U("BNI")) / 2)
+    dma("a", T.ANI[:], T.an[:], [], [("ANI", 0, 192)], nb(("ANI", 0, 192)))
+    for q, out, src in (("s", TH, T.th), ("s", ("YW", 0, K), T.yt), ("s", ("YW", K, L2), T.wt), ("g", zr(0, W), T.th),
+                        ("s", VA, T.va)):
+        dma(q, ap(out), src[:], [], [out], nb(out))
     iota(("RI", 0, 4), [[0, 4]], 0, 1, False)
-    iota(("CS", 0, 4), [[1, 4]], 0, 0)
-    iota(("V1", 0, 144), [[16, 9], [1000, 16]], 0, -1)
-    iota(("V0", 0, 128), [[1, 128]], 0, -1)
-    TH = ("NVB", W, 2 * W)
-    dma("s", ap(TH), T.th[:], [], [TH])
-    dma("g", T.Z[:, 0:W], T.th[:], [], [("Z", 0, W)])
-    iota(("KI", 0, L2), [[1, L2]], 0, 0)
-    iota(("MI", 0, 128), [[-16, 8], [0, 16]], 128, 1, False)
-    dma("s", T.YW[:, 0:K], T.yt[:], [], [("YW", 0, K)])
-    dma("s", T.YW[:, K:L2], T.wt[:], [], [("YW", K, L2)])
-    dma("s", T.NVB[:, 0:W], T.va[:], [], [VA])
-    op("v", lambda: g.vector.memset(T.POS[:], 1.0), [], [U("POS")])
-
-    def cols(t):
-        scan(U("LOC", t), U("POS"), U("POS"), float(K * t - 1), A_.mult, A_.add)
-
-    def ids(t, src, out):
-        op("a", lambda: g.scalar.activation(ap(out), ap(src), F_.Identity, bias=T.CS[:, 36 + t:37 + t],
-                                            scale=T.CS[:, 24 + t:25 + t]),
-           [src, ("CS", 24, 40)], [out])
-
-    def index(out, src):
-        ts(out, src, 0.25, None, A_.add)
-    cols(0)
-    ts(("RI", 0, 4), ("RI", 0, 4), 15, None, A_.bitwise_and)
-    ts(("CS", 8, 12), ("CS", 0, 4), -float(L2), float(QB(0)), A_.mult, A_.add)
-    vcopy(("CS", 4, 8), ("RI", 0, 4))
-    ts(("CS", 12, 16), ("CS", 0, 4), float(2 * L2), float(FB(0) - QB(0)), A_.mult, A_.add)
-    tt(("CS", 16, 20), ("CS", 0, 4), ("CS", 4, 8), A_.subtract)
-    ts(("CS", 20, 24), ("CS", 4, 8), 0.0, None, A_.is_equal)
-    ts(("CS", 24, 28), ("CS", 16, 20), -2.5, None, A_.is_gt)
-    ts(("CS", 28, 32), ("CS", 16, 20), -2.0, ("CS", 20, 21), A_.is_equal, A_.add)
-    tt(("CS", 32, 36), ("CS", 24, 28), ("CS", 8, 12), A_.mult)
-    tt(("CS", 28, 32), ("CS", 28, 32), ("CS", 12, 16), A_.mult)
-    ts(("E2", 0, 144), ("V2", 0, 144), 15000.0, None, A_.is_equal)
-    tt(("CS", 36, 40), ("CS", 32, 36), ("CS", 28, 32), A_.add)
-    cols(1)
-    ids(0, ("LOC", 0, L2), ("IO", 0, L2))
+    iota(cs(0, 4), [[1, 4]], 0, 0)
+    iota(V2, [[16, 9], [1000, 16]], 0, -4)
+    iota(V1, [[16, 9], [1000, 16]], 0, -1)
+    iota(V0, [[1, 128]], 0, -1)
+    op("v", lambda: g.vector.memset(T.GT[:], 1.0), [], [U("GT")], K / 2)
+    op("v", lambda: g.vector.memset(T.CS[:, 60:64], -float(LIFT)), [], [cs(60, 4)], 4)
+    scan(("KI", 0, K), U("GT"), U("GT"), -1.0, A_.mult, A_.add)
+    ts(("KI", K, K + LIFT), ("KI", 0, LIFT), float(K), None, A_.add)
+    ts(("RI", 0, 1), ("RI", 0, 1), 7, None, A_.bitwise_and)
+    ts(("RI", 1, 2), ("RI", 1, 2), 15, None, A_.bitwise_and)
+    vcopy(cs(4, 2), ("RI", 0, 2))
+    ts(cs(64, 4), cs(0, 4), float(K), float(LIFT), A_.mult, A_.add)
+    for u in range(LOCA):
+        act(half(LOC, u, 4), ("KI", 0, K), F_.Silu, 1.0, cs(64 + u))
+        calls[-1]["hold"] += once.pop("table", 0.0)
+    for u in range(LOCA, 4):
+        scan(half(LOC, u, 4), U("GT"), U("GT"), float(K * u + LIFT - 1), A_.mult, A_.add)
+    ts(cs(8, 4), cs(0, 4), cs(4), None, A_.subtract)
+    ts(cs(6), cs(4), 0.5, None, A_.is_gt)
+    ts(cs(7), cs(4), 4.5, cs(6), A_.is_lt, A_.mult)
+    ts(cs(20, 4), cs(8, 4), -4.5, None, A_.is_lt)
+    ts(cs(24, 4), cs(8, 4), -2.0, cs(7), A_.is_equal, A_.mult)
+    tt(cs(20, 4), cs(20, 4), cs(24, 4), A_.add)
+    ts(cs(28, 4), cs(8, 4), -1.5, cs(7), A_.is_gt, A_.mult)
+    ts(cs(12, 4), cs(0, 4), float(L2), float(FB(0) + LIFT), A_.mult, A_.add)
+    ts(cs(16, 4), cs(0, 4), -float(W), float(QV(0) + LIFT + 2), A_.mult, A_.add)
+    tt(cs(12, 4), cs(12, 4), cs(20, 4), A_.mult)
+    tt(cs(16, 4), cs(16, 4), cs(28, 4), A_.mult)
+    tt(cs(40, 4), cs(12, 4), cs(16, 4), A_.add)
+    tt(cs(36, 4), cs(20, 4), cs(28, 4), A_.add)
+    ts(cs(68, 4), cs(28, 4), 2.0, None, A_.mult)
+    tt(cs(32, 4), cs(36, 4), cs(68, 4), A_.add)
+    ts(cs(48, 4), cs(36, 4), float(K), None, A_.mult)
+    ts(cs(52, 4), cs(28, 4), float(L2 - 2), None, A_.mult)
+    tt(cs(48, 4), cs(48, 4), cs(40, 4), A_.add)
+    tt(cs(44, 4), cs(48, 4), cs(52, 4), A_.add)
     op("v", lambda: g.vector.tensor_scalar(T.BNF[0:32, 0:K], T.BNI[0:32, :], -float(OFF), None, A_.add),
-       [U("BNI")], [U("BNF")])
-    for u in range(1, 4):
-        ts(("E2", 144 * u, 144 * u + 144), ("V2", 0, 144), float(15000 - 4 * u), None, A_.is_equal)
-    wr = [wrap(512 * t, [(U("BNF"), ("E2", 144 * t, 144 * t + 144))], 32) for t in range(4)]
-    cols(2)
-    cols(3)
+       [U("BNI")], [U("BNF")], K)
     for t in range(4):
+        e2 = ("E2", 144 * t, 144 * t + 144)
+        ts(e2, V2, float(15000 - 4 * t), None, A_.is_equal)
         vcopy(("LS", 96 * t, 96 * t + 48), ("ANI", 48 * t, 48 * t + 48))
-        ts(("LS", 96 * t + 48, 96 * t + 96), wr[t], float(OFF), None, A_.add)
-    send([(peer(t), [("LS", 96 * t, 96 * t + 96)], ("LV", 96 * t, 96 * t + 96), "lv%d" % t, NS_ * (t - 1), NS_)
-          for t in (1, 2, 3)])
+        ts(("LS", 96 * t + 48, 96 * t + 96), wrap([(U("BNF"), e2, ALL)], 32, True, 512 * t), float(OFF), None, A_.add)
+    for s in range(2):
+        send([(peer(t), [half(("LS", 96 * t, 96 * t + 96), s)], half(names(t), s), "l%d_%d" % (s, t), NS_ * (t - 1), NS_)
+              for t in (1, 2, 3)])
+    act(("YW", K, L2), ("YW", K, L2), F_.Copy, -0.125)
     for t in (1, 2, 3):
-        send([(peer(t), [("YW", 0, L2)], ("YW", L2 * t, L2 * t + L2), "yw%d" % t, 0, NE)])
-        arrive("lv%d" % t, NS_, names(t))
-        arrive("yw%d" % t, NE, ("YW", L2 * t, L2 * t + L2))
+        send([(peer(t), [("YW", 0, L2)], ("YW", L2 * t, L2 * t + L2), "yw%d" % t, 0, NE)], first=("LS", 96, 384))
 
-    def consts():
-        ts(("ID", 0, 128), ("V0", 0, 128), 0.0, None, A_.is_equal)
-        ts(("IW", 0, 128), ("V0", 0, 128), 0.0, -0.125, A_.is_equal, A_.mult)
-        ts(E1(0), ("V1", 0, 144), 15000.0, None, A_.is_equal)
+    def picks(reg, rows):
+        for r in rows:
+            select(reg, [[16, 9], [1000, 16]], A_.not_equal, 1.0, r - 15000, -1)
+    ts(ID, V0, 0.0, -1.0 if PE_E else 1.0, A_.is_equal, A_.mult)
+    ts(IB, V0, 0.0, None, A_.is_equal)
+    ts(IDF, V0, 0.0, None, A_.is_equal)
+    ts(E1(ROW_F[3]), V1, float(15000 - ROW_F[3]), None, A_.is_equal)
+    ts(("EH", 0, 144), V1, 15000.0, None, A_.is_equal)
+    ts(("EH", 144, 288), V1, 15000.0, -1.0, A_.is_equal, A_.mult)
+    ts(("WO", 0, 48), ("KI", 0, 48), 16.0, cs(5), A_.mult, A_.add)
+    ts(cs(56), cs(5), 7.5, -1.0, A_.is_gt, A_.mult)
+    ts(("BNF", 7, 8), cs(60), 0.0, NONE, A_.mult, A_.add)
+    vcopy(("EH", 288, 289), ("EH", 0, 1))
+    tt(("EH", 289, 432), ("EH", 145, 288), ("EH", 0, 143), A_.add)
+    fill(NIF, 0)
+    select(NIF, [[1, 128]], A_.not_equal, -1.0, 0, -1)
 
-    def later():
-        ts(("MI", 0, 128), ("MI", 0, 128), 4, 7, A_.arith_shift_right, A_.bitwise_and)
-        for r in range(1, 5):
-            ts(E1(r), ("V1", 0, 144), float(15000 - r), None, A_.is_equal)
-        ts(("EH", 0, 144), ("V1", 0, 144), 15000.0, None, A_.is_equal)
-        ts(("EH", 144, 288), ("V1", 0, 144), 15000.0, -1.0, A_.is_equal, A_.mult)
-        op("v", lambda: g.vector.memset(T.CS[:, 8:12], -64.0), [], [("CS", 8, 12)])
-        ts(("WO", 0, 48), ("KI", 0, 48), 16.0, ("CS", 4, 5), A_.mult, A_.add)
-        ts(("MV", 0, 128), ("MI", 0, 128), 1.5, None, A_.is_lt)
+    def factors(t):
+        fill(lane("Z", D0 + L3 * t, 0), 0)
+        w2, wt = lane("Z", D0 + L3 * t, 2), ("YW", L2 * t + K, L2 * t + L2)
+        if GLANE:
+            op("g", lambda: g.affine_select(ap(w2), ap(wt), [[0, K]], A_.is_ge, 0.0, 0, 0), [wt], [w2], 150 + 2 * K)
+        else:
+            act(w2, wt, F_.Copy)
+    for t in (3, 2, 1):
+        factors(t)
+    for r in ROW_N + (ROW_FIN,):
+        fill(E1(r), 0)
+        picks(E1(r), [r])
+    for r in range(2, 8):
+        fill(EG(r), 0)
+        picks(EG(r), [r, r + 8])
+    for m, b, v in ((MVN, BN_, int(BIG)), (MVC, BC_, -int(BIG))):
+        fill(m, v)
+        fill(b, -33 * v // 2)
+        select(m, [[-16, 8], [0, 16]], A_.is_ge, 0.0, 0, 1)
+        select(m, [[16, 8], [0, 16]], A_.is_ge, 0.0, 31, -1)
+        select((m[0], m[1] + 112, m[2]), [[0, 16]], A_.is_ge, float(v), -16, 1)
+    fill(ONE, 1)
 
-    def yw(t):
-        Xy, Xw = (X[0], X[1]) if t % 2 else (X[2], X[3])
-        place(Xy, ("ID", 0, 128), ("YW", L2 * t, L2 * t + K))
-        place(Xw, ("IW", 0, 128), ("YW", L2 * t + K, L2 * t + L2))
+    def ids(t, s, out):
+        if (t, s) in IDV:
+            ts(out, ("KI", 0, K), cs(32 + 4 * s + t), cs(40 + 4 * s + t), A_.mult, A_.add)
+        else:
+            act(out, ("KI", 0, K), F_.Identity, cs(32 + 4 * s + t), cs(40 + 4 * s + t))
 
-    def squares(t):
-        Xa, Xb = (X[2], X[3]) if t % 2 else (X[0], X[1])
-        act(Xa, U("BB", t), F_.Square)
-        act(Xb, U("AB", t), F_.Square)
+    def index(out, src, base):
+        ts(out, src, 0.25 - LIFT - base, None, A_.add)
 
-    def inits(r):
-        for t in ((2, 1, 0) if r < RO - 1 else (2, 1, 0, -1, -2)):
-            z = ("Z", FB(t), FB(t) + L2)
-            s = ("NVB", z[1], z[2])
-            dma("g", ap(z), ap(s), [s, z], [z], add=True)
+    def index_n(t, out, src):
+        if t == 0:
+            x = ("WT", 0, size(src))
+            ts(x, src, QV(1) + LIFT - 0.5, float(QA(1) - QV(1)), A_.is_gt, A_.mult)
+            tt(x, src, x, A_.add)
+            src = x
+        index(out, src, FB(t))
 
-    def errors(P, Xy, A, B, EA, EB):
+    def minus_va(r, t):
+        z = zr(FB(t), L2)
+        dma("g", ap(z), T.NVD[t], [("NVD", t, t + 1), z], [z], nb(z), True)
+
+    def keep_va(t):
+        for s in range(2):
+            agat(half(TMP, s), VA, half(names(t), s), -1.0)
+        dma("s", T.NVD[t], ap(TMP), [TMP], [("NVD", t, t + 1)], nb(TMP))
+
+    def split(t, x):
+        act(U("GT"), x, F_.Copy, cs(56))
+        move("g", x, U("GT"), True)
+        move("g", U("G", t), x)
+
+    def compose(r, t):
+        agat(U("GT"), U("G", t), pl("PP", r, t))
+        if t > 0:
+            index(half(fwd(t), 1), wrap([(U("GT"), EG(ROW_F[t]), ALL)]), 0)
+        if t < 3:
+            index_n(t, half(nxt(t), 1), wrap([(U("GT"), EG(ROW_N[t]), ALL)]))
+
+    def pointers(t):
+        for s in range(2):
+            o, a = half(names(t), s), half(GB, s)
+            b = half(IO, s) if t < 3 else (EX[0], XU)[s]
+            ids(t, s, b)
+            if t == 0:
+                ascat(LOC, o, b)
+            elif t < 3:
+                op("v", lambda o=o, a=a, b=b: g.vector.tensor_tensor(ind(LOC, o), ap(a), ap(b), A_.max), [o, a, b], [LOC],
+                   K * SCA)
+            else:
+                tt(a, b, a, A_.max)
+                ascat(LOC, o, a)
+        if t < 3:
+            for s in (1, 0):
+                agat(half(GB, s), LOC, half(names(t + 1), s))
+            index(fwd(t + 1), wrap([(GB, E1(ROW_F[3]), ALL)]), 0)
+        if t == 2:
+            move("s", U("AB", 1), half(GB, 1))
+            split(3, U("AB", 1))
+
+    def back_pointers(t, a, b):
+        for s, x in enumerate((a, b)):
+            agat(x, LOC, half(names(t), s))
+        if a[2] == b[1]:
+            index_n(t, nxt(t), wrap([((a[0], a[1], b[2]), E1(ROW_N[t]), ALL)]))
+        else:
+            for s, x in enumerate((a, b)):
+                index_n(t, half(nxt(t), s), wrap([(x, E1(ROW_N[t]), ALL)]))
+        split(t, b)
+
+    def fin():
         for i in range(2):
-            tt(half(Xy, i), half(P, i), half(Xy, i), A_.subtract)
-        for i in range(2):
-            tt(half(EA, i), half(Xy, i), half(A, i), A_.mult)
-        tt(EB, Xy, B, A_.mult)
+            wrap([(half(LOC, i), E1(ROW_FIN), ALL)], c0=B7 + 320 + 96 * i)
+        w = ("PS", B7 + 320, B7 + 512)
+        x, y = ("WT", 0, 192), ("WT", 192, 384)
+        ts(x, w, QV(1) + LIFT - 0.5, float(QA(1) - QV(1)), A_.is_gt, A_.mult)
+        ts(y, w, QV(0) + LIFT - 0.5, float(QA(0) - QV(0) - QA(1) + QV(1)), A_.is_gt, A_.mult)
+        tt(x, w, x, A_.add)
+        tt(x, x, y, A_.add)
+        ts(y, w, QV(0) + L3 + LIFT - 0.5, float(QB(0) - L3 - QA(0)), A_.is_gt, A_.mult)
+        tt(x, x, y, A_.add)
+        index(("FIN", 0, 192), x, 0)
 
     def forward(r, t):
-        Xy, Xw = (X[0], X[1]) if t % 2 else (X[2], X[3])
-        zw = ("Z", 0, FB(t))
+        last = r == RO - 1
+        Xy = EX[t % 2]
+        zw = TH if r == 0 and t == 0 else ("Z", 0, FB(t))
         fa, fb = half(fwd(t), 0), half(fwd(t), 1)
-        A, B, EA, EB = U("AB", t), U("BB", t), U("EA", t), U("EB", t)
-        oa, ob = ("Z", FB(t), FB(t) + K), ("Z", FB(t) + K, FB(t) + L2)
-        P = U("PR")
+        A, B = AA(t), BB(r, t)
+        oa, ob = zr(FB(t)), zr(FB(t) + K)
+        P = lane("Z", D0 + L3 * t, 1) if t > 0 or last else U("D1B", 1)
+        place(Xy, ID, ("YW", L2 * t, L2 * t + K), True, not PE_E)
+        place(XW, IB, ("YW", L2 * t + K, L2 * t + L2), True, not (ACC and t == 3))
+        if r == 0 and t == 0:
+            agat(A, zw, fa)
+            vgat(B, zw, fb)
+        elif t == 0:
+            pp = pl("PP", r, 0)
+            agat(B, zr(BS0), pp)
+        else:
+            for c in CUT:
+                agat(cut(B, c), zw, cut(fb, c))
+            for c in CUT:
+                agat(cut(A, c), zw, cut(fa, c))
+        for c in CUT:
+            if r > 0 and t == 0:
+                gtt(cut(P, c), zr(BS0), cut(pp, c), cut(A, c), A_.mult)
+            else:
+                gtt(cut(P, c), zw, cut(fa, c), cut(B, c), A_.mult)
+            if PE_E:
+                place(cut(Xy, c), IDF, cut(P, c), False, True)
+            else:
+                tt(cut(Xy, c), cut(P, c), cut(Xy, c), A_.subtract)
         if r == 0:
-            GB, IO = ("GB", 0, L2), ("IO", 0, L2)
-            wf = ("PS", B6, B6 + 96)
-
-            def mark(i, n):
-                o, a, b = half(names(t), i, n), half(GB, i, n), half(IO, i, n)
-                op("v", lambda: g.vector.tensor_tensor(ind(LOCW, o), ap(a), ap(b), A_.max), [o, a, b], [LOCW])
-
-            def smark(src):
-                op("a", lambda: g.scalar.activation(ind(LOCW, names(t)), ap(src), F_.Silu), [names(t), src], [LOCW])
-            if t == 0:
-                zw = TH
-                agat(A, zw, fa)
-                smark(IO)
-                vgat(B, zw, fb)
-                consts()
-                yw(0)
-            elif t == 1:
-                yw(1)
-                mark(0, 2)
-                index(fwd(1), wf)
-                agat(B, zw, fb)
-                agat(A, zw, fa)
-                mark(1, 2)
-            elif t == 2:
-                yw(2)
-                agat(B, zw, fb)
-                agat(A, zw, fa)
-                mark(0, 1)
-            else:
-                yw(3)
-                agat(A, zw, fa)
-                vgat(B, zw, fb)
-                ids(3, ("KI", 0, L2), ("PS", X[2][1], X[3][2]))
-                agat(nva(3), VA, names(3), -1.0)
-            if t < 3:
-                agat(GB, LOCW, names(t + 1))
-                wrap(B6, [(GB, E1(0))])
-                if t < 2:
-                    ids(t + 1, ("KI", 0, L2), IO)
-                if t > 0:
-                    for u in ((1,) if t == 1 else (0, 2)):
-                        agat(nva(u), VA, names(u), -1.0)
-                    for u in ((0, 1) if t == 1 else (2,)):
-                        act(U("NW", u), ("YW", L2 * u + K, L2 * u + L2), F_.Copy, -0.125)
-                if t == 1:
-                    act(U("BS0"), U("BB", 0), F_.Copy)
-            for i in range(2):
-                gtt(half(P, i), zw, half(fa, i), half(B, i), A_.mult)
-            if t == 3:
-                inits(r)
-            errors(P, Xy, A, B, EA, EB)
-            if t < 3:
-                if t > 0:
-                    tt(U("MM", t), Xy, P, A_.add)
-                tt(Xy, EA, Xw, A_.mult)
-                tt(Xw, EB, Xw, A_.mult)
-                tt(ob, Xy, B, A_.add)
-                if t > 0:
-                    index(fwd(t + 1), wf)
-                tt(oa, Xw, A, A_.add)
-                if t == 0:
-                    later()
-            else:
-                tt(GB, ("PS", X[2][1], X[3][2]), GB, A_.max)
-                squares(3)
-                act(U("NW", t), ("YW", L2 * t + K, L2 * t + L2), F_.Copy, -0.125)
-                smark(GB)
-                agat(GB, LOCW, names(2))
-                agat(IO, LOCW, names(1))
-                tt(X[4], EA, Xw, A_.mult)
-                tt(Xy, Xy, P, A_.add)
-                tt(Xw, EB, Xw, A_.mult)
-                tt(X[4], X[4], B, A_.add)
-                tt(Xw, Xw, A, A_.add)
-                tt(U("DB"), X[4], half(nva(3), 1), A_.add)
-                tt(U("DA"), Xw, half(nva(3), 0), A_.add)
-            return
-        pp, pi = pl("PP", r, t), pl("PI", r, t)
-        Bs = U("BS0") if t == 0 else U("DS")
-        if t > 0:
-            arrive("pp%d_%d" % (r, t), NS_, pp)
-            arrive("pi%d_%d" % (r, t), NS_, pi)
-            agat(Bs, zw, fb)
-            if t > 1 or r == RO - 1:
-                Xp = X[2] if t % 2 else X[0]
-                tt(U("MM", t - 1), Xp, P, A_.add)
-                vgat(half(A, 0), zw, half(fa, 0))
-                agat(half(A, 1), zw, half(fa, 1))
-            else:
-                vgat(A, zw, fa)
-            if t == 3:
-                inits(r)
-        else:
-            yw(0)
-        agat(B, Bs, pp)
-        if t == 0:
-            op("a", lambda: g.scalar.activation(ind(U("T5"), pp), T.KI[:, 64:64 + K], F_.Silu),
-               [pp, ("KI", 64, 64 + K)], [U("T5")])
-            op("a", lambda: g.scalar.activation(ap(U("BNF")), ap(U("T5")), F_.Identity, bias=T.CS[:, 8:9]),
-               [U("T5"), ("CS", 8, 9)], [U("BNF")])
-            wi = wrap(B7, [(U("BNF"), ("EH", 0, 144))])
+            pointers(t)
+            if t == 1:
+                for s in range(2):
+                    agat(half(N3, s), VA, half(names(3), s), -1.0)
+                for u in VAORDER:
+                    keep_va(u)
+        elif t == 0:
+            ascat(U("D1B"), pp, ("KI", LIFT, LIFT + K))
+            act(ST, U("D1B"), F_.Identity, 1.0, cs(60))
+            ts(pl("PI", r, 0), wrap([(ST, ("EH", 0, 144), ALL)]), 3.0, 2.25, A_.mult, A_.add)
+            send([(peer(u), [pl("PI", r, 0)], pl("PI", r, u), "pi%d_%d" % (r, u), NS_ * (u - 1), NS_) for u in (1, 2, 3)])
+            for u in (1, 2, 3, 0):
+                compose(r, u)
+            agat(NV3, half(N3, 1), pl("PP", r, 3))
             if r == 1:
-                agat(U("PN"), ("KI", 0, L2), pp)
-        if t < 3:
-            yw(t + 1)
-        else:
-            place(X[4], ("ID", 0, 128), half(nva(3), 1))
-            squares(3)
-        if r == 1 and t == 1:
-            wrap(B6, [(LOCW, E1(1))])
-        for i in range(2):
-            gtt(half(P, i), Bs, half(pp, i), half(A, i), A_.mult)
-        errors(P, Xy, A, B, EA, EB)
-        tt(U("T4"), EA, Xw, A_.mult)
+                for u in range(4):
+                    act(half(VA, u, 4), half(VA, u, 4), F_.Copy, -1.0)
         if t == 3:
-            tt(Xy, Xy, P, A_.add)
-        if r == 1 and t == 2:
-            index(("FIN", 0, 192), ("PS", B6, B6 + 192))
-        tt(Xw, EB, Xw, A_.mult)
-        if t == 0:
-            tt(half(oa, 0), half(Xw, 0), half(A, 0), A_.add)
-            ts(pi, wi, 0.25, None, A_.add)
-            send([(peer(u), [pi], pl("PI", r, u), "pi%d_%d" % (r, u), NS_ * (u - 1), NS_) for u in (1, 2, 3)])
-            tt(half(oa, 1), half(Xw, 1), half(A, 1), A_.add)
-            gtt(ob, U("T4"), pi, Bs, A_.add)
-        elif t < 3:
-            gtt(ob, U("T4"), pi, Bs, A_.add)
-            tt(oa, Xw, A, A_.add)
+            for u in (2, 1, 0):
+                minus_va(r, u)
+            if last:
+                for i in range(2):
+                    move("g", half(zr(0, W), i), half(VA, i), True)
+        for c in CUT:
+            tt(cut(EA(t), c), cut(Xy, c), cut(A, c), A_.mult)
+            tt(cut(EB(t), c), cut(Xy, c), cut(B, c), A_.mult)
+        if t > 0 or last:
+            tt(P, Xy, P, A_.add)
+        if t == 3 and ACC:
+            place(XU, IB, ("YW", L2 * t + K, L2 * t + L2), True, False)
+            tt(XU, EA(t), XU, A_.mult)
         else:
-            gtt(U("T5"), U("T4"), pi, Bs, A_.add)
-            tt(Xw, Xw, A, A_.add)
-            tt(U("DS"), X[4], U("T5"), A_.add)
-            tt(U("DA"), Xw, half(nva(3), 0), A_.add)
+            tt(XU, EA(t), XW, A_.mult)
+        if t == 3 and ACC:
+            for c in CUTU:
+                place(cut(XU, c), IDF, cut(B, c), False, False)
+                place(cut(XU, c), IB, cut(NV3 if r else half(N3, 1), c), False, True)
+        elif t == 3:
+            tt(XU, XU, B, A_.add)
+            tt(XU if EARLY else lane("D1B", 0, 2), XU, NV3 if r else half(N3, 1), A_.add)
+        elif r == 0:
+            tt(ob, XU, B, A_.add)
+        else:
+            tt(lane("SB", 0, 2), XU, B, A_.add)
+            agat(ob, ("SB", 0, L3), pl("PI", r, t))
+        tt(XW, EB(t), XW, A_.mult)
+        if t == 3 and ACC:
+            for c in CUTW:
+                place(cut(XW, c), IDF, cut(A, c), False, False)
+                place(cut(XW, c), IB, cut(half(N3, 0), c), False, True)
+        elif t == 3:
+            tt(XW, XW, A, A_.add)
+            tt(XW if EARLY else lane("D1B", 0, 0), XW, half(N3, 0), A_.add)
+        else:
+            tt(oa, XW, A, A_.add)
 
     def backward(r, t):
         last = r == RO - 1
-        Xa, Xb = (X[2], X[3]) if t % 2 else (X[0], X[1])
-        Xm = X[0] if t == 3 else X[4]
-        EA, EB, DA, DB, DS = U("EA", t), U("EB", t), U("DA"), U("DB"), U("DS")
-        T4, T5 = U("T4"), U("T5")
-        T1, T2 = (U("T1"), U("T2")) if t % 2 else (U("PR"), U("MM", 2))
-        full = last or t > 0
-        pp, pi = (pl("PP", r, t), pl("PI", r, t)) if r else (None, None)
-        wn = []
-        if t == 3:
-            if r == 0:
-                wn = wrap(B6, [(("GB", 0, L2), E1(4))])
-                tt(T2, EA, DB, A_.mult)
-                tt(T1, EB, DA, A_.mult)
-            else:
-                agat(DB, DS, pp)
-                act(X[4], EB, F_.Copy)
-                gtt(T2, DS, pp, EA, A_.mult)
-                tt(Xa, Xa, DA, A_.mult)
-                tt(T5, Xm, DA, A_.mult)
-                tt(T1, X[4], DA, A_.mult)
-        else:
-            zw = ("Z", 0, QB(t))
-            nl = ("NL", 96 * t, 96 * t + 96)
-            na, nb = half(nl, 0), half(nl, 1)
-            if r == 0:
-                if full:
-                    wn = wrap(X[2][1], [(("IO", 0, L2), E1(3))]) if t == 2 else wrap(0, [(("GB", 0, L2), E1(2))])
-                    agat(DA, zw, na)
-                    agat(DB, zw, nb)
-                gtt(T1, zw, na, EB, A_.mult)
-                gtt(T2, zw, nb, EA, A_.mult)
-            else:
-                agat(DS, zw, nb)
-                if full:
-                    agat(DA, zw, na)
-                    agat(DB, DS, pp)
-                gtt(T1, zw, na, EB, A_.mult)
-                gtt(T2, DS, pp, EA, A_.mult)
-        if t > 0:
-            send([(peer(-t), [T1, T2], U("C%d" % t), "c%d_%d" % (r, t), 0, NE)])
-            arrive("c%d_%d" % (r, t), NE, U("C%d" % t))
-            if t == 1:
-                dma("g", ap(U("C3")), ap(U("C2")), [U("C2"), U("C3")], [U("C3")], add=True)
-        elif last:
-            for s in (U("C1"), T1, T2):
-                dma("g", ap(U("C3")), ap(s), [s, U("C3")], [U("C3")], add=True)
-        if not full:
-            act(X[0], T1, F_.Copy)
-            tt(X[4], X[4], U("C1"), A_.subtract)
-            for (c0, c1) in CUT:
-                tt(("T4", c0, c1), ("PS", c0, c1), (T2[0], T2[1] + c0, T2[1] + c1), A_.add)
+        da, t2, db = [lane("D1B", 0, k) for k in range(3)]
+        d0 = zr(D0 + L3 * t, L3)
+        D1A, D1B, SB = ("D1A", 0, L3), ("D1B", 0, L3), ("SB", 0, L3)
+        zw = ("Z", FB(t), QV(2) if t == 2 else QV(1))
+        na, nb_ = half(nxt(t), 0), half(nxt(t), 1)
+        if not last and t == 0:
+            place(XU, IDF, EA(0))
+            place(EX[1], NIF, CC(3), True, False)
+            for c in CUT:
+                place(cut(EX[1], c), NIF, cut(CC(1), c), False, True)
+            agat(U("D1B"), zw, nb_)
+            gtt(EB(0), zw, na, EB(0), A_.mult)
+            tt(XU, XU, U("D1B"), A_.mult)
+            tt(U("D1B", 1), XU, EB(0), A_.add)
             return
-        if t < 3 or r == 0:
-            tt(Xa, Xa, DA, A_.mult)
-            tt(T5, Xm, DA, A_.mult)
-        tt(T4, Xm, DB, A_.mult)
-        tt(Xb, Xb, DB, A_.mult)
-        if r == 0 and t < 3:
-            index(("NL", 96 * t - 96, 96 * t), wn)
-        if t > 1 or (t == 1 and last):
-            squares(t - 1)
-        if (r > 0 or t < 3) and (t > 1 or (t == 1 and last)):
-            act(X[4], U("MM", t - 1), F_.Copy)
+        act(EX[0], AA(t), F_.Square)
+        act(EX[1], BB(r, t), F_.Square)
+        if r == 0 and t == 3:
+            back_pointers(2, U("AB", 6), U("AB", 7))
         if r == 0 and t == 2:
-            agat(("GB", 0, L2), LOCW, names(0))
-        if r == 1 and t == 2:
-            act(VA, VA, F_.Copy, -1.0)
-        tt(Xa, Xa, T4, A_.add)
-        tt(Xb, Xb, T5, A_.add)
-        qa, qb = ("Z", QB(t), QB(t) + K), ("Z", QB(t) + K, QB(t) + L2)
+            back_pointers(1, U("AB", 4), U("AB", 5))
+        if r == 0 and t == 1:
+            back_pointers(0, U("AB", 2), U("AB", 3))
+        if r == 1 and t == 3:
+            fin()
+            agat(PN, ("KI", 0, K), pl("PP", r, 0))
+            factors(0)
+        early = t < 2 or EARLY
+        if not early:
+            place(XW, IDF, EB(t))
+        if t < 3 or not early:
+            place(XU, IDF, EA(t))
+        if t == 3 and early:
+            for i in range(2):
+                act(half(db, i), half(XU, i), F_.Copy)
+            tt(EA(t), XU, EA(t), A_.mult)
+            for i in range(2):
+                act(half(da, i), half(XW, i), F_.Copy)
+            tt(EB(t), XW, EB(t), A_.mult)
+        elif t < 3:
+            for i in range(2):
+                agat(half(db, i), zw, half(nb_, i))
+            for i in range(2):
+                agat(half(da, i), zw, half(na, i))
+            if early:
+                gtt(EB(t), zw, na, EB(t), A_.mult)
+                tt(EA(t), XU, db, A_.mult)
+        act(lane("D1A", 0, 0), db, F_.Copy)
+        act(lane("D1A", 0, 2), da, F_.Copy)
+        n = 1 if t == 3 and not early else 2
+        for i in range(n):
+            tt(half(t2, i, n), half(EX[0], i, n), half(db, i, n), A_.mult)
+            scan(half(SB, i, n), half(d0, i, n), half(D1B, i, n), 0.0, A_.mult, A_.add)
+        tt(lane("D1A", 0, 1), EX[1], da, A_.mult)
         if r == 0:
-            tt(Xa, Xa, U("NW", t), A_.mult)
-            tt(Xb, Xb, U("NW", t), A_.mult)
-            if t == 3:
-                index(("NL", 192, 288), wn)
-                act(X[4], U("MM", t - 1), F_.Copy)
-            tt(qa, Xa, DA, A_.add)
-            tt(qb, Xb, DB, A_.add)
+            act(zr(QB(t)), lane("SB", 0, 2), F_.Copy)
         else:
-            tt(Xa, Xa, U("NW", t), A_.mult)
-            tt(T4, Xb, U("NW", t), A_.mult)
-            tt(qa, Xa, DA, A_.add)
-            gtt(qb, T4, pi, DS, A_.add)
-        if t == 1 and not last:
-            act(X[4], U("C3"), F_.Copy, -1.0)
+            agat(zr(QB(t)), SB, pl("PI", r, t))
+        scan(zr(QA(t), L3), d0, D1A, 0.0, A_.mult, A_.add)
+        if not early:
+            tt(EB(t), XW, lane("D1A", 0, 2), A_.mult)
+            tt(EA(t), XU, lane("D1A", 0, 0), A_.mult)
+        if t > 0:
+            send([(peer(-t), [EB(t), EA(t)], CC(t), "c%d_%d" % (r, t), 0, NE)])
+        if t == 2:
+            move("g", CC(3), CC(2), True)
+        if t == 0:
+            move("g", CC(3), EB(0), True)
+            for i, s in enumerate((EA(0), CC(3), CC(1))):
+                place(XW, IDF, s, i == 0, i == 2)
 
     def vote(r):
-        old = U("KI") if r == 0 else U("PN")
-        for (c0, c1) in CUT:
-            tt(("POS", c0, c1), ("T4", c0, c1), ("PS", B6 + c0, B6 + c1), A_.is_lt)
-            place(("PS", c0, c1), ("MV", 0, 128), ("POS", c0, c1))
-        for (c0, c1) in CUT:
-            ts(("PS", c0, c1), ("PS", c0, c1), 16.5, BIG, A_.is_lt, A_.mult)
-        for (c0, c1) in CUT:
-            tt(("T4", c0, c1), (old[0], c0, c1), ("PS", c0, c1), A_.subtract)
-        scan(U("T5"), X[0], U("T4"), 0.0, A_.min, A_.max)
-        scan(("BNF", 8, 8 + K), X[0], U("T4"), ("T5", K - 1, K), A_.min, A_.max)
-        vcopy(("BNF", 7, 8), ("T5", K - 1, K))
-        wp = wrap(B6, [(("BNF", 8, 8 + K), ("EH", 144, 288)), (("BNF", 7, 7 + K), ("EH", 0, 144))])
+        old = U("KI") if r == 0 else PN
+        p0, lo = U("D1B", 1), U("D1B", 2)
+        for x, b, cuts in ((EX[0], BN_, CUT), (XW, BC_, CUTW)):
+            for c in cuts:
+                place(cut(x, c), b, cut(ONE, (0, c[1] - c[0]), 512), True, False, 1)
+        for c in CUT:
+            tt(cut(POS, c), cut(p0, c), cut(EX[1], c), A_.is_lt)
+            place(cut(EX[0], c), MVN, cut(POS, c), False, True)
+        place(XW, MVC, POS, False, True)
+        for c in CUT:
+            tt(cut(lo, c), cut(EX[0], c), cut(old, c), A_.min)
+        place(("PS", B7, B7 + 48), IDF, ("WO", 0, 48), True, False)
+        scan(ST, XW, lo, NONE, A_.min, A_.max)
+        wp = wrap([(ST, ("EH", 288, 432), range(15)), (ST, ("EH", 144, 288), [15]),
+                   (("BNF", 7, 7 + K), ("EH", 0, 144), [0])], 128, False, B7)
+        vcopy(cs(57), ("BNF", 7 + K, 8 + K))
         pp = pl("PP", r + 1, 0)
-        tt(("WO", 0, 48), wp, ("WO", 0, 48), A_.add)
+        ts(("WT", 0, 48), wp, -BIG, cs(57), A_.mult, A_.min)
+        tt(("WO", 0, 48), wp, ("WT", 0, 48), A_.max)
         vcopy(pp, ("WO", 0, 48))
         send([(peer(u), [pp], pl("PP", r + 1, u), "pp%d_%d" % (r + 1, u), NS_ * (u - 1), NS_) for u in (1, 2, 3)])
 
@@ -636,14 +810,11 @@ def rank_program(g, core, T, topo):
         if r < RO - 1:
             vote(r)
 
-    zw = ("Z", 0, W + 7 * L2)
+    zw = ("Z", 0, Q0B + K)
+    act(CC(2), XW, F_.Copy, -0.125)
+    dma("s", T.yh[:], ap(CC(2)), [CC(2)], [], nb(CC(2)))
     for i in range(4):
-        o = U("LOC", i)
+        o = U("AB", i)
         (agat if i % 2 else vgat)(o, zw, ("FIN", 48 * i, 48 * i + 48))
-        dma("s", T.yd[:, K * i:K * i + K], ap(o), [o], [])
-        if i == 1:
-            act(U("C2"), U("C3"), F_.Copy, -0.125)
-            dma("s", T.yh[:], ap(U("C2")), [U("C2")], [])
-    for s, v in final.items():
-        if max([waited.get((q, s), 0) for q in Q]) < v:
-            g.wait_ge(T.sem[s], v)
+        dma("s", T.yd[:, K * i:K * i + K], ap(o), [o], [], nb(o))
+    issue()

@@ -11,22 +11,18 @@ NONE = -1024.0
 BS0 = W
 Q0B = W + K + 3 * L2 + 2 * W
 D0 = Q0B + K
-PE_E = True
-ACC = False
-EARLY = True
-GLANE = True
-START = False
-LOCA = 2
-IDV = ()
-VAORDER = (2, 1, 0)
-PASSES = 3
+PASSES = 2
+GDUP = ()
+GQB = True
+RELAY = False
+LAST = (768, 512, 256)
 LOG = []
 ORDER = []
-X0 = 128
-ONCE = {"remote": 2.0, "table": 1.3, "dma": 1.0}
 
-CYC, PCYC, GAT, SCA, FIX, SIG = 0.83e-3, 0.62e-3, 1.5, 3.0, 0.07, 0.1
-ISSUE, LAT, RATE = {"g": 1.0, "s": 0.1, "a": 0.1, "r": 0.6}, {"d": 2.5, "r": 3.0}, {"d": 500e3, "r": 8e3}
+CYC, PCYC, GAT, SCA, SIG = 0.83e-3, 0.6e-3, 1.3, 2.5, 0.15
+START = {"v": 0.05, "a": 0.15, "p": 0.05, "g": 0.05}
+ISSUE, LAT, RATE = {"g": 1.0, "s": 0.1, "a": 0.1, "r": 0.6}, {"d": 2.0, "r": 2.5}, {"d": 550e3, "r": 10e3}
+ONCE = {"remote": 2.0, "table": 1.3, "dma": 1.0}
 
 
 def FB(t):
@@ -76,10 +72,10 @@ SCRATCH = {
     "E2": ("sbuf", [128, 4 * 144], IDX),
     "EH": ("sbuf", [128, 3 * 144], IDX),
     "EG": ("sbuf", [128, 6 * 144], "bfloat16"),
-    "MB": ("sbuf", [128, 10 * 128], "bfloat16"),
+    "MB": ("sbuf", [128, 9 * 128], "bfloat16"),
     "MF": ("sbuf", [128, 2 * 128], "float32"),
     "WO": ("sbuf", [128, 48], "float32"),
-    "WT": ("sbuf", [128, 2 * 192], "float32"),
+    "WT": ("sbuf", [128, 3 * 192], "float32"),
     "RI": ("sbuf", [128, 4], "int32"),
     "CS": ("sbuf", [128, 72], "float32"),
 }
@@ -89,7 +85,9 @@ ARR = (["yw%d" % t for t in (1, 2, 3)] + ["l%d_%d" % (s, t) for s in (0, 1) for 
        + ["c%d_%d" % (r, t) for r in range(RO) for t in (1, 2, 3)]
        + ["pp%d_%d" % (r, t) for r in (1, 2) for t in (1, 2, 3)]
        + ["pi%d_%d" % (r, t) for r in (1, 2) for t in (1, 2, 3)])
-SEMAPHORES = ["qv", "qa", "qp", "qg"] + ARR + ["s%d" % i for i in range(NPOOL)]
+RELAYED = [("YW", 2 * L2, 2, 2 * L2, L2, "yw2")] + [("C", K * r, -3, 2 * K, K, "c%d_3" % r) for r in range(RO)]
+SEMAPHORES = (["qv", "qa", "qp", "qg"] + ARR + ["s%d" % i for i in range(NPOOL)]
+              + ["h%d" % i for i in range(len(RELAYED))])
 
 
 def step(r):
@@ -126,18 +124,31 @@ def issue_order(calls):
             seen.setdefault(r[0], []).append((r, i, False))
         p.discard(i)
         before.append(p)
+    data = [set(p) for p in before]
+    for q in "vag":
+        line = [i for i, c in enumerate(calls) if c["line"] and c["q"] == q]
+        for i, j in zip(line, line[1:]):
+            before[j].add(i)
     behind = [[] for _ in calls]
     for i in range(n):
         for j in before[i]:
             behind[j].append(i)
     span = [c["hold"] + c["lag"] + c["bytes"] for c in calls]
-    uses = [([(c["q"], 0.0, c["hold"])] if c["q"] != "x" else []) + ([(c["way"], c["hold"], c["bytes"])] if c["bytes"] else [])
-            + [(b, 0.0, c["hold"] + (SIG if c["q"] != "v" else 0.0)) for b in banks_of(c["reads"] + c["writes"])] for c in calls]
+    uses = [([(c["q"], 0.0, c["hold"])] if c["q"] != "x" else [])
+            + ([(c["way"], c["hold"], c["bytes"])] if c["bytes"] else [])
+            + [(b, 0.0, c["hold"] + (SIG if c["q"] != "v" else 0.0)) for b in banks_of(c["reads"] + c["writes"])]
+            for c in calls]
+
+    def gap(i, j, back):
+        a, b = (i, j) if back else (j, i)
+        if a not in data[b]:
+            return span[j] + (calls[a]["hold"] - span[a])
+        return span[j] + (0.0 if calls[i]["q"] + calls[j]["q"] == "pp" else SIG)
 
     def lay(order, first, back):
         busy, start = {}, [0.0] * n
         for i in order:
-            s = max([start[j] + span[j] + (0.0 if calls[i]["q"] == calls[j]["q"] == "p" else SIG) for j in first[i]] + [0.0])
+            s = max([start[j] + gap(i, j, back) for j in first[i]] + [0.0])
             use = [(k, span[i] - a - d if back else a, d) for k, a, d in uses[i]]
             moved = True
             while moved:
@@ -151,26 +162,59 @@ def issue_order(calls):
                 busy[k].sort()
             start[i] = s
         return start
-    order, kept = list(range(n)), None
-    if START:
-        late = lay(order[::-1], behind, True)
-        order = sorted(range(n), key=lambda i: (-late[i] - span[i], i))
+
+    def ranked(key):
+        done, out = set(), []
+
+        def put(i):
+            if i not in done:
+                done.add(i)
+                for j in sorted(before[i], key=key):
+                    put(j)
+                out.append(i)
+        for i in sorted(range(n), key=key):
+            put(i)
+        return out
+    tail = [0.0] * n
+    for i in reversed(range(n)):
+        tail[i] = max([tail[j] + gap(j, i, False) for j in behind[i]] + [span[i]])
+    order, kept = ranked(lambda i: (-tail[i], i)), None
     for _ in range(PASSES):
         start = lay(order, before, False)
         t = max(start[i] + span[i] for i in range(n))
         LOG.append(t)
         if not kept or t < kept[0]:
-            kept = (t, sorted(range(n), key=lambda i: (start[i], i)))
-        late = lay(sorted(range(n), key=lambda i: (-start[i] - span[i], -i)), behind, True)
-        order = sorted(range(n), key=lambda i: (-late[i] - span[i], i))
+            kept = (t, ranked(lambda i: (start[i], i)))
+        late = lay(ranked(lambda i: (start[i] + span[i], i))[::-1], behind, True)
+        order = ranked(lambda i: (-late[i] - span[i], i))
     return kept[1]
+
+
+def helper_of(c, T, topo):
+    return [h for h in topo.cores_of(c) if topo.die(h) != topo.die(c) and h not in T.cores
+            and all(topo.may_write(h, d) for d in T.cores)][0]
+
+
+def relay(g, core, T, topo, rank):
+    cores = list(T.cores)
+    total = 0
+    for i, (buf, c0, d, c1, n, sem) in enumerate(RELAYED):
+        to = cores[(rank + d) % len(cores)]
+        rid, pid, _ = topo.addr(to)
+        g.wait_ge(T.sem["h%d" % i], len(topo.engines(cores[rank], core)) - len(topo.engines(core, to)))
+        g.remote_dma(T[buf][:, c1:c1 + n], T[buf][:, c0:c0 + n], T.sem[sem], T.sem.s0, pid, rid, topo.mask(core, to))
+        total += len(topo.engines(core, to))
+    g.wait_ge(T.sem.s0, total)
 
 
 def rank_program(g, core, T, topo):
     rank = T.rank_of(core)
-    if rank is None:
-        return
     cores = list(T.cores)
+    if rank is None:
+        for r, c in enumerate(cores):
+            if RELAY and helper_of(c, T, topo) == core:
+                relay(g, core, T, topo, r)
+        return
     N = len(cores)
     A_ = AluOpType
     F_ = ActivationFunctionType
@@ -178,17 +222,24 @@ def rank_program(g, core, T, topo):
     calls = []
     pool = [0]
     once = dict(ONCE)
+    lined = {"v": 0, "a": 0, "g": 0}
 
     def newsem():
         pool[0] += 1
         return "s%d" % (pool[0] - 1)
 
-    def call(q, fn, tok, reads, writes, hold, lag=0.0, nbytes=0.0, way=None, after=()):
+    def call(q, fn, tok, reads, writes, hold, lag=0.0, nbytes=0.0, way=None, after=(), cycles=0):
         calls.append(dict(q=q, fn=fn, tok=tok, reads=list(reads), writes=list(writes), hold=hold, lag=lag, bytes=nbytes,
-                          way=way, after=after))
+                          way=way, after=after, line=lined.get(q) is not None and cycles >= lined[q]))
 
     def op(q, fn, reads, writes, cycles):
-        call(q, fn, None, reads, writes, FIX + cycles * (PCYC if q == "p" else CYC))
+        call(q, fn, None, reads, writes, START[q] + cycles * (PCYC if q == "p" else CYC), cycles=cycles)
+
+    def free(f, *args):
+        was = dict(lined)
+        lined.update(v=None, a=None, g=None)
+        f(*args)
+        lined.update(was)
 
     def dma(q, out, in_, reads, writes, nbytes, add=False):
         s = newsem()
@@ -196,9 +247,8 @@ def rank_program(g, core, T, topo):
         def fn():
             ins = Q[q].dma_start(out, in_, accum_op=A_.add) if add else Q[q].dma_start(out, in_)
             ins.then_inc(T.sem[s], 16)
-        call(q, fn, (s, 16, "d"), reads, writes, ISSUE[q], LAT["d"], nbytes * (2 if add else 1) / RATE["d"], "d")
-        if q == "g":
-            calls[-1]["hold"] += once.pop("dma", 0.0)
+        call(q, fn, (s, 16, "d"), reads, writes, ISSUE[q] + (once.pop("dma", 0.0) if q == "g" else 0.0), LAT["d"],
+             nbytes * (2 if add else 1) / RATE["d"], "d")
 
     def ap(r):
         return T[r[0]][:, r[1]:r[2]:r[3]] if len(r) > 3 else T[r[0]][:, r[1]:r[2]]
@@ -227,7 +277,7 @@ def rank_program(g, core, T, topo):
     NE = len(topo.engines(core, peer(1)))
     NS_ = NE // 4
 
-    def send(items, first=None):
+    def send(items):
         s = newsem()
         trs = []
         for (c, srcs, land, sem, i0, n) in items:
@@ -238,11 +288,33 @@ def rank_program(g, core, T, topo):
                 trs.append(RemoteDMATransfer(dst_ids=[dst(c)], dma_engine_mask=emask(c, i0, n), remote_sem=T.sem[sem],
                                              srcs=[ap(r) for r in srcs], dsts=[ap(land)], alu_op=1))
         call("g", lambda: g.remote_dma_fused(trs, local_sem=T.sem[s]), (s, sum(it[5] for it in items), "d"),
-             [r for it in items for r in it[1]] + cols(first), [], ISSUE["r"], LAT["r"] / 2, nb(items[0][2]) / items[0][5] / RATE["r"], "r")
-        calls[-1]["hold"] += once.pop("remote", 0.0)
+             [r for it in items for r in it[1]], [], ISSUE["r"] + once.pop("remote", 0.0), LAT["r"] / 2,
+             nb(items[0][2]) / items[0][5] / RATE["r"], "r")
         me = len(calls) - 1
         for it in items:
             call("x", None, (it[3], it[5], "d"), [], [it[2]], 0.0, LAT["r"] / 2, after=(me,))
+
+    def hand(i, srcs):
+        buf, c0, d, c1, n, sem = RELAYED[i]
+        h = helper_of(core, T, topo)
+        mask = topo.mask(core, h) & ~topo.mask(core, peer(1))
+        ne = len(topo.engines(core, h)) - NE
+        s = newsem()
+        land = (buf, c0, c0 + n)
+        if len(srcs) == 1:
+            tr = RemoteDMATransfer(dst_ids=[dst(h)], dma_engine_mask=mask, remote_sem=T.sem["h%d" % i], src=ap(srcs[0]),
+                                   dst=ap(land))
+        else:
+            tr = RemoteDMATransfer(dst_ids=[dst(h)], dma_engine_mask=mask, remote_sem=T.sem["h%d" % i],
+                                   srcs=[ap(r) for r in srcs], dsts=[ap(land)], alu_op=1)
+        call("g", lambda: g.remote_dma_fused([tr], local_sem=T.sem[s]), (s, ne, "d"), srcs, [], ISSUE["r"], LAT["r"] / 2,
+             nb(land) / ne / RATE["r"] / 2, "h")
+        call("x", None, (sem, NE, "d"), [], [(buf, c1, c1 + n)], 0.0, 2 * LAT["r"] + nb(land) / NE / RATE["r"],
+             after=(len(calls) - 1,))
+
+    def spread(n, r):
+        send([(peer(u), [pl(n.upper(), r, 0)], pl(n.upper(), r, u), "%s%d_%d" % (n, r, u), NS_ * (u - 1), NS_)
+              for u in (1, 2, 3)])
 
     def issue():
         count = {q: 0 for q in Q}
@@ -300,13 +372,17 @@ def rank_program(g, core, T, topo):
         op("v", lambda: g.vector.tensor_tensor(ap(out), ind(win, off), ap(b), o), [win, off, b], [out], size(out) * GAT)
 
     def ts(out, a, s1, s2, o0, *o1):
-        op("v", lambda: g.vector.tensor_scalar(ap(out), ap(a), val(s1), val(s2), o0, *o1), cols(a, s1, s2), [out], size(out))
+        op("v", lambda: g.vector.tensor_scalar(ap(out), ap(a), val(s1), val(s2), o0, *o1), cols(a, s1, s2), [out],
+           size(out))
 
     def vcopy(out, a):
         op("v", lambda: g.vector.tensor_copy(ap(out), ap(a)), [a], [out], size(out))
 
     def vgat(out, win, off):
         op("v", lambda: g.vector.tensor_copy(ap(out), ind(win, off)), [win, off], [out], size(out) * GAT)
+
+    def memset(out, v):
+        op("v", lambda: g.vector.memset(ap(out), v), [], [out], size(out))
 
     def agat(out, win, off, scale=1.0):
         op("a", lambda: g.scalar.activation(ap(out), ind(win, off), F_.Copy, scale=scale), [win, off], [out],
@@ -319,7 +395,6 @@ def rank_program(g, core, T, topo):
 
     def ascat(win, off, src):
         op("a", lambda: g.scalar.activation(ind(win, off), ap(src), F_.Silu), [off, src], [win], size(src) * SCA)
-        calls[-1]["hold"] += once.pop("table", 0.0)
 
     def scan(out, d0, d1, init, o0, o1):
         op("v", lambda: g.vector.tensor_tensor_scan(ap(out), ap(d0), ap(d1), init, o0, o1), [d0, d1], [out], size(out))
@@ -331,12 +406,11 @@ def rank_program(g, core, T, topo):
     def fill(out, v):
         iota(out, [[0, size(out)]], v, 0)
 
-    def select(reg, pat, o, v, base, cm):
-        op("g", lambda: g.affine_select(ap(reg), ap(reg), pat, o, v, base, cm), [reg], [reg], 150 + 2 * size(reg))
+    def select(out, src, pat, o, v, base, cm):
+        op("g", lambda: g.affine_select(ap(out), ap(src), pat, o, v, base, cm), [src], [out], 150 + 2 * size(out))
 
-    def matmuls(out, rd, todo, start, stop):
+    def matmuls(out, rd, todo, shut):
         grp = [("GRP", b, b + 1) for b in banks_of([out])]
-        shut = start and stop
 
         def fn():
             ins = None
@@ -344,30 +418,28 @@ def rank_program(g, core, T, topo):
                 ins = g.tensor.matmul(o, lhs, rhs, st, sp)
             return ins
         n = sum(max(64, o.shape[1]) for (o, lhs, rhs, st, sp) in todo)
-        op("p", fn, rd + (grp if shut else []), [out] + ([] if shut else grp), n * (4 if SCRATCH[rd[0][0]][2] == "float32" else 1))
+        op("p", fn, rd + (grp if shut else []), [out] + ([] if shut else grp),
+           n * (4 if SCRATCH[rd[0][0]][2] == "float32" else 1))
 
     def place(out, lhs, src, start=True, stop=True, parts=128):
         cuts = [out[1]] + [b for b in range(0, 4096, 512) if out[1] < b < out[2]] + [out[2]]
-        k = step(src)
-        todo = []
-        for c0, c1 in zip(cuts[:-1], cuts[1:]):
-            s0 = src[1] + k * (c0 - out[1])
-            todo.append((T.PS[:, c0:c1], T[lhs[0]][0:parts, lhs[1]:lhs[2]],
-                         T[src[0]][0:parts, s0:s0 + k * (c1 - c0 - 1) + 1:k], start, stop))
-        matmuls(out, [lhs, src], todo, start, stop)
+        todo = [(T.PS[:, c0:c1], T[lhs[0]][0:parts, lhs[1]:lhs[2]],
+                 T[src[0]][0:parts, src[1] + c0 - out[1]:src[1] + c1 - out[1]], start, stop)
+                for c0, c1 in zip(cuts[:-1], cuts[1:])]
+        matmuls(out, [lhs, src], todo, start and stop)
 
-    slot = [0]
+    slot = [48]
 
     def wrap(terms, parts=128, start=True, c0=None):
-        if c0 is None:
-            c0 = B7 + 96 * slot[0]
-            slot[0] = (slot[0] + 1) % 3
         n = size(terms[0][0]) // 16
+        if c0 is None:
+            c0 = B7 + (slot[0] if slot[0] + n <= 320 else 48)
+            slot[0] = c0 - B7 + n
         out = ("PS", c0, c0 + n)
         each = [(src, em, i) for src, em, which in terms for i in which]
         todo = [(ap(out), T[em[0]][0:parts, em[1] + 15 - i:em[1] + 143 - i], T[src[0]][0:parts, src[1] + i:src[2]:16],
                  start and j == 0, j == len(each) - 1) for j, (src, em, i) in enumerate(each)]
-        matmuls(out, [x for tm in terms for x in tm[:2]], todo, start, True)
+        matmuls(out, [x for tm in terms for x in tm[:2]], todo, start)
         return out
     ALL = range(16)
 
@@ -396,15 +468,12 @@ def rank_program(g, core, T, topo):
 
     def EG(r):
         return ("EG", 144 * (r - 2), 144 * (r - 2) + 144)
-    ID, IB, MVN, MVC, BN_, BC_ = [("MB", 128 * i, 128 * i + 128) for i in range(6)]
-    ONE = ("MB", 768, 1280)
+    IB, MVN, MVC, BN_, BC_ = [("MB", 128 * i, 128 * i + 128) for i in range(5)]
+    ONE = ("MB", 640, 1152)
     IDF, NIF = ("MF", 0, 128), ("MF", 128, 256)
-    EX = [("PS", X0, X0 + K), ("PS", 1024 + X0, 1024 + X0 + K)]
+    EX = [("PS", 128, 128 + K), ("PS", 1152, 1152 + K)]
     XW, XU = ("PS", 2048, 2048 + K), ("PS", 2048 + K, 2048 + L2)
     B7 = 3584
-    CUTU = ((0, 256), (256, K))
-    CUT = ((0, 512 - X0), (512 - X0, K))
-    CUTW = ((0, 512), (512, K))
 
     def names(t):
         return ("LS" if t == 0 else "LV", 96 * t, 96 * t + 96)
@@ -424,7 +493,9 @@ def rank_program(g, core, T, topo):
     POS, NV3 = half(TMP, 0), half(TMP, 1)
     PN = zr(Q0B)
     ST = ("BNF", 8, 8 + K)
-    V0, V1, V2 = ("D1B", 0, 128), ("D1B", 128, 272), ("D1B", 272, 416)
+    ZERO, V2 = ("WT", 192, 336), ("WT", 0, 144)
+    KK = ("KI", 0, K)
+    ROWS = [[16, 9], [1000, 16]]
 
     def AA(t):
         return U("AB", 2 * t)
@@ -441,183 +512,213 @@ def rank_program(g, core, T, topo):
     def CC(t):
         return U("C", t - 1)
 
+    def WW(t):
+        return ("YW", L2 * t + K, L2 * t + L2)
+
+    def ones(out, pat, v, base, cm):
+        select(out, cut(ZERO, (0, size(out)), 144), pat, A_.not_equal, v, base, cm)
+
     dma("s", T.BNI[0:32, :], T.bn[:], [], [U("BNI")], nb(U("BNI")) / 2)
     dma("a", T.ANI[:], T.an[:], [], [("ANI", 0, 192)], nb(("ANI", 0, 192)))
-    for q, out, src in (("s", TH, T.th), ("s", ("YW", 0, K), T.yt), ("s", ("YW", K, L2), T.wt), ("g", zr(0, W), T.th),
-                        ("s", VA, T.va)):
-        dma(q, ap(out), src[:], [], [out], nb(out))
+    for out, src in ((TH, T.th), (WW(0), T.wt), (("YW", 0, K), T.yt), (VA, T.va)):
+        dma("s", ap(out), src[:], [], [out], nb(out))
     iota(("RI", 0, 4), [[0, 4]], 0, 1, False)
     iota(cs(0, 4), [[1, 4]], 0, 0)
-    iota(V2, [[16, 9], [1000, 16]], 0, -4)
-    iota(V1, [[16, 9], [1000, 16]], 0, -1)
-    iota(V0, [[1, 128]], 0, -1)
-    op("v", lambda: g.vector.memset(T.GT[:], 1.0), [], [U("GT")], K / 2)
-    op("v", lambda: g.vector.memset(T.CS[:, 60:64], -float(LIFT)), [], [cs(60, 4)], 4)
-    scan(("KI", 0, K), U("GT"), U("GT"), -1.0, A_.mult, A_.add)
-    ts(("KI", K, K + LIFT), ("KI", 0, LIFT), float(K), None, A_.add)
+    iota(V2, ROWS, 0, -4)
+    iota(("KI", 0, K + LIFT), [[1, K + LIFT]], 0, 0)
+    memset(cs(59), float(LIFT))
+    memset(cs(60), -float(LIFT))
+    memset(ZERO, 0.0)
+    act(cs(64, 4), cs(0, 4), F_.Silu, float(K), cs(59))
+    calls[-1]["hold"] += once.pop("table")
     ts(("RI", 0, 1), ("RI", 0, 1), 7, None, A_.bitwise_and)
     ts(("RI", 1, 2), ("RI", 1, 2), 15, None, A_.bitwise_and)
+    ts(cs(12, 4), cs(0, 4), float(L2), float(FB(0) + LIFT), A_.mult, A_.add)
     vcopy(cs(4, 2), ("RI", 0, 2))
-    ts(cs(64, 4), cs(0, 4), float(K), float(LIFT), A_.mult, A_.add)
-    for u in range(LOCA):
-        act(half(LOC, u, 4), ("KI", 0, K), F_.Silu, 1.0, cs(64 + u))
-        calls[-1]["hold"] += once.pop("table", 0.0)
-    for u in range(LOCA, 4):
-        scan(half(LOC, u, 4), U("GT"), U("GT"), float(K * u + LIFT - 1), A_.mult, A_.add)
-    ts(cs(8, 4), cs(0, 4), cs(4), None, A_.subtract)
+    ts(cs(16, 4), cs(0, 4), -float(W), float(QV(0) + LIFT + 2), A_.mult, A_.add)
+
+    def e2(t):
+        ts(("E2", 144 * t, 144 * t + 144), V2, float(15000 - 4 * t), None, A_.is_equal)
     ts(cs(6), cs(4), 0.5, None, A_.is_gt)
+    ts(cs(8, 4), cs(0, 4), cs(4), None, A_.subtract)
+    e2(0)
     ts(cs(7), cs(4), 4.5, cs(6), A_.is_lt, A_.mult)
     ts(cs(20, 4), cs(8, 4), -4.5, None, A_.is_lt)
+    e2(1)
     ts(cs(24, 4), cs(8, 4), -2.0, cs(7), A_.is_equal, A_.mult)
-    tt(cs(20, 4), cs(20, 4), cs(24, 4), A_.add)
     ts(cs(28, 4), cs(8, 4), -1.5, cs(7), A_.is_gt, A_.mult)
-    ts(cs(12, 4), cs(0, 4), float(L2), float(FB(0) + LIFT), A_.mult, A_.add)
-    ts(cs(16, 4), cs(0, 4), -float(W), float(QV(0) + LIFT + 2), A_.mult, A_.add)
-    tt(cs(12, 4), cs(12, 4), cs(20, 4), A_.mult)
+    e2(2)
+    tt(cs(20, 4), cs(20, 4), cs(24, 4), A_.add)
     tt(cs(16, 4), cs(16, 4), cs(28, 4), A_.mult)
-    tt(cs(40, 4), cs(12, 4), cs(16, 4), A_.add)
-    tt(cs(36, 4), cs(20, 4), cs(28, 4), A_.add)
     ts(cs(68, 4), cs(28, 4), 2.0, None, A_.mult)
+    ts(cs(52, 4), cs(28, 4), float(L2 - 2), None, A_.mult)
+    e2(3)
+    tt(cs(12, 4), cs(12, 4), cs(20, 4), A_.mult)
+    tt(cs(36, 4), cs(20, 4), cs(28, 4), A_.add)
+    for t in (1, 2, 3, 0):
+        vcopy(("LS", 96 * t, 96 * t + 48), ("ANI", 48 * t, 48 * t + 48))
+    tt(cs(40, 4), cs(12, 4), cs(16, 4), A_.add)
     tt(cs(32, 4), cs(36, 4), cs(68, 4), A_.add)
     ts(cs(48, 4), cs(36, 4), float(K), None, A_.mult)
-    ts(cs(52, 4), cs(28, 4), float(L2 - 2), None, A_.mult)
-    tt(cs(48, 4), cs(48, 4), cs(40, 4), A_.add)
-    tt(cs(44, 4), cs(48, 4), cs(52, 4), A_.add)
-    op("v", lambda: g.vector.tensor_scalar(T.BNF[0:32, 0:K], T.BNI[0:32, :], -float(OFF), None, A_.add),
-       [U("BNI")], [U("BNF")], K)
-    for t in range(4):
-        e2 = ("E2", 144 * t, 144 * t + 144)
-        ts(e2, V2, float(15000 - 4 * t), None, A_.is_equal)
-        vcopy(("LS", 96 * t, 96 * t + 48), ("ANI", 48 * t, 48 * t + 48))
-        ts(("LS", 96 * t + 48, 96 * t + 96), wrap([(U("BNF"), e2, ALL)], 32, True, 512 * t), float(OFF), None, A_.add)
-    for s in range(2):
+    tt(cs(52, 4), cs(52, 4), cs(40, 4), A_.add)
+
+    def share(s):
         send([(peer(t), [half(("LS", 96 * t, 96 * t + 96), s)], half(names(t), s), "l%d_%d" % (s, t), NS_ * (t - 1), NS_)
               for t in (1, 2, 3)])
-    act(("YW", K, L2), ("YW", K, L2), F_.Copy, -0.125)
-    for t in (1, 2, 3):
-        send([(peer(t), [("YW", 0, L2)], ("YW", L2 * t, L2 * t + L2), "yw%d" % t, 0, NE)], first=("LS", 96, 384))
+    share(0)
+    for u in (0, 1):
+        act(half(LOC, u, 4), KK, F_.Identity, 1.0, cs(64 + u))
+    ts(half(LOC, 2, 4), KK, float(2 * K + LIFT), None, A_.add)
+    op("v", lambda: g.vector.tensor_scalar(T.BNF[0:32, 0:K], T.BNI[0:32, :], -float(OFF), None, A_.add),
+       [U("BNI")], [U("BNF")], K)
+    tt(cs(44, 4), cs(48, 4), cs(52, 4), A_.add)
+    ts(half(LOC, 3, 4), KK, float(3 * K + LIFT), None, A_.add)
+    wb = [wrap([(U("BNF"), ("E2", 144 * t, 144 * t + 144), ALL)], 32, True, 512 * t) for t in range(4)]
 
-    def picks(reg, rows):
-        for r in rows:
-            select(reg, [[16, 9], [1000, 16]], A_.not_equal, 1.0, r - 15000, -1)
-    ts(ID, V0, 0.0, -1.0 if PE_E else 1.0, A_.is_equal, A_.mult)
-    ts(IB, V0, 0.0, None, A_.is_equal)
-    ts(IDF, V0, 0.0, None, A_.is_equal)
-    ts(E1(ROW_F[3]), V1, float(15000 - ROW_F[3]), None, A_.is_equal)
-    ts(("EH", 0, 144), V1, 15000.0, None, A_.is_equal)
-    ts(("EH", 144, 288), V1, 15000.0, -1.0, A_.is_equal, A_.mult)
-    ts(("WO", 0, 48), ("KI", 0, 48), 16.0, cs(5), A_.mult, A_.add)
-    ts(cs(56), cs(5), 7.5, -1.0, A_.is_gt, A_.mult)
-    ts(("BNF", 7, 8), cs(60), 0.0, NONE, A_.mult, A_.add)
-    vcopy(("EH", 288, 289), ("EH", 0, 1))
-    tt(("EH", 289, 432), ("EH", 145, 288), ("EH", 0, 143), A_.add)
-    fill(NIF, 0)
-    select(NIF, [[1, 128]], A_.not_equal, -1.0, 0, -1)
+    def names_b(t):
+        ts(("LS", 96 * t + 48, 96 * t + 96), wb[t], float(OFF), None, A_.add)
+    names_b(0)
+    vgat(zr(BS0), TH, half(names(0), 1))
+    names_b(1)
+    ts(WW(0), WW(0), -0.125, None, A_.mult)
+    names_b(2)
+    names_b(3)
+    ones(IB, [[1, 128]], 1.0, 0, -1)
+    share(1)
+    send([(peer(1), [("YW", 0, L2)], ("YW", L2, 2 * L2), "yw1", 0, NE)])
+    ones(E1(ROW_F[3]), ROWS, 1.0, ROW_F[3] - 15000, -1)
+    dma("g", ap(zr(0, W)), T.th[:], [], [zr(0, W)], nb(zr(0, W)))
+    if RELAY:
+        hand(0, [("YW", 0, L2)])
+    else:
+        send([(peer(2), [("YW", 0, L2)], ("YW", 2 * L2, 3 * L2), "yw2", 0, NE)])
+    send([(peer(3), [("YW", 0, L2)], ("YW", 3 * L2, 4 * L2), "yw3", 0, NE)])
+    lined.update(v=256, g=None)
 
     def factors(t):
         fill(lane("Z", D0 + L3 * t, 0), 0)
-        w2, wt = lane("Z", D0 + L3 * t, 2), ("YW", L2 * t + K, L2 * t + L2)
-        if GLANE:
-            op("g", lambda: g.affine_select(ap(w2), ap(wt), [[0, K]], A_.is_ge, 0.0, 0, 0), [wt], [w2], 150 + 2 * K)
-        else:
-            act(w2, wt, F_.Copy)
+        select(lane("Z", D0 + L3 * t, 2), WW(t), [[0, K]], A_.is_ge, 0.0, 0, 0)
+    for m, v in ((IDF, 1.0), (NIF, -1.0)):
+        ones(m, [[1, 128]], v, 0, -1)
+    for r in (ROW_FIN,) + ROW_N:
+        ones(E1(r), ROWS, 1.0, r - 15000, -1)
+    ones(("EH", 0, 144), ROWS, 1.0, -15000, -1)
+    for c in (144, 288):
+        ones(("EH", c, c + 144), ROWS, -1.0, -15000, -1)
+    select(("EH", 289, 417), ("EH", 289, 417), [[16, 8], [1000, 16]], A_.not_equal, 1.0, -15000, -1)
+    ts(("WO", 0, 48), ("KI", 0, 48), 16.0, cs(5), A_.mult, A_.add)
+    ts(cs(56), cs(5), 7.5, -1.0, A_.is_gt, A_.mult)
+    ts(("BNF", 7, 8), cs(60), 0.0, NONE, A_.mult, A_.add)
     for t in (3, 2, 1):
         factors(t)
-    for r in ROW_N + (ROW_FIN,):
-        fill(E1(r), 0)
-        picks(E1(r), [r])
     for r in range(2, 8):
-        fill(EG(r), 0)
-        picks(EG(r), [r, r + 8])
+        ones(EG(r), ROWS, 1.0, r - 15000, -1)
+        select(EG(r), EG(r), ROWS, A_.not_equal, 1.0, r + 8 - 15000, -1)
     for m, b, v in ((MVN, BN_, int(BIG)), (MVC, BC_, -int(BIG))):
         fill(m, v)
         fill(b, -33 * v // 2)
-        select(m, [[-16, 8], [0, 16]], A_.is_ge, 0.0, 0, 1)
-        select(m, [[16, 8], [0, 16]], A_.is_ge, 0.0, 31, -1)
-        select((m[0], m[1] + 112, m[2]), [[0, 16]], A_.is_ge, float(v), -16, 1)
+        select(m, m, [[-16, 8], [0, 16]], A_.is_ge, 0.0, 0, 1)
+        select(m, m, [[16, 8], [0, 16]], A_.is_ge, 0.0, 31, -1)
+        last16 = (m[0], m[1] + 112, m[2])
+        select(last16, last16, [[0, 16]], A_.is_ge, float(v), -16, 1)
     fill(ONE, 1)
 
-    def ids(t, s, out):
-        if (t, s) in IDV:
-            ts(out, ("KI", 0, K), cs(32 + 4 * s + t), cs(40 + 4 * s + t), A_.mult, A_.add)
+    small = []
+
+    def soon(skip, f, *args):
+        small.append([skip, f, args])
+
+    def flush(need=None):
+        if need is None and small and small[0][0] <= 0:
+            need = small[0][2][0]
+            turn = 1
         else:
-            act(out, ("KI", 0, K), F_.Identity, cs(32 + 4 * s + t), cs(40 + 4 * s + t))
+            turn = max([i + 1 for i, x in enumerate(small) if need and x[2][0][0] == need[0] and meet(x[2][0], need)] + [0])
+        lined["v"] = 0
+        for skip, f, args in small[:turn]:
+            f(*args)
+        lined["v"] = 256
+        del small[:turn]
+        for x in small:
+            x[0] -= 1
 
-    def index(out, src, base):
-        ts(out, src, 0.25 - LIFT - base, None, A_.add)
+    def index(out, src, base, skip=0):
+        soon(skip, ts, out, src, 0.25 - LIFT - base, None, A_.add)
 
-    def index_n(t, out, src):
+    def index_n(t, out, src, skip=0):
         if t == 0:
             x = ("WT", 0, size(src))
-            ts(x, src, QV(1) + LIFT - 0.5, float(QA(1) - QV(1)), A_.is_gt, A_.mult)
-            tt(x, src, x, A_.add)
+            soon(skip, ts, x, src, QV(1) + LIFT - 0.5, float(QA(1) - QV(1)), A_.is_gt, A_.mult)
+            soon(skip, tt, x, src, x, A_.add)
             src = x
-        index(out, src, FB(t))
+        index(out, src, FB(t), skip)
 
-    def minus_va(r, t):
-        z = zr(FB(t), L2)
-        dma("g", ap(z), T.NVD[t], [("NVD", t, t + 1), z], [z], nb(z), True)
+    def ids(t, s):
+        act(half(IO, s) if t < 3 else (EX[0], XU)[s], KK, F_.Identity, cs(32 + 4 * s + t), cs(40 + 4 * s + t))
 
-    def keep_va(t):
+    def marks(t, s):
+        o, a, b = half(names(t), s), half(GB, s), half(IO, s)
+        if t in (0, 3):
+            ascat(LOC, o, a if t else b)
+        else:
+            op("v", lambda: g.vector.tensor_tensor(ind(LOC, o), ap(a), ap(b), A_.max), [o, a, b], [LOC], K * SCA)
+
+    def lookup(t):
+        for s in (1, 0):
+            agat(half(GB, s), LOC, half(names(t), s))
+        index(fwd(t), wrap([(GB, E1(ROW_F[3]), ALL)]), 0, 4)
+    KEPT = {3: U("AB", 1), 2: U("AB", 6), 1: U("AB", 7), 0: U("AB", 5)}
+
+    def lookback(t):
+        x = zr(QV(2) + L2 * (2 - t), L2) if t else ("AB", 4 * K, 6 * K)
         for s in range(2):
-            agat(half(TMP, s), VA, half(names(t), s), -1.0)
-        dma("s", T.NVD[t], ap(TMP), [TMP], [("NVD", t, t + 1)], nb(TMP))
+            agat(half(x, s), LOC, half(names(t), s))
+        index_n(t, nxt(t), wrap([(x, E1(ROW_N[t]), ALL)]), (3, 2, 1)[t])
 
-    def split(t, x):
-        act(U("GT"), x, F_.Copy, cs(56))
-        move("g", x, U("GT"), True)
-        move("g", U("G", t), x)
+    def keep(t):
+        move("s", KEPT[t], zr(QV(2) + L2 * (2 - t) + K))
+
+    def gcopy(out, src):
+        select(out, src, [[0, size(out)]], A_.is_ge, 0.0, 0, 0)
+
+    def split(t, src=None):
+        act(U("G", t), src or KEPT[t], F_.Copy, cs(56))
+        move("g", KEPT[t], U("G", t), True)
+        move("g", U("G", t), KEPT[t])
 
     def compose(r, t):
         agat(U("GT"), U("G", t), pl("PP", r, t))
         if t > 0:
-            index(half(fwd(t), 1), wrap([(U("GT"), EG(ROW_F[t]), ALL)]), 0)
+            index(half(fwd(t), 1), wrap([(U("GT"), EG(ROW_F[t]), ALL)]), 0, 1)
         if t < 3:
-            index_n(t, half(nxt(t), 1), wrap([(U("GT"), EG(ROW_N[t]), ALL)]))
-
-    def pointers(t):
-        for s in range(2):
-            o, a = half(names(t), s), half(GB, s)
-            b = half(IO, s) if t < 3 else (EX[0], XU)[s]
-            ids(t, s, b)
-            if t == 0:
-                ascat(LOC, o, b)
-            elif t < 3:
-                op("v", lambda o=o, a=a, b=b: g.vector.tensor_tensor(ind(LOC, o), ap(a), ap(b), A_.max), [o, a, b], [LOC],
-                   K * SCA)
-            else:
-                tt(a, b, a, A_.max)
-                ascat(LOC, o, a)
-        if t < 3:
-            for s in (1, 0):
-                agat(half(GB, s), LOC, half(names(t + 1), s))
-            index(fwd(t + 1), wrap([(GB, E1(ROW_F[3]), ALL)]), 0)
-        if t == 2:
-            move("s", U("AB", 1), half(GB, 1))
-            split(3, U("AB", 1))
-
-    def back_pointers(t, a, b):
-        for s, x in enumerate((a, b)):
-            agat(x, LOC, half(names(t), s))
-        if a[2] == b[1]:
-            index_n(t, nxt(t), wrap([((a[0], a[1], b[2]), E1(ROW_N[t]), ALL)]))
-        else:
-            for s, x in enumerate((a, b)):
-                index_n(t, half(nxt(t), s), wrap([(x, E1(ROW_N[t]), ALL)]))
-        split(t, b)
+            index_n(t, half(nxt(t), 1), wrap([(U("GT"), EG(ROW_N[t]), ALL)]), 2)
 
     def fin():
         for i in range(2):
             wrap([(half(LOC, i), E1(ROW_FIN), ALL)], c0=B7 + 320 + 96 * i)
         w = ("PS", B7 + 320, B7 + 512)
         x, y = ("WT", 0, 192), ("WT", 192, 384)
-        ts(x, w, QV(1) + LIFT - 0.5, float(QA(1) - QV(1)), A_.is_gt, A_.mult)
-        ts(y, w, QV(0) + LIFT - 0.5, float(QA(0) - QV(0) - QA(1) + QV(1)), A_.is_gt, A_.mult)
-        tt(x, w, x, A_.add)
-        tt(x, x, y, A_.add)
-        ts(y, w, QV(0) + L3 + LIFT - 0.5, float(QB(0) - L3 - QA(0)), A_.is_gt, A_.mult)
-        tt(x, x, y, A_.add)
-        index(("FIN", 0, 192), x, 0)
+        z = ("WT", 384, 576)
+        soon(3, ts, x, w, QV(1) + LIFT - 0.5, float(QA(1) - QV(1)), A_.is_gt, A_.mult)
+        soon(3, ts, y, w, QV(0) + LIFT - 0.5, float(QA(0) - QV(0) - QA(1) + QV(1)), A_.is_gt, A_.mult)
+        soon(3, ts, z, w, QV(0) + L3 + LIFT - 0.5, float(QB(0) - L3 - QA(0)), A_.is_gt, A_.mult)
+        soon(3, tt, x, w, x, A_.add)
+        for i, s in enumerate((x, y, z)):
+            soon(3, place, w, IDF, s, i == 0, i == 2)
+        index(("FIN", 0, 192), w, 0, 3)
+
+    def take_va(t):
+        for s in range(2):
+            agat(half(TMP if t < 3 else N3, s), VA, half(names(t), s), -1.0)
+        if t < 3:
+            dma("s", T.NVD[t], ap(TMP), [TMP], [("NVD", t, t + 1)], nb(TMP))
+
+    def minus_va(t):
+        z = zr(FB(t), L2)
+        dma("g", ap(z), T.NVD[t], [("NVD", t, t + 1), z], [z], nb(z), True)
+
+    def negate(u):
+        act(half(VA, u, 4), half(VA, u, 4), F_.Copy, -1.0)
 
     def forward(r, t):
         last = r == RO - 1
@@ -627,180 +728,231 @@ def rank_program(g, core, T, topo):
         A, B = AA(t), BB(r, t)
         oa, ob = zr(FB(t)), zr(FB(t) + K)
         P = lane("Z", D0 + L3 * t, 1) if t > 0 or last else U("D1B", 1)
-        place(Xy, ID, ("YW", L2 * t, L2 * t + K), True, not PE_E)
-        place(XW, IB, ("YW", L2 * t + K, L2 * t + L2), True, not (ACC and t == 3))
+        place(Xy, IB, ("YW", L2 * t, L2 * t + K))
+        place(XW, IB, WW(t))
         if r == 0 and t == 0:
+            ids(0, 0)
+            marks(0, 0)
             agat(A, zw, fa)
-            vgat(B, zw, fb)
+            ids(0, 1)
+            marks(0, 1)
         elif t == 0:
             pp = pl("PP", r, 0)
             agat(B, zr(BS0), pp)
         else:
-            for c in CUT:
-                agat(cut(B, c), zw, cut(fb, c))
-            for c in CUT:
-                agat(cut(A, c), zw, cut(fa, c))
-        for c in CUT:
+            if r == 0 and t < 3:
+                marks(t, 0)
+            if r == 0 and t == 1:
+                marks(t, 1)
+            if r == 0 and t == 3:
+                tt(half(GB, 0), EX[0], half(GB, 0), A_.max)
+            flush(fwd(t))
+            for x, f in ((B, fb), (A, fa)):
+                for i in range(2):
+                    agat(half(x, i), zw, half(f, i))
+            if (t > 1 or last) and not (r == 0 and t == 3):
+                m = lane("Z", D0 + L3 * (t - 1), 1)
+                tt(m, EX[1 - t % 2], m, A_.add)
+        for i in range(2):
             if r > 0 and t == 0:
-                gtt(cut(P, c), zr(BS0), cut(pp, c), cut(A, c), A_.mult)
+                gtt(half(P, i), zr(BS0), half(pp, i), half(A, i), A_.mult)
             else:
-                gtt(cut(P, c), zw, cut(fa, c), cut(B, c), A_.mult)
-            if PE_E:
-                place(cut(Xy, c), IDF, cut(P, c), False, True)
+                gtt(half(P, i), zw, half(fa, i), half(B, i), A_.mult)
+        if r == 0 and t == 2:
+            take_va(1)
+            marks(t, 1)
+        if r == 0 and t == 3:
+            tt(half(GB, 1), XU, half(GB, 1), A_.max)
+            marks(t, 0)
+            marks(t, 1)
+        for i in range(2):
+            tt(half(Xy, i), half(P, i), half(Xy, i), A_.subtract)
+        if r == 0 and t < 3:
+            lookup(t + 1)
+            if t < 2:
+                ids(t + 1, 0)
+                ids(t + 1, 1)
             else:
-                tt(cut(Xy, c), cut(P, c), cut(Xy, c), A_.subtract)
-        if r == 0:
-            pointers(t)
-            if t == 1:
-                for s in range(2):
-                    agat(half(N3, s), VA, half(names(3), s), -1.0)
-                for u in VAORDER:
-                    keep_va(u)
-        elif t == 0:
+                move("s", KEPT[3], half(GB, 1))
+                split(3, half(GB, 1))
+            take_va((3, 2, 0)[t])
+        if r > 0 and t == 0:
             ascat(U("D1B"), pp, ("KI", LIFT, LIFT + K))
             act(ST, U("D1B"), F_.Identity, 1.0, cs(60))
-            ts(pl("PI", r, 0), wrap([(ST, ("EH", 0, 144), ALL)]), 3.0, 2.25, A_.mult, A_.add)
-            send([(peer(u), [pl("PI", r, 0)], pl("PI", r, u), "pi%d_%d" % (r, u), NS_ * (u - 1), NS_) for u in (1, 2, 3)])
-            for u in (1, 2, 3, 0):
-                compose(r, u)
-            agat(NV3, half(N3, 1), pl("PP", r, 3))
-            if r == 1:
-                for u in range(4):
-                    act(half(VA, u, 4), half(VA, u, 4), F_.Copy, -1.0)
+            soon(0, ts, pl("PI", r, 0), wrap([(ST, ("EH", 0, 144), ALL)]), 3.0, 2.25, A_.mult, A_.add)
+        if r > 0 and t < 3:
+            compose(r, t + 1)
+            if t == 1:
+                agat(NV3, half(N3, 1), pl("PP", r, 3))
+            if t == 2:
+                compose(r, 0)
+            if t > 0 and r == 1:
+                negate(t)
         if t == 3:
             for u in (2, 1, 0):
-                minus_va(r, u)
+                minus_va(u)
             if last:
                 for i in range(2):
                     move("g", half(zr(0, W), i), half(VA, i), True)
-        for c in CUT:
-            tt(cut(EA(t), c), cut(Xy, c), cut(A, c), A_.mult)
-            tt(cut(EB(t), c), cut(Xy, c), cut(B, c), A_.mult)
-        if t > 0 or last:
+            act(EX[0], A, F_.Square)
+        for i in range(2):
+            tt(half(EA(t), i), half(Xy, i), half(A, i), A_.mult)
+        tt(half(EB(t), 0), half(Xy, 0), half(B, 0), A_.mult)
+        tt(XU, EA(t), XW, A_.mult)
+        tt(half(EB(t), 1), half(Xy, 1), half(B, 1), A_.mult)
+        if r == 0 and t == 2:
             tt(P, Xy, P, A_.add)
-        if t == 3 and ACC:
-            place(XU, IB, ("YW", L2 * t + K, L2 * t + L2), True, False)
-            tt(XU, EA(t), XU, A_.mult)
-        else:
-            tt(XU, EA(t), XW, A_.mult)
-        if t == 3 and ACC:
-            for c in CUTU:
-                place(cut(XU, c), IDF, cut(B, c), False, False)
-                place(cut(XU, c), IB, cut(NV3 if r else half(N3, 1), c), False, True)
-        elif t == 3:
-            tt(XU, XU, B, A_.add)
-            tt(XU if EARLY else lane("D1B", 0, 2), XU, NV3 if r else half(N3, 1), A_.add)
-        elif r == 0:
-            tt(ob, XU, B, A_.add)
-        else:
-            tt(lane("SB", 0, 2), XU, B, A_.add)
-            agat(ob, ("SB", 0, L3), pl("PI", r, t))
-        tt(XW, EB(t), XW, A_.mult)
-        if t == 3 and ACC:
-            for c in CUTW:
-                place(cut(XW, c), IDF, cut(A, c), False, False)
-                place(cut(XW, c), IB, cut(half(N3, 0), c), False, True)
-        elif t == 3:
-            tt(XW, XW, A, A_.add)
-            tt(XW if EARLY else lane("D1B", 0, 0), XW, half(N3, 0), A_.add)
-        else:
+            ids(3, 0)
+        if t < 3:
+            if t > 0:
+                flush()
+            tt(lane("SB", 0, 2) if r else ob, XU, B, A_.add)
+            flush()
+            if r and t == 0:
+                spread("pi", r)
+            if r:
+                agat(ob, ("SB", 0, L3), pl("PI", r, t))
+            elif t == 2:
+                ids(3, 1)
+            tt(XW, EB(t), XW, A_.mult)
+            flush()
             tt(oa, XW, A, A_.add)
+            return
+        da, db = lane("D1B", 0, 0), lane("D1B", 0, 2)
+        if r == 0:
+            lookback(2)
+        if r:
+            flush()
+        tt(XU, XU, B, A_.add)
+        tt(XW, EB(t), XW, A_.mult)
+        if r:
+            flush()
+        tt(XU, XU, NV3 if r else half(N3, 1), A_.add)
+        tt(XW, XW, A, A_.add)
+        if r:
+            flush()
+        tt(P, Xy, P, A_.add)
+        tt(XW, XW, half(N3, 0), A_.add)
+        for x, y in ((db, XU), (da, XW)):
+            for i in range(2):
+                act(half(x, i), half(y, i), F_.Copy)
+        act(EX[1], B, F_.Square)
+        tt(EA(t), XU, EA(t), A_.mult)
 
     def backward(r, t):
         last = r == RO - 1
+        more = t > 1 or (t == 1 and last)
         da, t2, db = [lane("D1B", 0, k) for k in range(3)]
         d0 = zr(D0 + L3 * t, L3)
         D1A, D1B, SB = ("D1A", 0, L3), ("D1B", 0, L3), ("SB", 0, L3)
         zw = ("Z", FB(t), QV(2) if t == 2 else QV(1))
         na, nb_ = half(nxt(t), 0), half(nxt(t), 1)
+        Xe = ("PS", 3072, 3072 + K) if last and t == 0 else XU
+        if t < 3:
+            place(Xe, IDF, EA(t))
+            flush(nxt(t))
+        if t == 0:
+            flush(("FIN", 0, 192))
         if not last and t == 0:
-            place(XU, IDF, EA(0))
-            place(EX[1], NIF, CC(3), True, False)
-            for c in CUT:
-                place(cut(EX[1], c), NIF, cut(CC(1), c), False, True)
-            agat(U("D1B"), zw, nb_)
+            for i in range(2):
+                agat(half(U("D1B"), i), zw, half(nb_, i))
+            if r == 0:
+                split(0)
+            else:
+                agat(PN, KK, pl("PP", r, 0))
             gtt(EB(0), zw, na, EB(0), A_.mult)
-            tt(XU, XU, U("D1B"), A_.mult)
-            tt(U("D1B", 1), XU, EB(0), A_.add)
+            for i in range(2):
+                tt(half(XU, i), half(XU, i), half(U("D1B"), i), A_.mult)
+            for i in range(2):
+                tt(half(U("D1B", 1), i), half(XU, i), half(EB(0), i), A_.add)
             return
-        act(EX[0], AA(t), F_.Square)
-        act(EX[1], BB(r, t), F_.Square)
-        if r == 0 and t == 3:
-            back_pointers(2, U("AB", 6), U("AB", 7))
-        if r == 0 and t == 2:
-            back_pointers(1, U("AB", 4), U("AB", 5))
-        if r == 0 and t == 1:
-            back_pointers(0, U("AB", 2), U("AB", 3))
         if r == 1 and t == 3:
             fin()
-            agat(PN, ("KI", 0, K), pl("PP", r, 0))
-            factors(0)
-        early = t < 2 or EARLY
-        if not early:
-            place(XW, IDF, EB(t))
-        if t < 3 or not early:
-            place(XU, IDF, EA(t))
-        if t == 3 and early:
-            for i in range(2):
-                act(half(db, i), half(XU, i), F_.Copy)
-            tt(EA(t), XU, EA(t), A_.mult)
-            for i in range(2):
-                act(half(da, i), half(XW, i), F_.Copy)
+
+        def side_b(i):
+            scan(half(SB, i), half(d0, i), half(D1B, i), 0.0, A_.mult, A_.add)
+        if t == 3:
+            tt(half(t2, 0), half(EX[0], 0), half(db, 0), A_.mult)
             tt(EB(t), XW, EB(t), A_.mult)
-        elif t < 3:
-            for i in range(2):
-                agat(half(db, i), zw, half(nb_, i))
-            for i in range(2):
-                agat(half(da, i), zw, half(na, i))
-            if early:
-                gtt(EB(t), zw, na, EB(t), A_.mult)
-                tt(EA(t), XU, db, A_.mult)
-        act(lane("D1A", 0, 0), db, F_.Copy)
-        act(lane("D1A", 0, 2), da, F_.Copy)
-        n = 1 if t == 3 and not early else 2
-        for i in range(n):
-            tt(half(t2, i, n), half(EX[0], i, n), half(db, i, n), A_.mult)
-            scan(half(SB, i, n), half(d0, i, n), half(D1B, i, n), 0.0, A_.mult, A_.add)
-        tt(lane("D1A", 0, 1), EX[1], da, A_.mult)
-        if r == 0:
-            act(zr(QB(t)), lane("SB", 0, 2), F_.Copy)
         else:
-            agat(zr(QB(t)), SB, pl("PI", r, t))
-        scan(zr(QA(t), L3), d0, D1A, 0.0, A_.mult, A_.add)
-        if not early:
-            tt(EB(t), XW, lane("D1A", 0, 2), A_.mult)
-            tt(EA(t), XU, lane("D1A", 0, 0), A_.mult)
-        if t > 0:
+            for x, f in ((db, nb_), (da, na)):
+                for i in range(2):
+                    agat(half(x, i), zw, half(f, i))
+            gtt(EB(t), zw, na, EB(t), A_.mult)
+            tt(half(t2, 0), half(EX[0], 0), half(db, 0), A_.mult)
+            tt(EA(t), Xe, db, A_.mult)
+        if t == 3 and RELAY:
+            hand(1 + r, [EB(t), EA(t)])
+        elif t > 0:
             send([(peer(-t), [EB(t), EA(t)], CC(t), "c%d_%d" % (r, t), 0, NE)])
         if t == 2:
             move("g", CC(3), CC(2), True)
         if t == 0:
-            move("g", CC(3), EB(0), True)
-            for i, s in enumerate((EA(0), CC(3), CC(1))):
-                place(XW, IDF, s, i == 0, i == 2)
+            for i, s in enumerate((CC(3), CC(1), EB(0), EA(0))):
+                place(XW, IDF, s, i == 0, i == 3)
+        if r == 0 and t == 2:
+            lookback(0)
+        act(lane("D1A", 0, 0), db, F_.Copy)
+        if r in GDUP:
+            gcopy(lane("D1A", 0, 2), da)
+        else:
+            act(lane("D1A", 0, 2), da, F_.Copy)
+        side_b(0)
+        flush()
+        tt(half(t2, 1), half(EX[0], 1), half(db, 1), A_.mult)
+        tt(lane("D1A", 0, 1), EX[1], da, A_.mult)
+        flush()
+        if r == 0 and t == 1:
+            split(1)
+        if more:
+            act(EX[0], AA(t - 1), F_.Square)
+        side_b(1)
+        flush()
+        if r == 0 and GQB:
+            gcopy(zr(QB(t)), lane("SB", 0, 2))
+        elif r == 0:
+            act(zr(QB(t)), lane("SB", 0, 2), F_.Copy)
+        else:
+            agat(zr(QB(t)), SB, pl("PI", r, t))
+        if more:
+            act(EX[1], BB(r, t - 1), F_.Square)
+        if r == 0 and t == 3:
+            lookback(1)
+            keep(2)
+            keep(1)
+        if r == 0 and t == 1:
+            split(2)
+        if r == 1 and t < 3:
+            negate(3 * (t - 1))
+        if r == 1 and t == 1:
+            factors(0)
+        scan(zr(QA(t), L3), d0, D1A, 0.0, A_.mult, A_.add)
 
     def vote(r):
-        old = U("KI") if r == 0 else PN
+        old = KK if r == 0 else PN
         p0, lo = U("D1B", 1), U("D1B", 2)
-        for x, b, cuts in ((EX[0], BN_, CUT), (XW, BC_, CUTW)):
-            for c in cuts:
-                place(cut(x, c), b, cut(ONE, (0, c[1] - c[0]), 512), True, False, 1)
-        for c in CUT:
-            tt(cut(POS, c), cut(p0, c), cut(EX[1], c), A_.is_lt)
-            place(cut(EX[0], c), MVN, cut(POS, c), False, True)
+        place(EX[1], NIF, CC(3), True, False)
+        for i in range(2):
+            place(half(EX[1], i), NIF, half(CC(1), i), False, True)
+        summed = (len(calls) - 1,)
+        for x, b in ((half(EX[0], 0), BN_), (half(EX[0], 1), BN_), (cut(XW, (0, 512)), BC_), (cut(XW, (512, K)), BC_)):
+            place(x, b, cut(ONE, (0, size(x)), 512), True, False, 1)
+            calls[-1]["after"] = summed
+        for i in range(2):
+            tt(half(POS, i), half(p0, i), half(EX[1], i), A_.is_lt)
+            place(half(EX[0], i), MVN, half(POS, i), False, True)
         place(XW, MVC, POS, False, True)
-        for c in CUT:
-            tt(cut(lo, c), cut(EX[0], c), cut(old, c), A_.min)
+        for i in range(2):
+            tt(half(lo, i), half(EX[0], i), half(old, i), A_.min)
         place(("PS", B7, B7 + 48), IDF, ("WO", 0, 48), True, False)
         scan(ST, XW, lo, NONE, A_.min, A_.max)
         wp = wrap([(ST, ("EH", 288, 432), range(15)), (ST, ("EH", 144, 288), [15]),
                    (("BNF", 7, 7 + K), ("EH", 0, 144), [0])], 128, False, B7)
         vcopy(cs(57), ("BNF", 7 + K, 8 + K))
-        pp = pl("PP", r + 1, 0)
         ts(("WT", 0, 48), wp, -BIG, cs(57), A_.mult, A_.min)
         tt(("WO", 0, 48), wp, ("WT", 0, 48), A_.max)
-        vcopy(pp, ("WO", 0, 48))
-        send([(peer(u), [pp], pl("PP", r + 1, u), "pp%d_%d" % (r + 1, u), NS_ * (u - 1), NS_) for u in (1, 2, 3)])
+        vcopy(pl("PP", r + 1, 0), ("WO", 0, 48))
+        spread("pp", r + 1)
 
     for r in range(RO):
         for t in range(4):
@@ -813,8 +965,11 @@ def rank_program(g, core, T, topo):
     zw = ("Z", 0, Q0B + K)
     act(CC(2), XW, F_.Copy, -0.125)
     dma("s", T.yh[:], ap(CC(2)), [CC(2)], [], nb(CC(2)))
-    for i in range(4):
-        o = U("AB", i)
-        (agat if i % 2 else vgat)(o, zw, ("FIN", 48 * i, 48 * i + 48))
-        dma("s", T.yd[:, K * i:K * i + K], ap(o), [o], [], nb(o))
+    c = 0
+    for n in LAST:
+        for gat in (vgat, agat):
+            o = ("AB", c, c + n)
+            gat(o, zw, ("FIN", c // 16, (c + n) // 16))
+            dma("s", T.yd[:, c:c + n], ap(o), [o], [], nb(o))
+            c += n
     issue()

@@ -12,7 +12,7 @@ BS0 = W
 Q0B = W + K + 3 * L2 + 2 * W
 D0 = Q0B + K
 PASSES = 2
-GDUP = ()
+GDUP = ((0, 3), (0, 2))
 GQB = True
 RELAY = False
 LAST = (768, 512, 256)
@@ -75,14 +75,14 @@ SCRATCH = {
     "MB": ("sbuf", [128, 9 * 128], "bfloat16"),
     "MF": ("sbuf", [128, 2 * 128], "float32"),
     "WO": ("sbuf", [128, 48], "float32"),
-    "WT": ("sbuf", [128, 3 * 192], "float32"),
+    "WT": ("sbuf", [128, 720], "float32"),
     "RI": ("sbuf", [128, 4], "int32"),
     "CS": ("sbuf", [128, 72], "float32"),
 }
 BYTES = {"float32": 4, "int32": 4, "bfloat16": 2, "float16": 2, "uint16": 2}
 NPOOL = 90
 ARR = (["yw%d" % t for t in (1, 2, 3)] + ["l%d_%d" % (s, t) for s in (0, 1) for t in (1, 2, 3)]
-       + ["c%d_%d" % (r, t) for r in range(RO) for t in (1, 2, 3)]
+       + ["c%d_%d" % (r, t) for r in range(RO) for t in (0, 1, 2, 3)]
        + ["pp%d_%d" % (r, t) for r in (1, 2) for t in (1, 2, 3)]
        + ["pi%d_%d" % (r, t) for r in (1, 2) for t in (1, 2, 3)])
 RELAYED = [("YW", 2 * L2, 2, 2 * L2, L2, "yw2")] + [("C", K * r, -3, 2 * K, K, "c%d_3" % r) for r in range(RO)]
@@ -125,7 +125,7 @@ def issue_order(calls):
         p.discard(i)
         before.append(p)
     data = [set(p) for p in before]
-    for q in "vag":
+    for q in "vagp":
         line = [i for i, c in enumerate(calls) if c["line"] and c["q"] == q]
         for i, j in zip(line, line[1:]):
             before[j].add(i)
@@ -141,7 +141,7 @@ def issue_order(calls):
 
     def gap(i, j, back):
         a, b = (i, j) if back else (j, i)
-        if a not in data[b]:
+        if a not in data[b] or (a in calls[b]["after"] and calls[b]["q"] != "x"):
             return span[j] + (calls[a]["hold"] - span[a])
         return span[j] + (0.0 if calls[i]["q"] + calls[j]["q"] == "pp" else SIG)
 
@@ -291,6 +291,7 @@ def rank_program(g, core, T, topo):
              [r for it in items for r in it[1]], [], ISSUE["r"] + once.pop("remote", 0.0), LAT["r"] / 2,
              nb(items[0][2]) / items[0][5] / RATE["r"], "r")
         me = len(calls) - 1
+        calls[me]["line"] = True
         for it in items:
             call("x", None, (it[3], it[5], "d"), [], [it[2]], 0.0, LAT["r"] / 2, after=(me,))
 
@@ -562,32 +563,36 @@ def rank_program(g, core, T, topo):
     ts(cs(48, 4), cs(36, 4), float(K), None, A_.mult)
     tt(cs(52, 4), cs(52, 4), cs(40, 4), A_.add)
 
-    def share(s):
+    def share(s, visits):
         send([(peer(t), [half(("LS", 96 * t, 96 * t + 96), s)], half(names(t), s), "l%d_%d" % (s, t), NS_ * (t - 1), NS_)
-              for t in (1, 2, 3)])
-    share(0)
+              for t in visits])
+    iota(half(LOC, 3, 4), [[1, K]], 3 * K + LIFT, 0)
+    share(0, (1, 2, 3))
     for u in (0, 1):
         act(half(LOC, u, 4), KK, F_.Identity, 1.0, cs(64 + u))
     ts(half(LOC, 2, 4), KK, float(2 * K + LIFT), None, A_.add)
+    tt(cs(44, 4), cs(48, 4), cs(52, 4), A_.add)
     op("v", lambda: g.vector.tensor_scalar(T.BNF[0:32, 0:K], T.BNI[0:32, :], -float(OFF), None, A_.add),
        [U("BNI")], [U("BNF")], K)
-    tt(cs(44, 4), cs(48, 4), cs(52, 4), A_.add)
-    ts(half(LOC, 3, 4), KK, float(3 * K + LIFT), None, A_.add)
-    wb = [wrap([(U("BNF"), ("E2", 144 * t, 144 * t + 144), ALL)], 32, True, 512 * t) for t in range(4)]
+    lined.update(p=0)
+    wb = {t: wrap([(U("BNF"), ("E2", 144 * t, 144 * t + 144), ALL)], 32, True, 512 * t) for t in (1, 0, 2, 3)}
+    lined.update(p=None)
 
     def names_b(t):
         ts(("LS", 96 * t + 48, 96 * t + 96), wb[t], float(OFF), None, A_.add)
+    ts(WW(0), WW(0), -0.125, None, A_.mult)
+    names_b(1)
+    share(1, (1,))
     names_b(0)
     vgat(zr(BS0), TH, half(names(0), 1))
-    names_b(1)
-    ts(WW(0), WW(0), -0.125, None, A_.mult)
     names_b(2)
     names_b(3)
     ones(IB, [[1, 128]], 1.0, 0, -1)
-    share(1)
     send([(peer(1), [("YW", 0, L2)], ("YW", L2, 2 * L2), "yw1", 0, NE)])
+    share(1, (2, 3))
     ones(E1(ROW_F[3]), ROWS, 1.0, ROW_F[3] - 15000, -1)
     dma("g", ap(zr(0, W)), T.th[:], [], [zr(0, W)], nb(zr(0, W)))
+    begun = len(calls) - 1
     if RELAY:
         hand(0, [("YW", 0, L2)])
     else:
@@ -622,6 +627,9 @@ def rank_program(g, core, T, topo):
         last16 = (m[0], m[1] + 112, m[2])
         select(last16, last16, [[0, 16]], A_.is_ge, float(v), -16, 1)
     fill(ONE, 1)
+    for c in calls[begun + 1:]:
+        if c["tok"] is None:
+            c["after"] = (begun,)
 
     small = []
 
@@ -656,12 +664,12 @@ def rank_program(g, core, T, topo):
     def ids(t, s):
         act(half(IO, s) if t < 3 else (EX[0], XU)[s], KK, F_.Identity, cs(32 + 4 * s + t), cs(40 + 4 * s + t))
 
-    def marks(t, s):
-        o, a, b = half(names(t), s), half(GB, s), half(IO, s)
+    def marks(t, s, n=2):
+        o, a, b = half(names(t), s, n), half(GB, s, n), half(IO, s, n)
         if t in (0, 3):
-            ascat(LOC, o, a if t else b)
+            ascat(LOC, o, b)
         else:
-            op("v", lambda: g.vector.tensor_tensor(ind(LOC, o), ap(a), ap(b), A_.max), [o, a, b], [LOC], K * SCA)
+            op("v", lambda: g.vector.tensor_tensor(ind(LOC, o), ap(a), ap(b), A_.max), [o, a, b], [LOC], size(a) * SCA)
 
     def lookup(t):
         for s in (1, 0):
@@ -669,17 +677,21 @@ def rank_program(g, core, T, topo):
         index(fwd(t), wrap([(GB, E1(ROW_F[3]), ALL)]), 0, 4)
     KEPT = {3: U("AB", 1), 2: U("AB", 6), 1: U("AB", 7), 0: U("AB", 5)}
 
-    def lookback(t):
+    def lookback(t, sides=(0, 1)):
         x = zr(QV(2) + L2 * (2 - t), L2) if t else ("AB", 4 * K, 6 * K)
-        for s in range(2):
+        for s in sides:
             agat(half(x, s), LOC, half(names(t), s))
-        index_n(t, nxt(t), wrap([(x, E1(ROW_N[t]), ALL)]), (3, 2, 1)[t])
+        if 1 in sides:
+            lined.update(p=0)
+            index_n(t, nxt(t), wrap([(x, E1(ROW_N[t]), ALL)]), 0 if t else 1)
+            lined.update(p=None)
 
     def keep(t):
         move("s", KEPT[t], zr(QV(2) + L2 * (2 - t) + K))
 
     def gcopy(out, src):
         select(out, src, [[0, size(out)]], A_.is_ge, 0.0, 0, 0)
+        calls[-1]["line"] = True
 
     def split(t, src=None):
         act(U("G", t), src or KEPT[t], F_.Copy, cs(56))
@@ -689,28 +701,38 @@ def rank_program(g, core, T, topo):
     def compose(r, t):
         agat(U("GT"), U("G", t), pl("PP", r, t))
         if t > 0:
-            index(half(fwd(t), 1), wrap([(U("GT"), EG(ROW_F[t]), ALL)]), 0, 1)
+            index(half(fwd(t), 1), wrap([(U("GT"), EG(ROW_F[t]), ALL)]), 0)
         if t < 3:
-            index_n(t, half(nxt(t), 1), wrap([(U("GT"), EG(ROW_N[t]), ALL)]), 2)
+            index_n(t, half(nxt(t), 1), wrap([(U("GT"), EG(ROW_N[t]), ALL)]))
 
-    def fin():
-        for i in range(2):
-            wrap([(half(LOC, i), E1(ROW_FIN), ALL)], c0=B7 + 320 + 96 * i)
+    def fin(part):
         w = ("PS", B7 + 320, B7 + 512)
-        x, y = ("WT", 0, 192), ("WT", 192, 384)
-        z = ("WT", 384, 576)
-        soon(3, ts, x, w, QV(1) + LIFT - 0.5, float(QA(1) - QV(1)), A_.is_gt, A_.mult)
-        soon(3, ts, y, w, QV(0) + LIFT - 0.5, float(QA(0) - QV(0) - QA(1) + QV(1)), A_.is_gt, A_.mult)
-        soon(3, ts, z, w, QV(0) + L3 + LIFT - 0.5, float(QB(0) - L3 - QA(0)), A_.is_gt, A_.mult)
-        soon(3, tt, x, w, x, A_.add)
-        for i, s in enumerate((x, y, z)):
-            soon(3, place, w, IDF, s, i == 0, i == 2)
-        index(("FIN", 0, 192), w, 0, 3)
+        x, y, z = [("WT", 96 + 192 * i, 288 + 192 * i) for i in range(3)]
+        was = lined["v"]
+        lined.update(v=0)
+        if part == 0:
+            for i in range(2):
+                wrap([(half(LOC, i), E1(ROW_FIN), ALL)], c0=B7 + 320 + 96 * i)
+        elif part == 1:
+            ts(x, w, QV(1) + LIFT - 0.5, float(QA(1) - QV(1)), A_.is_gt, A_.mult)
+            ts(y, w, QV(0) + LIFT - 0.5, float(QA(0) - QV(0) - QA(1) + QV(1)), A_.is_gt, A_.mult)
+            ts(z, w, QV(0) + L3 + LIFT - 0.5, float(QB(0) - L3 - QA(0)), A_.is_gt, A_.mult)
+        elif part == 2:
+            tt(x, w, x, A_.add)
+            for i, s in enumerate((x, y, z)):
+                place(w, IDF, s, i == 0, i == 2)
+        else:
+            ts(("FIN", 0, 192), w, 0.25 - LIFT, None, A_.add)
+        lined.update(v=was)
 
-    def take_va(t):
-        for s in range(2):
-            agat(half(TMP if t < 3 else N3, s), VA, half(names(t), s), -1.0)
-        if t < 3:
+    def take_va(t, sides=(0, 1)):
+        for s in sides:
+            out, off = half(TMP if t < 3 else N3, s), half(names(t), s)
+            if (t, s) == (0, 1):
+                op("v", lambda: g.vector.tensor_scalar(ap(out), ind(VA, off), -1.0, None, A_.mult), [VA, off], [out], K * GAT)
+            else:
+                agat(out, VA, off, -1.0)
+        if t < 3 and 1 in sides:
             dma("s", T.NVD[t], ap(TMP), [TMP], [("NVD", t, t + 1)], nb(TMP))
 
     def minus_va(t):
@@ -743,16 +765,22 @@ def rank_program(g, core, T, topo):
             if r == 0 and t < 3:
                 marks(t, 0)
             if r == 0 and t == 1:
-                marks(t, 1)
+                marks(t, 2, 4)
             if r == 0 and t == 3:
-                tt(half(GB, 0), EX[0], half(GB, 0), A_.max)
+                tt(half(IO, 0), EX[0], half(GB, 0), A_.max)
             flush(fwd(t))
             for x, f in ((B, fb), (A, fa)):
                 for i in range(2):
                     agat(half(x, i), zw, half(f, i))
-            if (t > 1 or last) and not (r == 0 and t == 3):
+            if r == 0 and t == 1:
+                marks(t, 3, 4)
+            elif r == 0 and t == 3:
+                take_va(0, (1,))
+            elif t > 1 or last:
                 m = lane("Z", D0 + L3 * (t - 1), 1)
                 tt(m, EX[1 - t % 2], m, A_.add)
+            if r:
+                flush()
         for i in range(2):
             if r > 0 and t == 0:
                 gtt(half(P, i), zr(BS0), half(pp, i), half(A, i), A_.mult)
@@ -762,7 +790,7 @@ def rank_program(g, core, T, topo):
             take_va(1)
             marks(t, 1)
         if r == 0 and t == 3:
-            tt(half(GB, 1), XU, half(GB, 1), A_.max)
+            tt(half(IO, 1), XU, half(GB, 1), A_.max)
             marks(t, 0)
             marks(t, 1)
         for i in range(2):
@@ -775,7 +803,7 @@ def rank_program(g, core, T, topo):
             else:
                 move("s", KEPT[3], half(GB, 1))
                 split(3, half(GB, 1))
-            take_va((3, 2, 0)[t])
+            take_va((3, 2, 0)[t], (0, 1) if t < 2 else (0,))
         if r > 0 and t == 0:
             ascat(U("D1B"), pp, ("KI", LIFT, LIFT + K))
             act(ST, U("D1B"), F_.Identity, 1.0, cs(60))
@@ -794,9 +822,38 @@ def rank_program(g, core, T, topo):
             if last:
                 for i in range(2):
                     move("g", half(zr(0, W), i), half(VA, i), True)
-            act(EX[0], A, F_.Square)
+            if not last:
+                act(EX[0], A, F_.Square)
+            if r == 1:
+                negate(0)
+                negate(3)
         for i in range(2):
             tt(half(EA(t), i), half(Xy, i), half(A, i), A_.mult)
+        if last and t == 3:
+            da, db = lane("D1B", 0, 0), lane("D1B", 0, 2)
+            xa, xb = U("D1A", 0), U("D1A", 1)
+            lined.update(p=0)
+            for x, v, nv in ((XU, B, NV3), (EX[0], A, half(N3, 0))):
+                place(x, IB, nv, True, False)
+                place(x, IDF, v, False, True)
+            lined.update(p=None)
+            tt(EB(t), Xy, B, A_.mult)
+            tt(xb, EA(t), XW, A_.mult)
+            tt(xa, EB(t), XW, A_.mult)
+            tt(XU, XU, xb, A_.add)
+            act(XW, A, F_.Square)
+            tt(EX[0], EX[0], xa, A_.add)
+            tt(P, Xy, P, A_.add)
+            for i in range(2):
+                act(half(db, i), half(XU, i), F_.Copy)
+            copied = len(calls) - 1
+            tt(EB(t), EX[0], EB(t), A_.mult)
+            for i in range(2):
+                act(half(da, i), half(EX[0], i), F_.Copy)
+            act(EX[1], B, F_.Square)
+            tt(EA(t), XU, EA(t), A_.mult)
+            calls[-1]["after"] = (copied,)
+            return
         tt(half(EB(t), 0), half(Xy, 0), half(B, 0), A_.mult)
         tt(XU, EA(t), XW, A_.mult)
         tt(half(EB(t), 1), half(Xy, 1), half(B, 1), A_.mult)
@@ -804,38 +861,33 @@ def rank_program(g, core, T, topo):
             tt(P, Xy, P, A_.add)
             ids(3, 0)
         if t < 3:
-            if t > 0:
-                flush()
             tt(lane("SB", 0, 2) if r else ob, XU, B, A_.add)
-            flush()
             if r and t == 0:
+                flush()
                 spread("pi", r)
             if r:
                 agat(ob, ("SB", 0, L3), pl("PI", r, t))
             elif t == 2:
                 ids(3, 1)
             tt(XW, EB(t), XW, A_.mult)
-            flush()
+            if r:
+                flush()
             tt(oa, XW, A, A_.add)
             return
         da, db = lane("D1B", 0, 0), lane("D1B", 0, 2)
         if r == 0:
-            lookback(2)
-        if r:
-            flush()
+            lookback(2, (0,))
         tt(XU, XU, B, A_.add)
         tt(XW, EB(t), XW, A_.mult)
-        if r:
-            flush()
         tt(XU, XU, NV3 if r else half(N3, 1), A_.add)
         tt(XW, XW, A, A_.add)
-        if r:
-            flush()
         tt(P, Xy, P, A_.add)
         tt(XW, XW, half(N3, 0), A_.add)
         for x, y in ((db, XU), (da, XW)):
             for i in range(2):
                 act(half(x, i), half(y, i), F_.Copy)
+            if r == 0 and y == XU:
+                lookback(2, (1,))
         act(EX[1], B, F_.Square)
         tt(EA(t), XU, EA(t), A_.mult)
 
@@ -848,11 +900,9 @@ def rank_program(g, core, T, topo):
         zw = ("Z", FB(t), QV(2) if t == 2 else QV(1))
         na, nb_ = half(nxt(t), 0), half(nxt(t), 1)
         Xe = ("PS", 3072, 3072 + K) if last and t == 0 else XU
-        if t < 3:
-            place(Xe, IDF, EA(t))
-            flush(nxt(t))
-        if t == 0:
-            flush(("FIN", 0, 192))
+        Xa = XW if last and t == 3 else EX[0]
+        if t < 3 and r:
+            flush()
         if not last and t == 0:
             for i in range(2):
                 agat(half(U("D1B"), i), zw, half(nb_, i))
@@ -866,48 +916,75 @@ def rank_program(g, core, T, topo):
             for i in range(2):
                 tt(half(U("D1B", 1), i), half(XU, i), half(EB(0), i), A_.add)
             return
-        if r == 1 and t == 3:
-            fin()
+        if t == 3 and r:
+            fin(2 * r - 2)
 
         def side_b(i):
             scan(half(SB, i), half(d0, i), half(D1B, i), 0.0, A_.mult, A_.add)
+
+        def home(i, n, sem):
+            send([(peer(-t), [half(EB(t), i, n), half(EA(t), i, n)], half(CC(t), i, n), sem, 0, NE)])
         if t == 3:
-            tt(half(t2, 0), half(EX[0], 0), half(db, 0), A_.mult)
-            tt(EB(t), XW, EB(t), A_.mult)
+            tt(half(t2, 0), half(Xa, 0), half(db, 0), A_.mult)
+            if not last:
+                tt(EB(t), XW, EB(t), A_.mult)
         else:
             for x, f in ((db, nb_), (da, na)):
                 for i in range(2):
                     agat(half(x, i), zw, half(f, i))
+        if t == 1:
+            for i in range(2):
+                gtt(half(EB(t), i), zw, half(na, i), half(EB(t), i), A_.mult)
+            tt(half(EA(t), 0), half(Xe, 0), half(db, 0), A_.mult)
+            home(0, 2, "c%d_0" % r)
+            tt(half(t2, 0), half(EX[0], 0), half(db, 0), A_.mult)
+            tt(half(EA(t), 1), half(Xe, 1), half(db, 1), A_.mult)
+            home(1, 2, "c%d_1" % r)
+            if last:
+                move("g", CC(3), CC(2), True)
+                calls[-1]["after"] = (len(calls) - 3,)
+        elif t < 3:
             gtt(EB(t), zw, na, EB(t), A_.mult)
             tt(half(t2, 0), half(EX[0], 0), half(db, 0), A_.mult)
             tt(EA(t), Xe, db, A_.mult)
         if t == 3 and RELAY:
             hand(1 + r, [EB(t), EA(t)])
-        elif t > 0:
-            send([(peer(-t), [EB(t), EA(t)], CC(t), "c%d_%d" % (r, t), 0, NE)])
-        if t == 2:
-            move("g", CC(3), CC(2), True)
+        elif t > 1:
+            home(0, 1, "c%d_%d" % (r, t))
+        lined.update(p=0)
         if t == 0:
             for i, s in enumerate((CC(3), CC(1), EB(0), EA(0))):
                 place(XW, IDF, s, i == 0, i == 3)
+        else:
+            x = ("PS", 3072, 3072 + K) if last and t == 1 else XU
+            for c in ((0, 256), (256, K)):
+                place(cut(x, c), IDF, cut(EA(t - 1), c))
+            if r == 0 and t == 1:
+                place(EX[1], NIF, CC(3), True, False)
+        lined.update(p=None)
         if r == 0 and t == 2:
             lookback(0)
         act(lane("D1A", 0, 0), db, F_.Copy)
-        if r in GDUP:
+        if (r, t) in GDUP:
             gcopy(lane("D1A", 0, 2), da)
         else:
             act(lane("D1A", 0, 2), da, F_.Copy)
         side_b(0)
-        flush()
-        tt(half(t2, 1), half(EX[0], 1), half(db, 1), A_.mult)
-        tt(lane("D1A", 0, 1), EX[1], da, A_.mult)
-        flush()
+        if r == 0 and t == 1:
+            flush()
+        tt(half(t2, 1), half(Xa, 1), half(db, 1), A_.mult)
+        tt(lane("D1A", 0, 1), XW if t == 1 and not last else EX[1], da, A_.mult)
+        if r == 0:
+            flush()
+        if last and t == 3:
+            fin(3)
         if r == 0 and t == 1:
             split(1)
         if more:
             act(EX[0], AA(t - 1), F_.Square)
         side_b(1)
-        flush()
+        if r == 0 and t == 1:
+            flush()
         if r == 0 and GQB:
             gcopy(zr(QB(t)), lane("SB", 0, 2))
         elif r == 0:
@@ -915,15 +992,17 @@ def rank_program(g, core, T, topo):
         else:
             agat(zr(QB(t)), SB, pl("PI", r, t))
         if more:
-            act(EX[1], BB(r, t - 1), F_.Square)
+            act(XW if t == 2 and not last else EX[1], BB(r, t - 1), F_.Square)
         if r == 0 and t == 3:
             lookback(1)
             keep(2)
             keep(1)
         if r == 0 and t == 1:
             split(2)
-        if r == 1 and t < 3:
-            negate(3 * (t - 1))
+        if t == 2 and r == 1:
+            lined.update(p=0)
+            place(EX[1], NIF, CC(3), True, False)
+            lined.update(p=None)
         if r == 1 and t == 1:
             factors(0)
         scan(zr(QA(t), L3), d0, D1A, 0.0, A_.mult, A_.add)
@@ -931,27 +1010,35 @@ def rank_program(g, core, T, topo):
     def vote(r):
         old = KK if r == 0 else PN
         p0, lo = U("D1B", 1), U("D1B", 2)
-        place(EX[1], NIF, CC(3), True, False)
-        for i in range(2):
-            place(half(EX[1], i), NIF, half(CC(1), i), False, True)
-        summed = (len(calls) - 1,)
-        for x, b in ((half(EX[0], 0), BN_), (half(EX[0], 1), BN_), (cut(XW, (0, 512)), BC_), (cut(XW, (512, K)), BC_)):
+
+        def bias(x, b):
             place(x, b, cut(ONE, (0, size(x)), 512), True, False, 1)
-            calls[-1]["after"] = summed
+        lined.update(p=0)
+        for x, b in ((half(EX[0], 0), BN_), (half(EX[0], 1), BN_), (cut(XW, (0, 512)), BC_)):
+            bias(x, b)
+        for c in (2, 1):
+            for i in range(2):
+                place(half(EX[1], i), NIF, half(CC(c), i), False, c == 1)
+        bias(cut(XW, (512, K)), BC_)
+        place(("PS", 3072, 3072 + 48), IDF, ("WO", 0, 48), True, False)
         for i in range(2):
             tt(half(POS, i), half(p0, i), half(EX[1], i), A_.is_lt)
             place(half(EX[0], i), MVN, half(POS, i), False, True)
         place(XW, MVC, POS, False, True)
+        lined.update(p=None)
         for i in range(2):
             tt(half(lo, i), half(EX[0], i), half(old, i), A_.min)
-        place(("PS", B7, B7 + 48), IDF, ("WO", 0, 48), True, False)
         scan(ST, XW, lo, NONE, A_.min, A_.max)
         wp = wrap([(ST, ("EH", 288, 432), range(15)), (ST, ("EH", 144, 288), [15]),
-                   (("BNF", 7, 7 + K), ("EH", 0, 144), [0])], 128, False, B7)
+                   (("BNF", 7, 7 + K), ("EH", 0, 144), [0])], 128, False, 3072)
+        lined.update(v=0)
         vcopy(cs(57), ("BNF", 7 + K, 8 + K))
-        ts(("WT", 0, 48), wp, -BIG, cs(57), A_.mult, A_.min)
-        tt(("WO", 0, 48), wp, ("WT", 0, 48), A_.max)
+        if r == 1:
+            fin(1)
+        ts(("WT", 672, 720), wp, -BIG, cs(57), A_.mult, A_.min)
+        tt(("WO", 0, 48), wp, ("WT", 672, 720), A_.max)
         vcopy(pl("PP", r + 1, 0), ("WO", 0, 48))
+        lined.update(v=256)
         spread("pp", r + 1)
 
     for r in range(RO):

@@ -11,18 +11,17 @@ NONE = -1024.0
 BS0 = W
 Q0B = W + K + 3 * L2 + 2 * W
 D0 = Q0B + K
+PC = ((0, 256), (256, K))
 PASSES = 2
-GDUP = ((0, 3), (0, 2))
-GQB = True
-RELAY = False
-LAST = (768, 512, 256)
+LANES = {(0, 3): "gg", (0, 1): "aa"}
+LAST = (("a", 0), ("v", 256), ("a", 256), ("v", 512), ("a", 512), ("v", 512), ("a", 448), ("v", 320), ("a", 256))
 LOG = []
 ORDER = []
 
-CYC, PCYC, GAT, SCA, SIG = 0.83e-3, 0.6e-3, 1.3, 2.5, 0.15
-START = {"v": 0.05, "a": 0.15, "p": 0.05, "g": 0.05}
+CYC, PCYC, GAT, SCA, SIG = 0.83e-3, 0.5e-3, 1.5, 3.0, 0.12
+START = {"v": 0.06, "a": 0.08, "p": 0.05, "g": 0.05}
 ISSUE, LAT, RATE = {"g": 1.0, "s": 0.1, "a": 0.1, "r": 0.6}, {"d": 2.0, "r": 2.5}, {"d": 550e3, "r": 10e3}
-ONCE = {"remote": 2.0, "table": 1.3, "dma": 1.0}
+ONCE = {"remote": 3.6, "table": 1.3, "dma": 1.0}
 
 
 def FB(t):
@@ -41,7 +40,7 @@ def QB(t):
     return Q0B if t == 0 else QA(t) + L3
 
 
-ROW_FIN, ROW_N, ROW_F = 1, (2, 3, 4), (None, 5, 6, 7)
+ROW_FIN, ROW_N, ROW_F = 0, (1, 2, 3), (None, 5, 6, 7)
 
 SCRATCH = {
     "PS": ("psum", [128, 4096], "float32"),
@@ -49,7 +48,7 @@ SCRATCH = {
     "AB": ("sbuf", [128, 4 * L2], "float32"),
     "EE": ("sbuf", [128, 4 * L2], "float32"),
     "D1A": ("sbuf", [128, L3], "float32"),
-    "D1B": ("sbuf", [128, L3], "float32"),
+    "D1": ("sbuf", [128, L3], "float32"),
     "SB": ("sbuf", [128, L3], "float32"),
     "C": ("sbuf", [128, L3], "float32"),
     "KI": ("sbuf", [128, K + LIFT], "float32"),
@@ -61,8 +60,8 @@ SCRATCH = {
     "BNI": ("sbuf", [128, K], "int32"),
     "BNF": ("sbuf", [128, K + 8], IDX),
     "ANI": ("sbuf", [128, 192], "int32"),
-    "LS": ("sbuf", [128, 4 * 96], "uint16"),
-    "LV": ("sbuf", [128, 4 * 96], "uint16"),
+    "LS": ("sbuf", [128, 2 * 192], "uint16"),
+    "LV": ("sbuf", [128, 2 * 192], "uint16"),
     "FL": ("sbuf", [128, 4 * 96], "uint16"),
     "NL": ("sbuf", [128, 3 * 96], "uint16"),
     "FIN": ("sbuf", [128, 192], "uint16"),
@@ -72,20 +71,23 @@ SCRATCH = {
     "E2": ("sbuf", [128, 4 * 144], IDX),
     "EH": ("sbuf", [128, 3 * 144], IDX),
     "EG": ("sbuf", [128, 6 * 144], "bfloat16"),
-    "MB": ("sbuf", [128, 9 * 128], "bfloat16"),
+    "MB": ("sbuf", [128, 10 * 128], "bfloat16"),
     "MF": ("sbuf", [128, 2 * 128], "float32"),
     "WO": ("sbuf", [128, 48], "float32"),
     "WT": ("sbuf", [128, 720], "float32"),
     "RI": ("sbuf", [128, 4], "int32"),
-    "CS": ("sbuf", [128, 72], "float32"),
+    "CS": ("sbuf", [128, 96], "float32"),
 }
 BYTES = {"float32": 4, "int32": 4, "bfloat16": 2, "float16": 2, "uint16": 2}
-NPOOL = 90
-ARR = (["yw%d" % t for t in (1, 2, 3)] + ["l%d_%d" % (s, t) for s in (0, 1) for t in (1, 2, 3)]
-       + ["c%d_%d" % (r, t) for r in range(RO) for t in (0, 1, 2, 3)]
+NPOOL = 95
+RELAYED = [(("YW", 0, K), 3, ("YW", 7 * K, 8 * K), "yw5")]
+for _r in range(RO):
+    RELAYED += [(("Z", L2 * _r, L2 * _r + K), -3, ("C", 2 * K, 3 * K), "c%d_3" % _r),
+                (("Z", L2 * _r + K, L2 * _r + K + 256), -2, ("C", K, K + 256), "c%d_4" % _r)]
+ARR = (["yw1", "yw2", "yw3", "yw4", "yw5"] + ["l%d_%d" % (s, t) for s in (0, 1) for t in (1, 2, 3)]
+       + ["c%d_%d" % (r, t) for r in range(RO) for t in range(5)]
        + ["pp%d_%d" % (r, t) for r in (1, 2) for t in (1, 2, 3)]
        + ["pi%d_%d" % (r, t) for r in (1, 2) for t in (1, 2, 3)])
-RELAYED = [("YW", 2 * L2, 2, 2 * L2, L2, "yw2")] + [("C", K * r, -3, 2 * K, K, "c%d_3" % r) for r in range(RO)]
 SEMAPHORES = (["qv", "qa", "qp", "qg"] + ARR + ["s%d" % i for i in range(NPOOL)]
               + ["h%d" % i for i in range(len(RELAYED))])
 
@@ -125,7 +127,7 @@ def issue_order(calls):
         p.discard(i)
         before.append(p)
     data = [set(p) for p in before]
-    for q in "vagp":
+    for q in "vagps":
         line = [i for i, c in enumerate(calls) if c["line"] and c["q"] == q]
         for i, j in zip(line, line[1:]):
             before[j].add(i)
@@ -198,11 +200,12 @@ def helper_of(c, T, topo):
 def relay(g, core, T, topo, rank):
     cores = list(T.cores)
     total = 0
-    for i, (buf, c0, d, c1, n, sem) in enumerate(RELAYED):
+    for i, (land, d, there, sem) in enumerate(RELAYED):
         to = cores[(rank + d) % len(cores)]
         rid, pid, _ = topo.addr(to)
         g.wait_ge(T.sem["h%d" % i], len(topo.engines(cores[rank], core)) - len(topo.engines(core, to)))
-        g.remote_dma(T[buf][:, c1:c1 + n], T[buf][:, c0:c0 + n], T.sem[sem], T.sem.s0, pid, rid, topo.mask(core, to))
+        g.remote_dma(T[there[0]][:, there[1]:there[2]], T[land[0]][:, land[1]:land[2]], T.sem[sem], T.sem.s0, pid, rid,
+                     topo.mask(core, to))
         total += len(topo.engines(core, to))
     g.wait_ge(T.sem.s0, total)
 
@@ -212,7 +215,7 @@ def rank_program(g, core, T, topo):
     cores = list(T.cores)
     if rank is None:
         for r, c in enumerate(cores):
-            if RELAY and helper_of(c, T, topo) == core:
+            if helper_of(c, T, topo) == core:
                 relay(g, core, T, topo, r)
         return
     N = len(cores)
@@ -222,24 +225,25 @@ def rank_program(g, core, T, topo):
     calls = []
     pool = [0]
     once = dict(ONCE)
-    lined = {"v": 0, "a": 0, "g": 0}
+    lined = {q: True for q in Q}
 
     def newsem():
         pool[0] += 1
         return "s%d" % (pool[0] - 1)
 
-    def call(q, fn, tok, reads, writes, hold, lag=0.0, nbytes=0.0, way=None, after=(), cycles=0):
+    def call(q, fn, tok, reads, writes, hold, lag=0.0, nbytes=0.0, way=None, after=()):
         calls.append(dict(q=q, fn=fn, tok=tok, reads=list(reads), writes=list(writes), hold=hold, lag=lag, bytes=nbytes,
-                          way=way, after=after, line=lined.get(q) is not None and cycles >= lined[q]))
+                          way=way, after=after, line=lined.get(q, False)))
 
     def op(q, fn, reads, writes, cycles):
-        call(q, fn, None, reads, writes, START[q] + cycles * (PCYC if q == "p" else CYC), cycles=cycles)
+        call(q, fn, None, reads, writes, START[q] + cycles * (PCYC if q == "p" else CYC))
 
     def free(f, *args):
         was = dict(lined)
-        lined.update(v=None, a=None, g=None)
-        f(*args)
+        lined.update(v=False, a=False, g=False, p=False)
+        out = f(*args)
         lined.update(was)
+        return out
 
     def dma(q, out, in_, reads, writes, nbytes, add=False):
         s = newsem()
@@ -275,18 +279,18 @@ def rank_program(g, core, T, topo):
             m |= 1 << e
         return m
     NE = len(topo.engines(core, peer(1)))
-    NS_ = NE // 4
+    SHARE = {1: (0, NE // 2), 2: (NE // 2, NE // 4), 3: (NE // 2 + NE // 4, NE // 4)}
+
+    def transfer(c, mask, sem, srcs, land):
+        if len(srcs) == 1:
+            return RemoteDMATransfer(dst_ids=[dst(c)], dma_engine_mask=mask, remote_sem=T.sem[sem], src=ap(srcs[0]),
+                                     dst=ap(land))
+        return RemoteDMATransfer(dst_ids=[dst(c)], dma_engine_mask=mask, remote_sem=T.sem[sem],
+                                 srcs=[ap(r) for r in srcs], dsts=[ap(land)], alu_op=1)
 
     def send(items):
         s = newsem()
-        trs = []
-        for (c, srcs, land, sem, i0, n) in items:
-            if len(srcs) == 1:
-                trs.append(RemoteDMATransfer(dst_ids=[dst(c)], dma_engine_mask=emask(c, i0, n), remote_sem=T.sem[sem],
-                                             src=ap(srcs[0]), dst=ap(land)))
-            else:
-                trs.append(RemoteDMATransfer(dst_ids=[dst(c)], dma_engine_mask=emask(c, i0, n), remote_sem=T.sem[sem],
-                                             srcs=[ap(r) for r in srcs], dsts=[ap(land)], alu_op=1))
+        trs = [transfer(c, emask(c, i0, n), sem, srcs, land) for (c, srcs, land, sem, i0, n) in items]
         call("g", lambda: g.remote_dma_fused(trs, local_sem=T.sem[s]), (s, sum(it[5] for it in items), "d"),
              [r for it in items for r in it[1]], [], ISSUE["r"] + once.pop("remote", 0.0), LAT["r"] / 2,
              nb(items[0][2]) / items[0][5] / RATE["r"], "r")
@@ -295,41 +299,35 @@ def rank_program(g, core, T, topo):
         for it in items:
             call("x", None, (it[3], it[5], "d"), [], [it[2]], 0.0, LAT["r"] / 2, after=(me,))
 
-    def hand(i, srcs):
-        buf, c0, d, c1, n, sem = RELAYED[i]
+    def hand(sem, srcs):
+        i = [x[3] for x in RELAYED].index(sem)
+        land, d, there = RELAYED[i][:3]
         h = helper_of(core, T, topo)
         mask = topo.mask(core, h) & ~topo.mask(core, peer(1))
         ne = len(topo.engines(core, h)) - NE
         s = newsem()
-        land = (buf, c0, c0 + n)
-        if len(srcs) == 1:
-            tr = RemoteDMATransfer(dst_ids=[dst(h)], dma_engine_mask=mask, remote_sem=T.sem["h%d" % i], src=ap(srcs[0]),
-                                   dst=ap(land))
-        else:
-            tr = RemoteDMATransfer(dst_ids=[dst(h)], dma_engine_mask=mask, remote_sem=T.sem["h%d" % i],
-                                   srcs=[ap(r) for r in srcs], dsts=[ap(land)], alu_op=1)
+        tr = transfer(h, mask, "h%d" % i, srcs, land)
         call("g", lambda: g.remote_dma_fused([tr], local_sem=T.sem[s]), (s, ne, "d"), srcs, [], ISSUE["r"], LAT["r"] / 2,
              nb(land) / ne / RATE["r"] / 2, "h")
-        call("x", None, (sem, NE, "d"), [], [(buf, c1, c1 + n)], 0.0, 2 * LAT["r"] + nb(land) / NE / RATE["r"],
+        calls[-1]["line"] = True
+        call("x", None, (sem, NE, "d"), [], [there], 0.0, 2 * LAT["r"] + nb(land) / NE / RATE["r"],
              after=(len(calls) - 1,))
 
     def spread(n, r):
-        send([(peer(u), [pl(n.upper(), r, 0)], pl(n.upper(), r, u), "%s%d_%d" % (n, r, u), NS_ * (u - 1), NS_)
-              for u in (1, 2, 3)])
+        for share in (({1: (0, NE)}, {2: (0, NE // 2), 3: (NE // 2, NE // 2)}) if n == "pp" else (SHARE,)):
+            send([(peer(u), [pl(n.upper(), r, 0)], pl(n.upper(), r, u), "%s%d_%d" % (n, r, u)) + e
+                  for u, e in share.items()])
 
     def issue():
         count = {q: 0 for q in Q}
         waited, final, acc, banks = {}, {}, {}, {}
-        if not ORDER:
-            ORDER.extend(issue_order(calls))
-        for i in ORDER:
-            c = calls[i]
+        for c in calls:
             q, tok = c["q"], c["tok"]
             want = {}
             for regs, isw in ((c["reads"], False), (c["writes"], True)):
                 for r in regs:
                     for (x, k, w) in acc.get(r[0], []):
-                        if (w or isw) and meet(x, r) and not (q == "p" and k[2] == "p"):
+                        if (w or isw) and meet(x, r) and not (q == k[2] and tok is None and (q == "p" or not w)):
                             want[k[0]] = max(want.get(k[0], 0), k[1])
             bs = banks_of(c["reads"] + c["writes"])
             for b in bs:
@@ -410,6 +408,9 @@ def rank_program(g, core, T, topo):
     def select(out, src, pat, o, v, base, cm):
         op("g", lambda: g.affine_select(ap(out), ap(src), pat, o, v, base, cm), [src], [out], 150 + 2 * size(out))
 
+    def gcopy(out, src):
+        select(out, src, [[0, size(out)]], A_.is_ge, 0.0, 0, 0)
+
     def matmuls(out, rd, todo, shut):
         grp = [("GRP", b, b + 1) for b in banks_of([out])]
 
@@ -424,17 +425,18 @@ def rank_program(g, core, T, topo):
 
     def place(out, lhs, src, start=True, stop=True, parts=128):
         cuts = [out[1]] + [b for b in range(0, 4096, 512) if out[1] < b < out[2]] + [out[2]]
+        s = step(src)
         todo = [(T.PS[:, c0:c1], T[lhs[0]][0:parts, lhs[1]:lhs[2]],
-                 T[src[0]][0:parts, src[1] + c0 - out[1]:src[1] + c1 - out[1]], start, stop)
+                 T[src[0]][0:parts, src[1] + s * (c0 - out[1]):min(src[2], src[1] + s * (c1 - out[1])):s], start, stop)
                 for c0, c1 in zip(cuts[:-1], cuts[1:])]
         matmuls(out, [lhs, src], todo, start and stop)
 
-    slot = [48]
+    slot = [0]
 
     def wrap(terms, parts=128, start=True, c0=None):
         n = size(terms[0][0]) // 16
         if c0 is None:
-            c0 = B7 + (slot[0] if slot[0] + n <= 320 else 48)
+            c0 = B7 + (slot[0] if slot[0] + n <= 320 else 0)
             slot[0] = c0 - B7 + n
         out = ("PS", c0, c0 + n)
         each = [(src, em, i) for src, em, which in terms for i in which]
@@ -450,6 +452,9 @@ def rank_program(g, core, T, topo):
 
     def half(r, i, n=2):
         return cut(r, (i, i + 1), n)
+
+    def pc(r, i):
+        return cut(r, PC[i])
 
     def lane(n, base, k):
         return (n, base + k, base + L3, 3)
@@ -468,19 +473,24 @@ def rank_program(g, core, T, topo):
         return ("E1", 144 * i.index(r), 144 * i.index(r) + 144)
 
     def EG(r):
-        return ("EG", 144 * (r - 2), 144 * (r - 2) + 144)
-    IB, MVN, MVC, BN_, BC_ = [("MB", 128 * i, 128 * i + 128) for i in range(5)]
-    ONE = ("MB", 640, 1152)
+        i = (ROW_N + ROW_F[1:]).index(r)
+        return ("EG", 144 * i, 144 * i + 144)
+    IB, MVN, BN_, MVC, BC_ = [("MB", 128 * i, 128 * i + 128) for i in range(5)]
+    ONE, NIB = ("MB", 640, 1152), ("MB", 1152, 1280)
     IDF, NIF = ("MF", 0, 128), ("MF", 128, 256)
-    EX = [("PS", 128, 128 + K), ("PS", 1152, 1152 + K)]
+    EX = [("PS", 256, 256 + K), ("PS", 1280, 1280 + K)]
     XW, XU = ("PS", 2048, 2048 + K), ("PS", 2048 + K, 2048 + L2)
+    AA3 = [("PS", 1024, 1280), pc(XU, 1)]
     B7 = 3584
 
-    def names(t):
-        return ("LS" if t == 0 else "LV", 96 * t, 96 * t + 96)
+    def own(t, s, n=1):
+        return ("LS", 192 * s + 48 * t, 192 * s + 48 * (t + n))
 
-    def fwd(t):
-        return names(0) if t == 0 else ("FL", 96 * t, 96 * t + 96)
+    def names(t, s):
+        return ("LV" if t else "LS",) + own(t, s)[1:]
+
+    def fwd(t, s):
+        return ("FL", 96 * t + 48 * s, 96 * t + 48 * s + 48) if t else names(0, s)
 
     def nxt(t):
         return ("NL", 96 * t, 96 * t + 96)
@@ -513,206 +523,80 @@ def rank_program(g, core, T, topo):
     def CC(t):
         return U("C", t - 1)
 
+    def YY(t):
+        return U("YW", 2 * t)
+
     def WW(t):
-        return ("YW", L2 * t + K, L2 * t + L2)
+        return U("YW", 2 * t + 1)
+
+    def MM(t):
+        return lane("Z", D0 + L3 * t, 1)
 
     def ones(out, pat, v, base, cm):
         select(out, cut(ZERO, (0, size(out)), 144), pat, A_.not_equal, v, base, cm)
 
-    dma("s", T.BNI[0:32, :], T.bn[:], [], [U("BNI")], nb(U("BNI")) / 2)
-    dma("a", T.ANI[:], T.an[:], [], [("ANI", 0, 192)], nb(("ANI", 0, 192)))
-    for out, src in ((TH, T.th), (WW(0), T.wt), (("YW", 0, K), T.yt), (VA, T.va)):
-        dma("s", ap(out), src[:], [], [out], nb(out))
-    iota(("RI", 0, 4), [[0, 4]], 0, 1, False)
-    iota(cs(0, 4), [[1, 4]], 0, 0)
-    iota(V2, ROWS, 0, -4)
-    iota(("KI", 0, K + LIFT), [[1, K + LIFT]], 0, 0)
-    memset(cs(59), float(LIFT))
-    memset(cs(60), -float(LIFT))
-    memset(ZERO, 0.0)
-    act(cs(64, 4), cs(0, 4), F_.Silu, float(K), cs(59))
-    calls[-1]["hold"] += once.pop("table")
-    ts(("RI", 0, 1), ("RI", 0, 1), 7, None, A_.bitwise_and)
-    ts(("RI", 1, 2), ("RI", 1, 2), 15, None, A_.bitwise_and)
-    ts(cs(12, 4), cs(0, 4), float(L2), float(FB(0) + LIFT), A_.mult, A_.add)
-    vcopy(cs(4, 2), ("RI", 0, 2))
-    ts(cs(16, 4), cs(0, 4), -float(W), float(QV(0) + LIFT + 2), A_.mult, A_.add)
+    small = {}
 
-    def e2(t):
-        ts(("E2", 144 * t, 144 * t + 144), V2, float(15000 - 4 * t), None, A_.is_equal)
-    ts(cs(6), cs(4), 0.5, None, A_.is_gt)
-    ts(cs(8, 4), cs(0, 4), cs(4), None, A_.subtract)
-    e2(0)
-    ts(cs(7), cs(4), 4.5, cs(6), A_.is_lt, A_.mult)
-    ts(cs(20, 4), cs(8, 4), -4.5, None, A_.is_lt)
-    e2(1)
-    ts(cs(24, 4), cs(8, 4), -2.0, cs(7), A_.is_equal, A_.mult)
-    ts(cs(28, 4), cs(8, 4), -1.5, cs(7), A_.is_gt, A_.mult)
-    e2(2)
-    tt(cs(20, 4), cs(20, 4), cs(24, 4), A_.add)
-    tt(cs(16, 4), cs(16, 4), cs(28, 4), A_.mult)
-    ts(cs(68, 4), cs(28, 4), 2.0, None, A_.mult)
-    ts(cs(52, 4), cs(28, 4), float(L2 - 2), None, A_.mult)
-    e2(3)
-    tt(cs(12, 4), cs(12, 4), cs(20, 4), A_.mult)
-    tt(cs(36, 4), cs(20, 4), cs(28, 4), A_.add)
-    for t in (1, 2, 3, 0):
-        vcopy(("LS", 96 * t, 96 * t + 48), ("ANI", 48 * t, 48 * t + 48))
-    tt(cs(40, 4), cs(12, 4), cs(16, 4), A_.add)
-    tt(cs(32, 4), cs(36, 4), cs(68, 4), A_.add)
-    ts(cs(48, 4), cs(36, 4), float(K), None, A_.mult)
-    tt(cs(52, 4), cs(52, 4), cs(40, 4), A_.add)
+    def soon(key, f, *args):
+        small.setdefault(key, []).append((f, args))
 
-    def share(s, visits):
-        send([(peer(t), [half(("LS", 96 * t, 96 * t + 96), s)], half(names(t), s), "l%d_%d" % (s, t), NS_ * (t - 1), NS_)
-              for t in visits])
-    iota(half(LOC, 3, 4), [[1, K]], 3 * K + LIFT, 0)
-    share(0, (1, 2, 3))
-    for u in (0, 1):
-        act(half(LOC, u, 4), KK, F_.Identity, 1.0, cs(64 + u))
-    ts(half(LOC, 2, 4), KK, float(2 * K + LIFT), None, A_.add)
-    tt(cs(44, 4), cs(48, 4), cs(52, 4), A_.add)
-    op("v", lambda: g.vector.tensor_scalar(T.BNF[0:32, 0:K], T.BNI[0:32, :], -float(OFF), None, A_.add),
-       [U("BNI")], [U("BNF")], K)
-    lined.update(p=0)
-    wb = {t: wrap([(U("BNF"), ("E2", 144 * t, 144 * t + 144), ALL)], 32, True, 512 * t) for t in (1, 0, 2, 3)}
-    lined.update(p=None)
-
-    def names_b(t):
-        ts(("LS", 96 * t + 48, 96 * t + 96), wb[t], float(OFF), None, A_.add)
-    ts(WW(0), WW(0), -0.125, None, A_.mult)
-    names_b(1)
-    share(1, (1,))
-    names_b(0)
-    vgat(zr(BS0), TH, half(names(0), 1))
-    names_b(2)
-    names_b(3)
-    ones(IB, [[1, 128]], 1.0, 0, -1)
-    send([(peer(1), [("YW", 0, L2)], ("YW", L2, 2 * L2), "yw1", 0, NE)])
-    share(1, (2, 3))
-    ones(E1(ROW_F[3]), ROWS, 1.0, ROW_F[3] - 15000, -1)
-    dma("g", ap(zr(0, W)), T.th[:], [], [zr(0, W)], nb(zr(0, W)))
-    begun = len(calls) - 1
-    if RELAY:
-        hand(0, [("YW", 0, L2)])
-    else:
-        send([(peer(2), [("YW", 0, L2)], ("YW", 2 * L2, 3 * L2), "yw2", 0, NE)])
-    send([(peer(3), [("YW", 0, L2)], ("YW", 3 * L2, 4 * L2), "yw3", 0, NE)])
-    lined.update(v=256, g=None)
-
-    def factors(t):
-        fill(lane("Z", D0 + L3 * t, 0), 0)
-        select(lane("Z", D0 + L3 * t, 2), WW(t), [[0, K]], A_.is_ge, 0.0, 0, 0)
-    for m, v in ((IDF, 1.0), (NIF, -1.0)):
-        ones(m, [[1, 128]], v, 0, -1)
-    for r in (ROW_FIN,) + ROW_N:
-        ones(E1(r), ROWS, 1.0, r - 15000, -1)
-    ones(("EH", 0, 144), ROWS, 1.0, -15000, -1)
-    for c in (144, 288):
-        ones(("EH", c, c + 144), ROWS, -1.0, -15000, -1)
-    select(("EH", 289, 417), ("EH", 289, 417), [[16, 8], [1000, 16]], A_.not_equal, 1.0, -15000, -1)
-    ts(("WO", 0, 48), ("KI", 0, 48), 16.0, cs(5), A_.mult, A_.add)
-    ts(cs(56), cs(5), 7.5, -1.0, A_.is_gt, A_.mult)
-    ts(("BNF", 7, 8), cs(60), 0.0, NONE, A_.mult, A_.add)
-    for t in (3, 2, 1):
-        factors(t)
-    for r in range(2, 8):
-        ones(EG(r), ROWS, 1.0, r - 15000, -1)
-        select(EG(r), EG(r), ROWS, A_.not_equal, 1.0, r + 8 - 15000, -1)
-    for m, b, v in ((MVN, BN_, int(BIG)), (MVC, BC_, -int(BIG))):
-        fill(m, v)
-        fill(b, -33 * v // 2)
-        select(m, m, [[-16, 8], [0, 16]], A_.is_ge, 0.0, 0, 1)
-        select(m, m, [[16, 8], [0, 16]], A_.is_ge, 0.0, 31, -1)
-        last16 = (m[0], m[1] + 112, m[2])
-        select(last16, last16, [[0, 16]], A_.is_ge, float(v), -16, 1)
-    fill(ONE, 1)
-    for c in calls[begun + 1:]:
-        if c["tok"] is None:
-            c["after"] = (begun,)
-
-    small = []
-
-    def soon(skip, f, *args):
-        small.append([skip, f, args])
-
-    def flush(need=None):
-        if need is None and small and small[0][0] <= 0:
-            need = small[0][2][0]
-            turn = 1
-        else:
-            turn = max([i + 1 for i, x in enumerate(small) if need and x[2][0][0] == need[0] and meet(x[2][0], need)] + [0])
-        lined["v"] = 0
-        for skip, f, args in small[:turn]:
+    def now(key, n=9):
+        for f, args in small.get(key, [])[:n]:
             f(*args)
-        lined["v"] = 256
-        del small[:turn]
-        for x in small:
-            x[0] -= 1
+        small[key] = small.get(key, [])[n:]
 
-    def index(out, src, base, skip=0):
-        soon(skip, ts, out, src, 0.25 - LIFT - base, None, A_.add)
+    def index(key, out, src, base):
+        soon(key, ts, out, src, 0.25 - LIFT - base, None, A_.add)
 
-    def index_n(t, out, src, skip=0):
+    def index_n(t, out, src):
+        key = "N%d" % t
         if t == 0:
             x = ("WT", 0, size(src))
-            soon(skip, ts, x, src, QV(1) + LIFT - 0.5, float(QA(1) - QV(1)), A_.is_gt, A_.mult)
-            soon(skip, tt, x, src, x, A_.add)
+            soon(key, ts, x, src, QV(1) + LIFT - 0.5, float(QA(1) - QV(1)), A_.is_gt, A_.mult)
+            soon(key, tt, x, src, x, A_.add)
             src = x
-        index(out, src, FB(t), skip)
+        index(key, out, src, FB(t))
 
     def ids(t, s):
-        act(half(IO, s) if t < 3 else (EX[0], XU)[s], KK, F_.Identity, cs(32 + 4 * s + t), cs(40 + 4 * s + t))
+        act(XU if s and t else half(IO, s), KK, F_.Identity, cs(32 + 4 * s + t), cs(40 + 4 * s + t))
 
-    def marks(t, s, n=2):
-        o, a, b = half(names(t), s, n), half(GB, s, n), half(IO, s, n)
-        if t in (0, 3):
-            ascat(LOC, o, b)
-        else:
-            op("v", lambda: g.vector.tensor_tensor(ind(LOC, o), ap(a), ap(b), A_.max), [o, a, b], [LOC], size(a) * SCA)
+    def marks_a(t, i):
+        o, a, b = half(names(t, 0), i), half(GB, i, 4), half(IO, i, 4)
+        op("v", lambda: g.vector.tensor_tensor(ind(LOC, o), ap(a), ap(b), A_.max), [o, a, b], [LOC], size(a) * SCA)
 
-    def lookup(t):
-        for s in (1, 0):
-            agat(half(GB, s), LOC, half(names(t), s))
-        index(fwd(t), wrap([(GB, E1(ROW_F[3]), ALL)]), 0, 4)
+    def lookup(t, s):
+        agat(half(GB, s), LOC, names(t, s))
+        index("F%d%d" % (t, s), fwd(t, s), wrap([(half(GB, s), E1(ROW_F[3]), ALL)], c0=None if s else EX[t % 2][1] - 48), 0)
     KEPT = {3: U("AB", 1), 2: U("AB", 6), 1: U("AB", 7), 0: U("AB", 5)}
 
-    def lookback(t, sides=(0, 1)):
+    def lookback(t, s):
         x = zr(QV(2) + L2 * (2 - t), L2) if t else ("AB", 4 * K, 6 * K)
-        for s in sides:
-            agat(half(x, s), LOC, half(names(t), s))
-        if 1 in sides:
-            lined.update(p=0)
-            index_n(t, nxt(t), wrap([(x, E1(ROW_N[t]), ALL)]), 0 if t else 1)
-            lined.update(p=None)
+        agat(half(x, s), LOC, names(t, s))
+        if s:
+            soon("W", lambda: index_n(t, nxt(t), wrap([(x, E1(ROW_N[t]), ALL)])))
 
     def keep(t):
         move("s", KEPT[t], zr(QV(2) + L2 * (2 - t) + K))
 
-    def gcopy(out, src):
-        select(out, src, [[0, size(out)]], A_.is_ge, 0.0, 0, 0)
-        calls[-1]["line"] = True
-
-    def split(t, src=None):
-        act(U("G", t), src or KEPT[t], F_.Copy, cs(56))
-        move("g", KEPT[t], U("G", t), True)
-        move("g", U("G", t), KEPT[t])
+    def split(t):
+        act(U("G", t), KEPT[t], F_.Copy, cs(56))
+        soon("G%d" % t, move, "g", KEPT[t], U("G", t), True)
+        soon("G%d" % t, move, "g", U("G", t), KEPT[t])
 
     def compose(r, t):
         agat(U("GT"), U("G", t), pl("PP", r, t))
         if t > 0:
-            index(half(fwd(t), 1), wrap([(U("GT"), EG(ROW_F[t]), ALL)]), 0)
-        if t < 3:
+            index("F%d1" % t, fwd(t, 1), wrap([(U("GT"), EG(ROW_F[t]), ALL)]), 0)
+        if t == 1:
+            soon("F11", lambda: index_n(t, half(nxt(t), 1), wrap([(U("GT"), EG(ROW_N[t]), ALL)])))
+        elif t < 3:
             index_n(t, half(nxt(t), 1), wrap([(U("GT"), EG(ROW_N[t]), ALL)]))
 
-    def fin(part):
+    def fin(part, i=0):
         w = ("PS", B7 + 320, B7 + 512)
         x, y, z = [("WT", 96 + 192 * i, 288 + 192 * i) for i in range(3)]
-        was = lined["v"]
-        lined.update(v=0)
         if part == 0:
-            for i in range(2):
-                wrap([(half(LOC, i), E1(ROW_FIN), ALL)], c0=B7 + 320 + 96 * i)
+            wrap([(half(LOC, i), E1(ROW_FIN), ALL)], 128, True, B7 + 320 + 96 * i)
         elif part == 1:
             ts(x, w, QV(1) + LIFT - 0.5, float(QA(1) - QV(1)), A_.is_gt, A_.mult)
             ts(y, w, QV(0) + LIFT - 0.5, float(QA(0) - QV(0) - QA(1) + QV(1)), A_.is_gt, A_.mult)
@@ -723,322 +607,495 @@ def rank_program(g, core, T, topo):
                 place(w, IDF, s, i == 0, i == 2)
         else:
             ts(("FIN", 0, 192), w, 0.25 - LIFT, None, A_.add)
-        lined.update(v=was)
 
-    def take_va(t, sides=(0, 1)):
-        for s in sides:
-            out, off = half(TMP if t < 3 else N3, s), half(names(t), s)
-            if (t, s) == (0, 1):
-                op("v", lambda: g.vector.tensor_scalar(ap(out), ind(VA, off), -1.0, None, A_.mult), [VA, off], [out], K * GAT)
-            else:
-                agat(out, VA, off, -1.0)
-        if t < 3 and 1 in sides:
-            dma("s", T.NVD[t], ap(TMP), [TMP], [("NVD", t, t + 1)], nb(TMP))
+    def va_part(i):
+        out, off = half(half(N3, 1), i), half(names(3, 1), i)
+        op("v", lambda: g.vector.tensor_scalar(ap(out), ind(VA, off), -1.0, None, A_.mult), [VA, off], [out], K * GAT)
 
-    def minus_va(t):
-        z = zr(FB(t), L2)
-        dma("g", ap(z), T.NVD[t], [("NVD", t, t + 1), z], [z], nb(z), True)
+    def take_va(t, s):
+        out = half(TMP if t < 3 else N3, s)
+        agat(out, VA, names(t, s), -1.0)
+        if t < 3:
+            dma("s", T.NVD[t, :, K * s:K * s + K], ap(out), [out], [("NVD", 2 * t + s, 2 * t + s + 1)], nb(out))
+
+    def minus_va(t, n=L2):
+        z = zr(FB(t), n)
+        dma("g", ap(z), T.NVD[t, :, 0:n], [("NVD", 2 * t, 2 * t + n // K), z], [z], nb(z), True)
 
     def negate(u):
         act(half(VA, u, 4), half(VA, u, 4), F_.Copy, -1.0)
 
+    def factors(t):
+        if t == 1:
+            fill(lane("Z", D0 + L3, 0), 0)
+        else:
+            move("s", zr(D0 + L3 * t, L3), zr(D0 + L3, L3))
+        soon("W%d" % t, gcopy, lane("Z", D0 + L3 * t, 2), WW(t))
+
+    dma("s", T.BNI[0:32, :], T.bn[:], [], [U("BNI")], nb(U("BNI")) / 2)
+    dma("a", T.ANI[:], T.an[:], [], [("ANI", 0, 192)], nb(("ANI", 0, 192)))
+    for out, src in ((TH, T.th), (WW(0), T.wt), (YY(0), T.yt)):
+        dma("s", ap(out), src[:], [], [out], nb(out))
+    iota(("RI", 0, 4), [[0, 4]], 0, 1, False)
+    iota(cs(0, 8), [[0, 2], [1, 4]], 0, 0)
+    iota(cs(8, 8), [[K, 2], [L2, 4]], FB(0) + LIFT, 0)
+    iota(cs(16, 8), [[L3 - 2, 2], [-W, 4]], QV(0) + LIFT + 2, 0)
+    iota(cs(24, 8), [[-2, 2], [0, 4]], 3, 0)
+    iota(V2, ROWS, 0, -4)
+    iota(("KI", 0, K + LIFT), [[1, K + LIFT]], 0, 0)
+    memset(cs(59), float(LIFT))
+    ts(("RI", 0, 1), ("RI", 0, 1), 7, None, A_.bitwise_and)
+    memset(cs(60), -float(LIFT))
+    vcopy(cs(61), ("RI", 0, 1))
+    memset(ZERO, 0.0)
+    act(cs(64, 4), cs(0, 4), F_.Silu, float(K), cs(59))
+    ts(cs(48, 8), cs(0, 8), cs(61), None, A_.subtract)
+    ts(("RI", 1, 2), ("RI", 1, 2), 15, None, A_.bitwise_and)
+    ts(cs(72, 8), cs(48, 8), -4.5, None, A_.is_lt)
+    ts(cs(80, 8), cs(48, 8), -1.0, None, A_.is_equal)
+    ts(cs(88, 8), cs(48, 8), -0.5, None, A_.is_gt)
+
+    def e2(t):
+        ts(("E2", 144 * t, 144 * t + 144), V2, float(15000 - 4 * t), None, A_.is_equal)
+    tt(cs(72, 8), cs(72, 8), cs(80, 8), A_.add)
+    tt(cs(16, 8), cs(16, 8), cs(88, 8), A_.mult)
+    tt(cs(24, 8), cs(24, 8), cs(88, 8), A_.mult)
+    tt(cs(8, 8), cs(8, 8), cs(72, 8), A_.mult)
+    e2(1)
+    tt(cs(32, 8), cs(24, 8), cs(72, 8), A_.add)
+    tt(cs(40, 8), cs(8, 8), cs(16, 8), A_.add)
+    e2(0)
+    e2(2)
+    vcopy(own(0, 0, 4), ("ANI", 0, 192))
+    op("v", lambda: g.vector.tensor_scalar(T.BNF[0:32, 0:K], T.BNI[0:32, :], -float(OFF), None, A_.add),
+       [U("BNI")], [U("BNF")], K)
+    e2(3)
+
+    def share(which):
+        n = NE // len(which)
+        send([(peer(t), [own(t, s)], names(t, s), "l%d_%d" % (s, t), n * i, n) for i, (t, s) in enumerate(which)])
+    DIAG = ("WT", 336, 464)
+    iota(DIAG, [[1, 128]], 0, -1)
+    share([(1, 0)])
+    move("s", half(LOC, 0, 4), ("KI", LIFT, LIFT + K))
+    dma("s", ap(VA), T.va[:], [], [VA], nb(VA))
+    for u in (1, 2):
+        act(half(LOC, u, 4), KK, F_.Identity, 1.0, cs(64 + u))
+    ids(0, 0)
+    for t in (1, 0, 2, 3):
+        wrap([(U("BNF"), ("E2", 144 * t, 144 * t + 144), ALL)], 32, True, 1024 + 48 * t if t > 1 else 48 * t)
+    ts(half(LOC, 3, 4), KK, float(3 * K + LIFT), None, A_.add)
+    for m, v in ((NIB, -1.0), (IDF, 1.0), (IB, 1.0)):
+        ts(m, DIAG, 0.0, v, A_.is_equal, A_.mult)
+    ts(own(0, 1, 2), ("PS", 0, 96), float(OFF), None, A_.add)
+    ts(WW(0), WW(0), -0.125, None, A_.mult)
+    vgat(zr(BS0), TH, names(0, 1))
+    ts(own(2, 1, 2), ("PS", 1024 + 96, 1024 + 192), float(OFF), None, A_.add)
+    ts(half(IO, 1), KK, cs(36), cs(44), A_.mult, A_.add)
+    share([(1, 1)])
+    send([(peer(1), [YY(0)], YY(1), "yw1", 0, NE)])
+    dma("g", ap(zr(0, W)), T.th[:], [], [zr(0, W)], nb(zr(0, W)))
+    ones(E1(ROW_F[3]), ROWS, 1.0, ROW_F[3] - 15000, -1)
+    send([(peer(1), [WW(0)], WW(1), "yw4", 0, NE)])
+    share([(2, 1), (2, 0), (3, 1), (3, 0)])
+    send([(peer(2), [("YW", 0, L2)], ("YW", 2 * L2, 3 * L2), "yw2", 0, NE)])
+    hand("yw5", [WW(0)])
+    send([(peer(3), [YY(0)], YY(3), "yw3", 0, NE)])
+    factors(1)
+    now("W1")
+    for r in ROW_N:
+        ones(E1(r), ROWS, 1.0, r - 15000, -1)
+    ones(("EH", 0, 144), ROWS, 1.0, -15000, -1)
+    for c in (144, 288):
+        ones(("EH", c, c + 144), ROWS, -1.0, -15000, -1)
+    select(("EH", 289, 417), ("EH", 289, 417), [[16, 8], [1000, 16]], A_.not_equal, 1.0, -15000, -1)
+    soon("K", vcopy, cs(62), ("RI", 1, 2))
+    soon("K", ts, ("BNF", 7, 8), cs(60), 0.0, NONE, A_.mult, A_.add)
+    soon("K", ts, ("WO", 0, 48), ("KI", 0, 48), 16.0, cs(62), A_.mult, A_.add)
+    soon("K", ts, cs(56), cs(62), 7.5, -1.0, A_.is_gt, A_.mult)
+    ones(NIF, [[1, 128]], -1.0, 0, -1)
+    for rows in ((ROW_F[1], ROW_N[1]), (ROW_F[2], ROW_N[2]), (ROW_F[3], ROW_N[0])):
+        for r in rows:
+            soon("EG", ones, EG(r), ROWS, 1.0, r - 15000, -1)
+        for r in rows:
+            soon("EG", select, EG(r), EG(r), ROWS, A_.not_equal, 1.0, r + 8 - 15000, -1)
+    soon("EG", ones, E1(ROW_FIN), ROWS, 1.0, ROW_FIN - 15000, -1)
+    fill(MVN, int(BIG))
+    fill(BN_, -33 * int(BIG) // 2)
+    select(MVN, MVN, [[-16, 8], [0, 16]], A_.is_ge, 0.0, 0, 1)
+    fill(ONE, 1)
+    select(MVN, MVN, [[16, 8], [0, 16]], A_.is_ge, 0.0, 31, -1)
+    last16 = (MVN[0], MVN[1] + 112, MVN[2])
+    select(last16, last16, [[0, 16]], A_.is_ge, BIG, -16, 1)
+
     def forward(r, t):
         last = r == RO - 1
-        Xy = EX[t % 2]
+        Xy, Xo = EX[t % 2], EX[1 - t % 2]
         zw = TH if r == 0 and t == 0 else ("Z", 0, FB(t))
-        fa, fb = half(fwd(t), 0), half(fwd(t), 1)
+        fa, fb = fwd(t, 0), fwd(t, 1)
         A, B = AA(t), BB(r, t)
         oa, ob = zr(FB(t)), zr(FB(t) + K)
-        P = lane("Z", D0 + L3 * t, 1) if t > 0 or last else U("D1B", 1)
-        place(Xy, IB, ("YW", L2 * t, L2 * t + K))
-        place(XW, IB, WW(t))
+        P = MM(t) if t > 0 or last else U("D1A", 2)
+        pp = pl("PP", r, 0) if r else None
+        early_w = r > 0 or t != 1
+
+        def gather(x, win, f):
+            for i in range(2):
+                agat(pc(x, i), win, pc(f, i))
+
+        def m_before():
+            if t > 1 or (t == 1 and last):
+                tt(MM(t - 1), Xo, MM(t - 1), A_.add)
         if r == 0 and t == 0:
-            ids(0, 0)
-            marks(0, 0)
-            agat(A, zw, fa)
-            ids(0, 1)
-            marks(0, 1)
-        elif t == 0:
-            pp = pl("PP", r, 0)
-            agat(B, zr(BS0), pp)
-        else:
-            if r == 0 and t < 3:
-                marks(t, 0)
-            if r == 0 and t == 1:
-                marks(t, 2, 4)
-            if r == 0 and t == 3:
-                tt(half(IO, 0), EX[0], half(GB, 0), A_.max)
-            flush(fwd(t))
-            for x, f in ((B, fb), (A, fa)):
-                for i in range(2):
-                    agat(half(x, i), zw, half(f, i))
-            if r == 0 and t == 1:
-                marks(t, 3, 4)
-            elif r == 0 and t == 3:
-                take_va(0, (1,))
-            elif t > 1 or last:
-                m = lane("Z", D0 + L3 * (t - 1), 1)
-                tt(m, EX[1 - t % 2], m, A_.add)
-            if r:
-                flush()
+            ascat(LOC, fa, half(IO, 0))
+        elif r == 0:
+            if t == 1:
+                take_va(0, 0)
+            ids(t, 1)
+            if t == 2:
+                va_part(0)
+            if t == 3:
+                now("F31")
+            marks_a(t, 0)
+            now("F%d1" % t)
+            marks_a(t, 1)
+            tt(half(IO, 1), XU, half(GB, 1), A_.max)
+            now("F%d0" % t)
+            if t == 2:
+                va_part(1)
+            if t == 3:
+                now("K")
+            gather(B, zw, fb)
+            if t != 2:
+                take_va(t - 1, 1)
+            gather(A, zw, fa)
+        elif t:
+            for i in range(3):
+                agat(half(B, i, 3), zw, half(fb, i, 3))
+            gather(A, zw, fa)
+            m_before()
+        for i in range(2):
+            place(pc(Xy, i), NIB, pc(YY(t), i), True, False)
+        if early_w:
+            place(XW, IB, WW(t))
         for i in range(2):
             if r > 0 and t == 0:
-                gtt(half(P, i), zr(BS0), half(pp, i), half(A, i), A_.mult)
+                gtt(pc(P, i), zr(BS0), pc(pp, i), pc(A, i), A_.mult)
+            elif r > 0 and i == 1:
+                for j in (1, 2):
+                    gtt(half(P, j, 3), zw, half(fa, j, 3), half(B, j, 3), A_.mult)
             else:
-                gtt(half(P, i), zw, half(fa, i), half(B, i), A_.mult)
-        if r == 0 and t == 2:
-            take_va(1)
-            marks(t, 1)
-        if r == 0 and t == 3:
-            tt(half(IO, 1), XU, half(GB, 1), A_.max)
-            marks(t, 0)
-            marks(t, 1)
-        for i in range(2):
-            tt(half(Xy, i), half(P, i), half(Xy, i), A_.subtract)
-        if r == 0 and t < 3:
-            lookup(t + 1)
-            if t < 2:
+                gtt(pc(P, i), zw, pc(fa, i), pc(B, i), A_.mult)
+            place(pc(Xy, i), IDF, pc(P, i), False, True)
+            if i == 0 and not early_w:
+                place(XW, IB, WW(t))
+        if r and t:
+            now("N%d" % (t % 3), 1)
+        if r == 0 and t == 0:
+            vgat(A, zw, fa)
+            ascat(LOC, fb, half(IO, 1))
+            ids(1, 0)
+            lookup(1, 1)
+            lookup(1, 0)
+        elif r == 0:
+            m_before()
+            if t == 1:
+                now("K", 1)
+                factors(2)
+                factors(3)
+                now("W2")
+            if t == 3:
+                move("g", zr(FB(2), L2), TMP, True)
+                now("W3")
+                minus_va(0)
+            ascat(LOC, names(t, 1), half(IO, 1))
+            if t < 3:
+                lookup(t + 1, 1)
+                if t == 2:
+                    move("s", KEPT[3], half(GB, 1))
+                lookup(t + 1, 0)
                 ids(t + 1, 0)
-                ids(t + 1, 1)
-            else:
-                move("s", KEPT[3], half(GB, 1))
-                split(3, half(GB, 1))
-            take_va((3, 2, 0)[t], (0, 1) if t < 2 else (0,))
-        if r > 0 and t == 0:
-            ascat(U("D1B"), pp, ("KI", LIFT, LIFT + K))
-            act(ST, U("D1B"), F_.Identity, 1.0, cs(60))
-            soon(0, ts, pl("PI", r, 0), wrap([(ST, ("EH", 0, 144), ALL)]), 3.0, 2.25, A_.mult, A_.add)
+                take_va(4 - t, 0)
+        elif t == 0:
+            ascat(U("D1A"), pp, ("KI", LIFT, LIFT + K))
+            vgat(pc(B, 0), zr(BS0), pc(pp, 0))
+            agat(pc(B, 1), zr(BS0), pc(pp, 1))
+            act(ST, U("D1A"), F_.Identity, 1.0, cs(60))
+            soon("PI", ts, pl("PI", r, 0), wrap([(ST, ("EH", 0, 144), ALL)], c0=EX[1][1] - 48), 3.0, 2.25, A_.mult, A_.add)
         if r > 0 and t < 3:
             compose(r, t + 1)
             if t == 1:
                 agat(NV3, half(N3, 1), pl("PP", r, 3))
             if t == 2:
-                compose(r, 0)
-            if t > 0 and r == 1:
-                negate(t)
-        if t == 3:
+                soon("F31", compose, r, 0)
+        if r > 0 and t == 3:
             for u in (2, 1, 0):
                 minus_va(u)
             if last:
                 for i in range(2):
-                    move("g", half(zr(0, W), i), half(VA, i), True)
-            if not last:
-                act(EX[0], A, F_.Square)
-            if r == 1:
-                negate(0)
-                negate(3)
-        for i in range(2):
-            tt(half(EA(t), i), half(Xy, i), half(A, i), A_.mult)
-        if last and t == 3:
-            da, db = lane("D1B", 0, 0), lane("D1B", 0, 2)
-            xa, xb = U("D1A", 0), U("D1A", 1)
-            lined.update(p=0)
-            for x, v, nv in ((XU, B, NV3), (EX[0], A, half(N3, 0))):
-                place(x, IB, nv, True, False)
-                place(x, IDF, v, False, True)
-            lined.update(p=None)
-            tt(EB(t), Xy, B, A_.mult)
-            tt(xb, EA(t), XW, A_.mult)
-            tt(xa, EB(t), XW, A_.mult)
-            tt(XU, XU, xb, A_.add)
-            act(XW, A, F_.Square)
-            tt(EX[0], EX[0], xa, A_.add)
-            tt(P, Xy, P, A_.add)
-            for i in range(2):
-                act(half(db, i), half(XU, i), F_.Copy)
-            copied = len(calls) - 1
-            tt(EB(t), EX[0], EB(t), A_.mult)
-            for i in range(2):
-                act(half(da, i), half(EX[0], i), F_.Copy)
-            act(EX[1], B, F_.Square)
-            tt(EA(t), XU, EA(t), A_.mult)
-            calls[-1]["after"] = (copied,)
-            return
-        tt(half(EB(t), 0), half(Xy, 0), half(B, 0), A_.mult)
-        tt(XU, EA(t), XW, A_.mult)
-        tt(half(EB(t), 1), half(Xy, 1), half(B, 1), A_.mult)
-        if r == 0 and t == 2:
-            tt(P, Xy, P, A_.add)
-            ids(3, 0)
+                    soon("TH", move, "g", half(zr(0, W), i), half(VA, i), True)
+        if r == 1 and t == 0:
+            now("G0", 1)
+
+        def eA(i):
+            tt(pc(EA(t), i), pc(Xy, i), pc(A, i), A_.mult)
+
+        def eB(i):
+            tt(pc(EB(t), i), pc(Xy, i), pc(B, i), A_.mult)
+
+        def xa(i):
+            tt(pc(XW, i), pc(EB(t), i), pc(XW, i), A_.mult)
         if t < 3:
-            tt(lane("SB", 0, 2) if r else ob, XU, B, A_.add)
-            if r and t == 0:
-                flush()
-                spread("pi", r)
+            bout = lane("SB", 0, 2) if r else ob
+            ua, ub = (pc(XU, 0), pc(XW, 1)), (pc(XW, 0), pc(XU, 1))
+
+            def xa(i):
+                tt(ua[i], pc(EB(t), i), pc(XW, i), A_.mult)
+
+            def xb(i):
+                tt(ub[i], pc(EA(t), i), pc(XW, i), A_.mult)
+
+            def na_(i):
+                tt(pc(oa, i), ua[i], pc(A, i), A_.add)
+
+            def nb_(i):
+                tt(pc(bout, i), ub[i], pc(B, i), A_.add)
+            for f, i in ((eB, 0), (eA, 0), (xa, 0), (xb, 0), (na_, 0), (eA, 1), (nb_, 0), (xb, 1), (eB, 1), (nb_, 1),
+                         (xa, 1)):
+                if r and t == 0 and (f, i) == (nb_, 1):
+                    now("PI")
+                    spread("pi", r)
+                    now("G0")
+                    now("EG")
+                f(i)
+            now("F%d1" % (t + 1) if r else "K", 2 if r else int(t < 2))
             if r:
                 agat(ob, ("SB", 0, L3), pl("PI", r, t))
-            elif t == 2:
-                ids(3, 1)
-            tt(XW, EB(t), XW, A_.mult)
-            if r:
-                flush()
-            tt(oa, XW, A, A_.add)
+            na_(1)
             return
-        da, db = lane("D1B", 0, 0), lane("D1B", 0, 2)
+        da, t2, db = [lane("D1", 0, k) for k in range(3)]
+        X = U("SB", 2)
+        nva, nvb = half(N3, 0), NV3 if r else half(N3, 1)
+
+        def xb(i):
+            tt(pc(X, i), pc(EA(t), i), pc(XW, i), A_.mult)
+            place(pc(Xo, i), IDF, pc(B, i), True, False)
+            place(pc(Xo, i), IDF, pc(X, i), False, False)
+            place(pc(Xo, i), IB, pc(nvb, i), False, True)
+
+        def na_(i):
+            tt(pc(XW, i), pc(XW, i), pc(A, i), A_.add)
+
+        def va_(i):
+            tt(pc(XW, i), pc(XW, i), pc(nva, i), A_.add)
+
+        def m_(i):
+            tt(pc(P, i), pc(Xy, i), pc(P, i), A_.add)
+        act(AA3[1], pc(A, 1), F_.Square)
+        for f, i in ((eA, 0), (eB, 0), (xb, 0), (xa, 0), (m_, 0), (na_, 0), (eA, 1), (va_, 0), (xb, 1), (eB, 1)):
+            f(i)
+        act(pc(db, 0), pc(Xo, 0), F_.Copy)
+        act(AA3[0], pc(A, 0), F_.Square)
+        act(pc(da, 0), pc(XW, 0), F_.Copy)
         if r == 0:
-            lookback(2, (0,))
-        tt(XU, XU, B, A_.add)
-        tt(XW, EB(t), XW, A_.mult)
-        tt(XU, XU, NV3 if r else half(N3, 1), A_.add)
-        tt(XW, XW, A, A_.add)
-        tt(P, Xy, P, A_.add)
-        tt(XW, XW, half(N3, 0), A_.add)
-        for x, y in ((db, XU), (da, XW)):
-            for i in range(2):
-                act(half(x, i), half(y, i), F_.Copy)
-            if r == 0 and y == XU:
-                lookback(2, (1,))
+            lookback(2, 0)
+        m_(1)
+        xa(1)
+        tt(pc(t2, 0), AA3[0], pc(db, 0), A_.mult)
+        na_(1)
+        tt(pc(EA(t), 0), pc(Xo, 0), pc(EA(t), 0), A_.mult)
+        va_(1)
+        act(pc(db, 1), pc(Xo, 1), F_.Copy)
+        if r == 0:
+            lookback(2, 1)
+            now("W")
+        act(pc(da, 1), pc(XW, 1), F_.Copy)
         act(EX[1], B, F_.Square)
-        tt(EA(t), XU, EA(t), A_.mult)
+        if r == 0:
+            keep(2)
 
     def backward(r, t):
         last = r == RO - 1
         more = t > 1 or (t == 1 and last)
-        da, t2, db = [lane("D1B", 0, k) for k in range(3)]
+        da, t2, db = [lane("D1", 0, k) for k in range(3)]
         d0 = zr(D0 + L3 * t, L3)
-        D1A, D1B, SB = ("D1A", 0, L3), ("D1B", 0, L3), ("SB", 0, L3)
+        D1, D1A, SB = ("D1", 0, L3), ("D1A", 0, L3), ("SB", 0, L3)
         zw = ("Z", FB(t), QV(2) if t == 2 else QV(1))
         na, nb_ = half(nxt(t), 0), half(nxt(t), 1)
         Xe = ("PS", 3072, 3072 + K) if last and t == 0 else XU
-        Xa = XW if last and t == 3 else EX[0]
-        if t < 3 and r:
-            flush()
+        Xa = XU if t == 3 else EX[0]
+        Xb = XW if t == 1 and not last else EX[1]
         if not last and t == 0:
-            for i in range(2):
-                agat(half(U("D1B"), i), zw, half(nb_, i))
+            for i in (1, 0):
+                agat(pc(U("D1A"), i), zw, pc(nb_, i))
             if r == 0:
                 split(0)
             else:
                 agat(PN, KK, pl("PP", r, 0))
+                for u in range(4):
+                    negate(u)
             gtt(EB(0), zw, na, EB(0), A_.mult)
-            for i in range(2):
-                tt(half(XU, i), half(XU, i), half(U("D1B"), i), A_.mult)
-            for i in range(2):
-                tt(half(U("D1B", 1), i), half(XU, i), half(EB(0), i), A_.add)
+            for i in (1, 0):
+                tt(pc(XU, i), pc(XU, i), pc(U("D1A"), i), A_.mult)
+            for i in (1, 0):
+                tt(pc(U("D1A", 1), i), pc(XU, i), pc(EB(0), i), A_.add)
             return
-        if t == 3 and r:
-            fin(2 * r - 2)
 
         def side_b(i):
-            scan(half(SB, i), half(d0, i), half(D1B, i), 0.0, A_.mult, A_.add)
+            scan(pc(SB, i), pc(d0, i), pc(D1, i), 0.0, A_.mult, A_.add)
 
-        def home(i, n, sem):
-            send([(peer(-t), [half(EB(t), i, n), half(EA(t), i, n)], half(CC(t), i, n), sem, 0, NE)])
-        if t == 3:
-            tt(half(t2, 0), half(Xa, 0), half(db, 0), A_.mult)
-            if not last:
-                tt(EB(t), XW, EB(t), A_.mult)
-        else:
-            for x, f in ((db, nb_), (da, na)):
-                for i in range(2):
-                    agat(half(x, i), zw, half(f, i))
-        if t == 1:
-            for i in range(2):
-                gtt(half(EB(t), i), zw, half(na, i), half(EB(t), i), A_.mult)
-            tt(half(EA(t), 0), half(Xe, 0), half(db, 0), A_.mult)
-            home(0, 2, "c%d_0" % r)
-            tt(half(t2, 0), half(EX[0], 0), half(db, 0), A_.mult)
-            tt(half(EA(t), 1), half(Xe, 1), half(db, 1), A_.mult)
-            home(1, 2, "c%d_1" % r)
-            if last:
-                move("g", CC(3), CC(2), True)
-                calls[-1]["after"] = (len(calls) - 3,)
-        elif t < 3:
-            gtt(EB(t), zw, na, EB(t), A_.mult)
-            tt(half(t2, 0), half(EX[0], 0), half(db, 0), A_.mult)
-            tt(EA(t), Xe, db, A_.mult)
-        if t == 3 and RELAY:
-            hand(1 + r, [EB(t), EA(t)])
-        elif t > 1:
-            home(0, 1, "c%d_%d" % (r, t))
-        lined.update(p=0)
-        if t == 0:
-            for i, s in enumerate((CC(3), CC(1), EB(0), EA(0))):
-                place(XW, IDF, s, i == 0, i == 3)
-        else:
+        def home(i, sem, via=None):
+            srcs = [pc(EB(t), i), pc(EA(t), i)]
+            send([(peer(-t), srcs, pc(CC(t), i), sem, 0, NE)])
+
+        def second(k):
+            x = (db, da)[k]
+            if LANES.get((r, t), "ga")[k] == "g":
+                gcopy(lane("D1A", 0, 2 * k), x)
+            else:
+                act(lane("D1A", 0, 2 * k), x, F_.Copy)
+
+        def ahead():
+            if t == 0:
+                for s in (EB(0), EA(0), CC(1)):
+                    place(XW, IDF, s, False, s == CC(1))
+                return
             x = ("PS", 3072, 3072 + K) if last and t == 1 else XU
-            for c in ((0, 256), (256, K)):
-                place(cut(x, c), IDF, cut(EA(t - 1), c))
-            if r == 0 and t == 1:
-                place(EX[1], NIF, CC(3), True, False)
-        lined.update(p=None)
-        if r == 0 and t == 2:
-            lookback(0)
-        act(lane("D1A", 0, 0), db, F_.Copy)
-        if (r, t) in GDUP:
-            gcopy(lane("D1A", 0, 2), da)
+            for i in range(2):
+                place(pc(x, i), IDF, pc(EA(t - 1), i))
+            if t == 1 and last:
+                for c in (3, 2):
+                    place(XW, IDF, CC(c), c == 3, False)
+        if t == 3:
+            side_b(0)
+            now("N0", 1)
+            tt(pc(EA(t), 1), pc(EX[0], 1), pc(EA(t), 1), A_.mult)
+            tt(EB(t), XW, EB(t), A_.mult)
+            tt(pc(t2, 1), AA3[1], pc(db, 1), A_.mult)
+            second(0)
+            second(1)
+            hand("c%d_3" % r, [EB(t), EA(t)])
+            ahead()
+            if r == 1:
+                fin(0, 0)
         else:
-            act(lane("D1A", 0, 2), da, F_.Copy)
-        side_b(0)
+            turn = (1, 0) if t == 1 else (0, 1)
+            for i in turn:
+                agat(pc(db, i), zw, pc(nb_, i))
+            agat(da, zw, na)
+            if t != 1:
+                second(0)
+            if t == 1:
+                for i in turn:
+                    gtt(pc(EB(t), i), zw, pc(na, i), pc(EB(t), i), A_.mult)
+                for i in turn:
+                    tt(pc(EA(t), i), pc(Xe, i), pc(db, i), A_.mult)
+                    home(i, "c%d_%d" % (r, i))
+                second(0)
+                tt(t2, Xa, db, A_.mult)
+            else:
+                gtt(EB(t), zw, na, EB(t), A_.mult)
+                for i in turn:
+                    tt(pc(t2, i), pc(Xa, i), pc(db, i), A_.mult)
+                    tt(pc(EA(t), i), pc(Xe, i), pc(db, i), A_.mult)
+            if t == 2:
+                home(1, "c%d_2" % r)
+                hand("c%d_4" % r, [pc(EB(t), 0), pc(EA(t), 0)])
+            second(1)
+            if t == 1 and not last:
+                place(pc(EX[1], 1), NIF, pc(CC(2), 1), True, False)
+            else:
+                ahead()
         if r == 0 and t == 1:
-            flush()
-        tt(half(t2, 1), half(Xa, 1), half(db, 1), A_.mult)
-        tt(lane("D1A", 0, 1), XW if t == 1 and not last else EX[1], da, A_.mult)
-        if r == 0:
-            flush()
+            now("N0", 1)
+        tt(lane("D1A", 0, 1), Xb, da, A_.mult)
+        if t == 1 and not last:
+            ahead()
+            for i in (1, 0):
+                place(pc(EX[1], i), NIF, pc(CC(3), i), i == 0, False)
         if last and t == 3:
-            fin(3)
-        if r == 0 and t == 1:
-            split(1)
+            fin(2)
+        if r == 0 and t == 2:
+            now("N1")
+            lookback(0, 0)
+            lookback(0, 1)
+            now("W")
         if more:
             act(EX[0], AA(t - 1), F_.Square)
-        side_b(1)
-        if r == 0 and t == 1:
-            flush()
-        if r == 0 and GQB:
-            gcopy(zr(QB(t)), lane("SB", 0, 2))
-        elif r == 0:
-            act(zr(QB(t)), lane("SB", 0, 2), F_.Copy)
-        else:
-            agat(zr(QB(t)), SB, pl("PI", r, t))
+        if r == 0 and t == 3:
+            lookback(1, 0)
+            lookback(1, 1)
+            keep(1)
+            take_va(1, 0)
+            take_va(1, 1)
         if more:
             act(XW if t == 2 and not last else EX[1], BB(r, t - 1), F_.Square)
-        if r == 0 and t == 3:
-            lookback(1)
-            keep(2)
-            keep(1)
         if r == 0 and t == 1:
-            split(2)
-        if t == 2 and r == 1:
-            lined.update(p=0)
-            place(EX[1], NIF, CC(3), True, False)
-            lined.update(p=None)
+            act(("MB", MVC[1], BC_[2]), ("MB", MVN[1], BN_[2]), F_.Copy, -1.0)
+            for u in (3, 1, 2):
+                split(u)
+            now("G3", 1)
+            now("N0", 1)
+        if r == 1 and t == 2:
+            fin(0, 1)
+        if t == 3:
+            side_b(1)
+        else:
+            scan(SB, d0, D1, 0.0, A_.mult, A_.add)
+        if r == 0:
+            gcopy(zr(QB(t)), lane("SB", 0, 2))
+            if t == 1:
+                for key, n in (("G1", 1), ("G2", 1), ("G3", 1), ("EG", 4), ("G1", 1), ("G2", 1)):
+                    now(key, n)
+                now("N0")
+            if t == 3:
+                move("g", zr(FB(1), L2), TMP, True)
+        else:
+            agat(zr(QB(t)), SB, pl("PI", r, t))
         if r == 1 and t == 1:
             factors(0)
-        scan(zr(QA(t), L3), d0, D1A, 0.0, A_.mult, A_.add)
+            now("W0")
+        if last and t == 2:
+            now("TH")
+        if r == 0 and t == 3:
+            for i in (1, 0):
+                scan(pc(zr(QA(t), L3), i), pc(d0, i), pc(D1A, i), 0.0, A_.mult, A_.add)
+                now("N%d" % (t - 1))
+                now("W")
+        else:
+            scan(zr(QA(t), L3), d0, D1A, 0.0, A_.mult, A_.add)
+        if r and t == 3:
+            now("N0", 1)
+        if last and t == 2:
+            fin(3)
 
     def vote(r):
         old = KK if r == 0 else PN
-        p0, lo = U("D1B", 1), U("D1B", 2)
+        p0, lo = U("D1A", 1), U("D1A", 2)
 
         def bias(x, b):
             place(x, b, cut(ONE, (0, size(x)), 512), True, False, 1)
-        lined.update(p=0)
-        for x, b in ((half(EX[0], 0), BN_), (half(EX[0], 1), BN_), (cut(XW, (0, 512)), BC_)):
+        for x, b in ((pc(EX[0], 0), BN_), (pc(EX[0], 1), BN_), (cut(XW, (0, 512)), BC_)):
             bias(x, b)
-        for c in (2, 1):
-            for i in range(2):
-                place(half(EX[1], i), NIF, half(CC(c), i), False, c == 1)
+        for c, i in ((2, 0), (1, 1), (1, 0)):
+            place(pc(EX[1], i), NIF, pc(CC(c), i), False, c == 1)
         bias(cut(XW, (512, K)), BC_)
         place(("PS", 3072, 3072 + 48), IDF, ("WO", 0, 48), True, False)
-        for i in range(2):
-            tt(half(POS, i), half(p0, i), half(EX[1], i), A_.is_lt)
-            place(half(EX[0], i), MVN, half(POS, i), False, True)
+        for i in (1, 0):
+            tt(pc(POS, i), pc(p0, i), pc(EX[1], i), A_.is_lt)
+            place(pc(EX[0], i), MVN, pc(POS, i), False, True)
         place(XW, MVC, POS, False, True)
-        lined.update(p=None)
-        for i in range(2):
-            tt(half(lo, i), half(EX[0], i), half(old, i), A_.min)
+        for i in (1, 0):
+            tt(pc(lo, i), pc(EX[0], i), pc(old, i), A_.min)
         scan(ST, XW, lo, NONE, A_.min, A_.max)
         wp = wrap([(ST, ("EH", 288, 432), range(15)), (ST, ("EH", 144, 288), [15]),
                    (("BNF", 7, 7 + K), ("EH", 0, 144), [0])], 128, False, 3072)
-        lined.update(v=0)
         vcopy(cs(57), ("BNF", 7 + K, 8 + K))
         if r == 1:
             fin(1)
         ts(("WT", 672, 720), wp, -BIG, cs(57), A_.mult, A_.min)
         tt(("WO", 0, 48), wp, ("WT", 672, 720), A_.max)
         vcopy(pl("PP", r + 1, 0), ("WO", 0, 48))
-        lined.update(v=256)
         spread("pp", r + 1)
 
     for r in range(RO):
@@ -1050,13 +1107,14 @@ def rank_program(g, core, T, topo):
             vote(r)
 
     zw = ("Z", 0, Q0B + K)
-    act(CC(2), XW, F_.Copy, -0.125)
-    dma("s", T.yh[:], ap(CC(2)), [CC(2)], [], nb(CC(2)))
     c = 0
-    for n in LAST:
-        for gat in (vgat, agat):
-            o = ("AB", c, c + n)
-            gat(o, zw, ("FIN", c // 16, (c + n) // 16))
-            dma("s", T.yd[:, c:c + n], ap(o), [o], [], nb(o))
-            c += n
+    for q, n in LAST:
+        if n == 0:
+            act(CC(2), XW, F_.Copy, -0.125)
+            dma("s", T.yh[:], ap(CC(2)), [CC(2)], [], nb(CC(2)))
+            continue
+        o = ("AB", c, c + n)
+        (vgat if q == "v" else agat)(o, zw, ("FIN", c // 16, (c + n) // 16))
+        dma("s", T.yd[:, c:c + n], ap(o), [o], [], nb(o))
+        c += n
     issue()

from concourse.bass import DstId, RemoteDMATransfer
from concourse.mybir import AluOpType, ActivationFunctionType

W, K, RO = 3072, 768, 3
L2, L3 = 2 * K, 3 * K
IDX = "float16"
OFF = 1536
BIG = 4096.0
LIFT = 64
NONE = -1024.0
BS0 = W
Q0B = W + K + 3 * L2 + 2 * W
D0 = Q0B + K
PC = ((0, 256), (256, K))
PASSES = 2
LANES = {(0, 3): "gg", (0, 1): "aa"}
LAST = (("a", 0), ("v", 256), ("a", 256), ("v", 512), ("a", 512), ("v", 512), ("a", 448), ("v", 320), ("a", 256))
LOG = []
ORDER = []

CYC, PCYC, GAT, SCA, SIG = 0.83e-3, 0.5e-3, 1.5, 3.0, 0.12
START = {"v": 0.06, "a": 0.08, "p": 0.05, "g": 0.05}
ISSUE, LAT, RATE = {"g": 1.0, "s": 0.1, "a": 0.1, "r": 0.6}, {"d": 2.0, "r": 2.5}, {"d": 550e3, "r": 10e3}
ONCE = {"remote": 3.6, "table": 1.3, "dma": 1.0}


def FB(t):
    return W + K + L2 * t


def QV(t):
    return FB(3) + W * (3 - t)


def QA(t):
    return {3: QV(3), 2: QV(2), 1: FB(1), 0: BS0}[t]


def QB(t):
    return Q0B if t == 0 else QA(t) + L3


ROW_FIN, ROW_N, ROW_F = 0, (1, 2, 3), (None, 5, 6, 7)

SCRATCH = {
    "PS": ("psum", [128, 4096], "float32"),
    "Z": ("sbuf", [128, D0 + 4 * L3], "float32"),
    "AB": ("sbuf", [128, 4 * L2], "float32"),
    "EE": ("sbuf", [128, 4 * L2], "float32"),
    "D1A": ("sbuf", [128, L3], "float32"),
    "D1": ("sbuf", [128, L3], "float32"),
    "SB": ("sbuf", [128, L3], "float32"),
    "C": ("sbuf", [128, L3], "float32"),
    "KI": ("sbuf", [128, K + LIFT], "float32"),
    "YW": ("sbuf", [128, 4 * L2], "bfloat16"),
    "NVB": ("sbuf", [128, 2 * W], "bfloat16"),
    "NVD": ("dram", [3, 128, L2], "bfloat16"),
    "G": ("sbuf", [128, 4 * K], "bfloat16"),
    "GT": ("sbuf", [128, K], "bfloat16"),
    "BNI": ("sbuf", [128, K], "int32"),
    "BNF": ("sbuf", [128, K + 8], IDX),
    "ANI": ("sbuf", [128, 192], "int32"),
    "LS": ("sbuf", [128, 2 * 192], "uint16"),
    "LV": ("sbuf", [128, 2 * 192], "uint16"),
    "FL": ("sbuf", [128, 4 * 96], "uint16"),
    "NL": ("sbuf", [128, 3 * 96], "uint16"),
    "FIN": ("sbuf", [128, 192], "uint16"),
    "PP": ("sbuf", [128, 8 * 48], "uint16"),
    "PI": ("sbuf", [128, 8 * 48], "uint16"),
    "E1": ("sbuf", [128, 5 * 144], "float32"),
    "E2": ("sbuf", [128, 4 * 144], IDX),
    "EH": ("sbuf", [128, 3 * 144], IDX),
    "EG": ("sbuf", [128, 6 * 144], "bfloat16"),
    "MB": ("sbuf", [128, 10 * 128], "bfloat16"),
    "MF": ("sbuf", [128, 2 * 128], "float32"),
    "WO": ("sbuf", [128, 48], "float32"),
    "WT": ("sbuf", [128, 720], "float32"),
    "RI": ("sbuf", [128, 4], "int32"),
    "CS": ("sbuf", [128, 96], "float32"),
}
BYTES = {"float32": 4, "int32": 4, "bfloat16": 2, "float16": 2, "uint16": 2}
NPOOL = 95
RELAYED = [(("YW", 0, K), 3, ("YW", 7 * K, 8 * K), "yw5")]
for _r in range(RO):
    RELAYED += [(("Z", L2 * _r, L2 * _r + K), -3, ("C", 2 * K, 3 * K), "c%d_3" % _r),
                (("Z", L2 * _r + K, L2 * _r + K + 256), -2, ("C", K, K + 256), "c%d_4" % _r)]
ARR = (["yw1", "yw2", "yw3", "yw4", "yw5"] + ["l%d_%d" % (s, t) for s in (0, 1) for t in (1, 2, 3)]
       + ["c%d_%d" % (r, t) for r in range(RO) for t in range(5)]
       + ["pp%d_%d" % (r, t) for r in (1, 2) for t in (1, 2, 3)]
       + ["pi%d_%d" % (r, t) for r in (1, 2) for t in (1, 2, 3)])
SEMAPHORES = (["qv", "qa", "qp", "qg"] + ARR + ["s%d" % i for i in range(NPOOL)]
              + ["h%d" % i for i in range(len(RELAYED))])


def step(r):
    return r[3] if len(r) > 3 else 1


def size(r):
    return len(range(r[1], r[2], step(r)))


def meet(x, y):
    return x[1] < y[2] and y[1] < x[2] and (step(x) != step(y) or (x[1] - y[1]) % step(x) == 0)


def covers(x, y):
    return x[1] <= y[1] and y[2] <= x[2] and (step(x) == 1 or (step(y) == step(x) and (x[1] - y[1]) % step(x) == 0))


def banks_of(regs):
    return {b for r in regs if r[0] == "PS" for b in range(r[1] // 512, (r[2] - 1) // 512 + 1)}


def issue_order(calls):
    n = len(calls)
    before, seen = [], {}
    for i, c in enumerate(calls):
        p = set(c["after"])
        for regs, isw in ((c["reads"], False), (c["writes"], True)):
            for r in regs:
                p.update(j for (x, j, w) in seen.get(r[0], []) if (w or isw) and meet(x, r))
        for r in c["writes"]:
            seen[r[0]] = [x for x in seen.get(r[0], []) if not covers(r, x[0])] + [(r, i, True)]
        for r in c["reads"]:
            seen.setdefault(r[0], []).append((r, i, False))
        p.discard(i)
        before.append(p)
    data = [set(p) for p in before]
    for q in "vagps":
        line = [i for i, c in enumerate(calls) if c["line"] and c["q"] == q]
        for i, j in zip(line, line[1:]):
            before[j].add(i)
    behind = [[] for _ in calls]
    for i in range(n):
        for j in before[i]:
            behind[j].append(i)
    span = [c["hold"] + c["lag"] + c["bytes"] for c in calls]
    uses = [([(c["q"], 0.0, c["hold"])] if c["q"] != "x" else [])
            + ([(c["way"], c["hold"], c["bytes"])] if c["bytes"] else [])
            + [(b, 0.0, c["hold"] + (SIG if c["q"] != "v" else 0.0)) for b in banks_of(c["reads"] + c["writes"])]
            for c in calls]

    def gap(i, j, back):
        a, b = (i, j) if back else (j, i)
        if a not in data[b] or (a in calls[b]["after"] and calls[b]["q"] != "x"):
            return span[j] + (calls[a]["hold"] - span[a])
        return span[j] + (0.0 if calls[i]["q"] + calls[j]["q"] == "pp" else SIG)

    def lay(order, first, back):
        busy, start = {}, [0.0] * n
        for i in order:
            s = max([start[j] + gap(i, j, back) for j in first[i]] + [0.0])
            use = [(k, span[i] - a - d if back else a, d) for k, a, d in uses[i]]
            moved = True
            while moved:
                moved = False
                for k, a, d in use:
                    for x, y in busy.get(k, ()):
                        if x < s + a + d - 1e-9 and s + a < y - 1e-9:
                            s, moved = y - a, True
            for k, a, d in use:
                busy.setdefault(k, []).append((s + a, s + a + d))
                busy[k].sort()
            start[i] = s
        return start

    def ranked(key):
        done, out = set(), []

        def put(i):
            if i not in done:
                done.add(i)
                for j in sorted(before[i], key=key):
                    put(j)
                out.append(i)
        for i in sorted(range(n), key=key):
            put(i)
        return out
    tail = [0.0] * n
    for i in reversed(range(n)):
        tail[i] = max([tail[j] + gap(j, i, False) for j in behind[i]] + [span[i]])
    order, kept = ranked(lambda i: (-tail[i], i)), None
    for _ in range(PASSES):
        start = lay(order, before, False)
        t = max(start[i] + span[i] for i in range(n))
        LOG.append(t)
        if not kept or t < kept[0]:
            kept = (t, ranked(lambda i: (start[i], i)))
        late = lay(ranked(lambda i: (start[i] + span[i], i))[::-1], behind, True)
        order = ranked(lambda i: (-late[i] - span[i], i))
    return kept[1]


def helper_of(c, T, topo):
    return [h for h in topo.cores_of(c) if topo.die(h) != topo.die(c) and h not in T.cores
            and all(topo.may_write(h, d) for d in T.cores)][0]


def relay(g, core, T, topo, rank):
    cores = list(T.cores)
    total = 0
    for i, (land, d, there, sem) in enumerate(RELAYED):
        to = cores[(rank + d) % len(cores)]
        rid, pid, _ = topo.addr(to)
        g.wait_ge(T.sem["h%d" % i], len(topo.engines(cores[rank], core)) - len(topo.engines(core, to)))
        g.remote_dma(T[there[0]][:, there[1]:there[2]], T[land[0]][:, land[1]:land[2]], T.sem[sem], T.sem.s0, pid, rid,
                     topo.mask(core, to))
        total += len(topo.engines(core, to))
    g.wait_ge(T.sem.s0, total)


def rank_program(g, core, T, topo):
    rank = T.rank_of(core)
    cores = list(T.cores)
    if rank is None:
        for r, c in enumerate(cores):
            if helper_of(c, T, topo) == core:
                relay(g, core, T, topo, r)
        return
    N = len(cores)
    A_ = AluOpType
    F_ = ActivationFunctionType
    Q = {"g": g, "v": g.vector, "a": g.scalar, "p": g.tensor, "s": g.sync}
    calls = []
    pool = [0]
    once = dict(ONCE)
    lined = {q: True for q in Q}

    def newsem():
        pool[0] += 1
        return "s%d" % (pool[0] - 1)

    def call(q, fn, tok, reads, writes, hold, lag=0.0, nbytes=0.0, way=None, after=()):
        calls.append(dict(q=q, fn=fn, tok=tok, reads=list(reads), writes=list(writes), hold=hold, lag=lag, bytes=nbytes,
                          way=way, after=after, line=lined.get(q, False)))

    def op(q, fn, reads, writes, cycles):
        call(q, fn, None, reads, writes, START[q] + cycles * (PCYC if q == "p" else CYC))

    def free(f, *args):
        was = dict(lined)
        lined.update(v=False, a=False, g=False, p=False)
        out = f(*args)
        lined.update(was)
        return out

    def dma(q, out, in_, reads, writes, nbytes, add=False):
        s = newsem()

        def fn():
            ins = Q[q].dma_start(out, in_, accum_op=A_.add) if add else Q[q].dma_start(out, in_)
            ins.then_inc(T.sem[s], 16)
        call(q, fn, (s, 16, "d"), reads, writes, ISSUE[q] + (once.pop("dma", 0.0) if q == "g" else 0.0), LAT["d"],
             nbytes * (2 if add else 1) / RATE["d"], "d")

    def ap(r):
        return T[r[0]][:, r[1]:r[2]:r[3]] if len(r) > 3 else T[r[0]][:, r[1]:r[2]]

    def nb(r):
        return 128 * size(r) * BYTES[SCRATCH[r[0]][2]]

    def ind(win, off):
        return ap(win).indirect(ap(off))

    def move(q, out, src, add=False):
        dma(q, ap(out), ap(src), [src, out] if add else [src], [out], nb(out), add)

    def peer(d):
        return cores[(rank + d) % N]

    def dst(c):
        a = topo.addr(c)
        return DstId(rid=a[0], pnc=a[1])

    def emask(c, i0, n):
        m = 0
        for e in topo.engines(core, c)[i0:i0 + n]:
            m |= 1 << e
        return m
    NE = len(topo.engines(core, peer(1)))
    SHARE = {1: (0, NE // 2), 2: (NE // 2, NE // 4), 3: (NE // 2 + NE // 4, NE // 4)}

    def transfer(c, mask, sem, srcs, land):
        if len(srcs) == 1:
            return RemoteDMATransfer(dst_ids=[dst(c)], dma_engine_mask=mask, remote_sem=T.sem[sem], src=ap(srcs[0]),
                                     dst=ap(land))
        return RemoteDMATransfer(dst_ids=[dst(c)], dma_engine_mask=mask, remote_sem=T.sem[sem],
                                 srcs=[ap(r) for r in srcs], dsts=[ap(land)], alu_op=1)

    def send(items):
        s = newsem()
        trs = [transfer(c, emask(c, i0, n), sem, srcs, land) for (c, srcs, land, sem, i0, n) in items]
        call("g", lambda: g.remote_dma_fused(trs, local_sem=T.sem[s]), (s, sum(it[5] for it in items), "d"),
             [r for it in items for r in it[1]], [], ISSUE["r"] + once.pop("remote", 0.0), LAT["r"] / 2,
             nb(items[0][2]) / items[0][5] / RATE["r"], "r")
        me = len(calls) - 1
        calls[me]["line"] = True
        for it in items:
            call("x", None, (it[3], it[5], "d"), [], [it[2]], 0.0, LAT["r"] / 2, after=(me,))

    def hand(sem, srcs):
        i = [x[3] for x in RELAYED].index(sem)
        land, d, there = RELAYED[i][:3]
        h = helper_of(core, T, topo)
        mask = topo.mask(core, h) & ~topo.mask(core, peer(1))
        ne = len(topo.engines(core, h)) - NE
        s = newsem()
        tr = transfer(h, mask, "h%d" % i, srcs, land)
        call("g", lambda: g.remote_dma_fused([tr], local_sem=T.sem[s]), (s, ne, "d"), srcs, [], ISSUE["r"], LAT["r"] / 2,
             nb(land) / ne / RATE["r"] / 2, "h")
        calls[-1]["line"] = True
        call("x", None, (sem, NE, "d"), [], [there], 0.0, 2 * LAT["r"] + nb(land) / NE / RATE["r"],
             after=(len(calls) - 1,))

    def spread(n, r):
        for share in (({1: (0, NE)}, {2: (0, NE // 2), 3: (NE // 2, NE // 2)}) if n == "pp" else (SHARE,)):
            send([(peer(u), [pl(n.upper(), r, 0)], pl(n.upper(), r, u), "%s%d_%d" % (n, r, u)) + e
                  for u, e in share.items()])

    def issue():
        count = {q: 0 for q in Q}
        waited, final, acc, banks = {}, {}, {}, {}
        for c in calls:
            q, tok = c["q"], c["tok"]
            want = {}
            for regs, isw in ((c["reads"], False), (c["writes"], True)):
                for r in regs:
                    for (x, k, w) in acc.get(r[0], []):
                        if (w or isw) and meet(x, r) and not (q == k[2] and tok is None and (q == "p" or not w)):
                            want[k[0]] = max(want.get(k[0], 0), k[1])
            bs = banks_of(c["reads"] + c["writes"])
            for b in bs:
                for e, k in banks.get(b, {}).items():
                    if e != q:
                        want[k[0]] = max(want.get(k[0], 0), k[1])
            if q != "x":
                for s, v in want.items():
                    if waited.get((q, s), 0) < v:
                        Q[q].wait_ge(T.sem[s], v)
                        waited[(q, s)] = v
                if tok is None:
                    count[q] += 1
                    tok = ("q" + q, count[q], q)
                    c["fn"]().then_inc(T.sem[tok[0]], 1)
                else:
                    c["fn"]()
            final[tok[0]] = max(final.get(tok[0], 0), tok[1])
            for r in c["writes"]:
                acc[r[0]] = [x for x in acc.get(r[0], []) if not covers(r, x[0])] + [(r, tok, True)]
            for r in c["reads"]:
                acc[r[0]] = [x for x in acc.get(r[0], [])
                             if not (not x[2] and x[1][0] == tok[0] and covers(r, x[0]))] + [(r, tok, False)]
            for b in bs:
                banks.setdefault(b, {})[q] = tok
        for s, v in final.items():
            if max([waited.get((q, s), 0) for q in Q]) < v:
                g.wait_ge(T.sem[s], v)

    def cols(*xs):
        return [x for x in xs if isinstance(x, tuple)]

    def val(x):
        return ap(x) if isinstance(x, tuple) else x

    def tt(out, a, b, o):
        op("v", lambda: g.vector.tensor_tensor(ap(out), ap(a), ap(b), o), [a, b], [out],
           size(out) * (1 if "PS" in (a[0], b[0]) else 2))

    def gtt(out, win, off, b, o):
        op("v", lambda: g.vector.tensor_tensor(ap(out), ind(win, off), ap(b), o), [win, off, b], [out], size(out) * GAT)

    def ts(out, a, s1, s2, o0, *o1):
        op("v", lambda: g.vector.tensor_scalar(ap(out), ap(a), val(s1), val(s2), o0, *o1), cols(a, s1, s2), [out],
           size(out))

    def vcopy(out, a):
        op("v", lambda: g.vector.tensor_copy(ap(out), ap(a)), [a], [out], size(out))

    def vgat(out, win, off):
        op("v", lambda: g.vector.tensor_copy(ap(out), ind(win, off)), [win, off], [out], size(out) * GAT)

    def memset(out, v):
        op("v", lambda: g.vector.memset(ap(out), v), [], [out], size(out))

    def agat(out, win, off, scale=1.0):
        op("a", lambda: g.scalar.activation(ap(out), ind(win, off), F_.Copy, scale=scale), [win, off], [out],
           size(out) * GAT)

    def act(out, a, f, scale=1.0, bias=None):
        more = {} if bias is None else {"bias": ap(bias)}
        op("a", lambda: g.scalar.activation(ap(out), ap(a), f, scale=val(scale), **more), cols(a, scale, bias), [out],
           size(out))

    def ascat(win, off, src):
        op("a", lambda: g.scalar.activation(ind(win, off), ap(src), F_.Silu), [off, src], [win], size(src) * SCA)

    def scan(out, d0, d1, init, o0, o1):
        op("v", lambda: g.vector.tensor_tensor_scan(ap(out), ap(d0), ap(d1), init, o0, o1), [d0, d1], [out], size(out))

    def iota(out, pat, base, cm, flt=True):
        more = {"allow_small_or_imprecise_dtypes": True} if flt else {}
        op("g", lambda: g.iota(ap(out), pat, base, cm, **more), [], [out], 100 + 2 * size(out))

    def fill(out, v):
        iota(out, [[0, size(out)]], v, 0)

    def select(out, src, pat, o, v, base, cm):
        op("g", lambda: g.affine_select(ap(out), ap(src), pat, o, v, base, cm), [src], [out], 150 + 2 * size(out))

    def gcopy(out, src):
        select(out, src, [[0, size(out)]], A_.is_ge, 0.0, 0, 0)

    def matmuls(out, rd, todo, shut):
        grp = [("GRP", b, b + 1) for b in banks_of([out])]

        def fn():
            ins = None
            for (o, lhs, rhs, st, sp) in todo:
                ins = g.tensor.matmul(o, lhs, rhs, st, sp)
            return ins
        n = sum(max(64, o.shape[1]) for (o, lhs, rhs, st, sp) in todo)
        op("p", fn, rd + (grp if shut else []), [out] + ([] if shut else grp),
           n * (4 if SCRATCH[rd[0][0]][2] == "float32" else 1))

    def place(out, lhs, src, start=True, stop=True, parts=128):
        cuts = [out[1]] + [b for b in range(0, 4096, 512) if out[1] < b < out[2]] + [out[2]]
        s = step(src)
        todo = [(T.PS[:, c0:c1], T[lhs[0]][0:parts, lhs[1]:lhs[2]],
                 T[src[0]][0:parts, src[1] + s * (c0 - out[1]):min(src[2], src[1] + s * (c1 - out[1])):s], start, stop)
                for c0, c1 in zip(cuts[:-1], cuts[1:])]
        matmuls(out, [lhs, src], todo, start and stop)

    slot = [0]

    def wrap(terms, parts=128, start=True, c0=None):
        n = size(terms[0][0]) // 16
        if c0 is None:
            c0 = B7 + (slot[0] if slot[0] + n <= 320 else 0)
            slot[0] = c0 - B7 + n
        out = ("PS", c0, c0 + n)
        each = [(src, em, i) for src, em, which in terms for i in which]
        todo = [(ap(out), T[em[0]][0:parts, em[1] + 15 - i:em[1] + 143 - i], T[src[0]][0:parts, src[1] + i:src[2]:16],
                 start and j == 0, j == len(each) - 1) for j, (src, em, i) in enumerate(each)]
        matmuls(out, [x for tm in terms for x in tm[:2]], todo, start)
        return out
    ALL = range(16)

    def cut(r, c, n=K):
        w = (3 * size(r) if len(r) > 3 else size(r))
        return (r[0], r[1] + c[0] * w // n, min(r[2], r[1] + c[1] * w // n)) + tuple(r[3:])

    def half(r, i, n=2):
        return cut(r, (i, i + 1), n)

    def pc(r, i):
        return cut(r, PC[i])

    def lane(n, base, k):
        return (n, base + k, base + L3, 3)

    def U(n, i=0):
        return (n, K * i, K * i + K)

    def zr(c0, n=K):
        return ("Z", c0, c0 + n)

    def cs(c, n=1):
        return ("CS", c, c + n)

    def E1(r):
        i = (ROW_F[3], ROW_FIN) + ROW_N
        return ("E1", 144 * i.index(r), 144 * i.index(r) + 144)

    def EG(r):
        i = (ROW_N + ROW_F[1:]).index(r)
        return ("EG", 144 * i, 144 * i + 144)
    IB, MVN, BN_, MVC, BC_ = [("MB", 128 * i, 128 * i + 128) for i in range(5)]
    ONE, NIB = ("MB", 640, 1152), ("MB", 1152, 1280)
    IDF, NIF = ("MF", 0, 128), ("MF", 128, 256)
    EX = [("PS", 256, 256 + K), ("PS", 1280, 1280 + K)]
    XW, XU = ("PS", 2048, 2048 + K), ("PS", 2048 + K, 2048 + L2)
    AA3 = [("PS", 1024, 1280), pc(XU, 1)]
    B7 = 3584

    def own(t, s, n=1):
        return ("LS", 192 * s + 48 * t, 192 * s + 48 * (t + n))

    def names(t, s):
        return ("LV" if t else "LS",) + own(t, s)[1:]

    def fwd(t, s):
        return ("FL", 96 * t + 48 * s, 96 * t + 48 * s + 48) if t else names(0, s)

    def nxt(t):
        return ("NL", 96 * t, 96 * t + 96)

    def pl(n, r, t):
        c = 48 * (4 * (r - 1) + t)
        return (n, c, c + 48)
    LOC = zr(Q0B, W)
    GB, IO = ("SB", 0, L2), ("D1A", 0, L2)
    VA, TH, N3, TMP = ("NVB", 0, W), ("NVB", W, 2 * W), ("NVB", W, W + L2), ("NVB", W + L2, 2 * W)
    POS, NV3 = half(TMP, 0), half(TMP, 1)
    PN = zr(Q0B)
    ST = ("BNF", 8, 8 + K)
    ZERO, V2 = ("WT", 192, 336), ("WT", 0, 144)
    KK = ("KI", 0, K)
    ROWS = [[16, 9], [1000, 16]]

    def AA(t):
        return U("AB", 2 * t)

    def BB(r, t):
        return zr(BS0) if r == 0 and t == 0 else U("AB", 2 * t + 1)

    def EA(t):
        return U("EE", 2 * t)

    def EB(t):
        return U("EE", 2 * t + 1)

    def CC(t):
        return U("C", t - 1)

    def YY(t):
        return U("YW", 2 * t)

    def WW(t):
        return U("YW", 2 * t + 1)

    def MM(t):
        return lane("Z", D0 + L3 * t, 1)

    def ones(out, pat, v, base, cm):
        select(out, cut(ZERO, (0, size(out)), 144), pat, A_.not_equal, v, base, cm)

    small = {}

    def soon(key, f, *args):
        small.setdefault(key, []).append((f, args))

    def now(key, n=9):
        for f, args in small.get(key, [])[:n]:
            f(*args)
        small[key] = small.get(key, [])[n:]

    def index(key, out, src, base):
        soon(key, ts, out, src, 0.25 - LIFT - base, None, A_.add)

    def index_n(t, out, src):
        key = "N%d" % t
        if t == 0:
            x = ("WT", 0, size(src))
            soon(key, ts, x, src, QV(1) + LIFT - 0.5, float(QA(1) - QV(1)), A_.is_gt, A_.mult)
            soon(key, tt, x, src, x, A_.add)
            src = x
        index(key, out, src, FB(t))

    def ids(t, s):
        act(XU if s and t else half(IO, s), KK, F_.Identity, cs(32 + 4 * s + t), cs(40 + 4 * s + t))

    def marks_a(t, i):
        o, a, b = half(names(t, 0), i), half(GB, i, 4), half(IO, i, 4)
        op("v", lambda: g.vector.tensor_tensor(ind(LOC, o), ap(a), ap(b), A_.max), [o, a, b], [LOC], size(a) * SCA)

    def lookup(t, s):
        agat(half(GB, s), LOC, names(t, s))
        index("F%d%d" % (t, s), fwd(t, s), wrap([(half(GB, s), E1(ROW_F[3]), ALL)], c0=None if s else EX[t % 2][1] - 48), 0)
    KEPT = {3: U("AB", 1), 2: U("AB", 6), 1: U("AB", 7), 0: U("AB", 5)}

    def lookback(t, s):
        x = zr(QV(2) + L2 * (2 - t), L2) if t else ("AB", 4 * K, 6 * K)
        agat(half(x, s), LOC, names(t, s))
        if s:
            soon("W", lambda: index_n(t, nxt(t), wrap([(x, E1(ROW_N[t]), ALL)])))

    def keep(t):
        move("s", KEPT[t], zr(QV(2) + L2 * (2 - t) + K))

    def split(t):
        act(U("G", t), KEPT[t], F_.Copy, cs(56))
        soon("G%d" % t, move, "g", KEPT[t], U("G", t), True)
        soon("G%d" % t, move, "g", U("G", t), KEPT[t])

    def compose(r, t):
        agat(U("GT"), U("G", t), pl("PP", r, t))
        if t > 0:
            index("F%d1" % t, fwd(t, 1), wrap([(U("GT"), EG(ROW_F[t]), ALL)]), 0)
        if t == 1:
            soon("F11", lambda: index_n(t, half(nxt(t), 1), wrap([(U("GT"), EG(ROW_N[t]), ALL)])))
        elif t < 3:
            index_n(t, half(nxt(t), 1), wrap([(U("GT"), EG(ROW_N[t]), ALL)]))

    def fin(part, i=0):
        w = ("PS", B7 + 320, B7 + 512)
        x, y, z = [("WT", 96 + 192 * i, 288 + 192 * i) for i in range(3)]
        if part == 0:
            wrap([(half(LOC, i), E1(ROW_FIN), ALL)], 128, True, B7 + 320 + 96 * i)
        elif part == 1:
            ts(x, w, QV(1) + LIFT - 0.5, float(QA(1) - QV(1)), A_.is_gt, A_.mult)
            ts(y, w, QV(0) + LIFT - 0.5, float(QA(0) - QV(0) - QA(1) + QV(1)), A_.is_gt, A_.mult)
            ts(z, w, QV(0) + L3 + LIFT - 0.5, float(QB(0) - L3 - QA(0)), A_.is_gt, A_.mult)
        elif part == 2:
            tt(x, w, x, A_.add)
            for i, s in enumerate((x, y, z)):
                place(w, IDF, s, i == 0, i == 2)
        else:
            ts(("FIN", 0, 192), w, 0.25 - LIFT, None, A_.add)

    def va_part(i):
        out, off = half(half(N3, 1), i), half(names(3, 1), i)
        op("v", lambda: g.vector.tensor_scalar(ap(out), ind(VA, off), -1.0, None, A_.mult), [VA, off], [out], K * GAT)

    def take_va(t, s):
        out = half(TMP if t < 3 else N3, s)
        agat(out, VA, names(t, s), -1.0)
        if t < 3:
            dma("s", T.NVD[t, :, K * s:K * s + K], ap(out), [out], [("NVD", 2 * t + s, 2 * t + s + 1)], nb(out))

    def minus_va(t, n=L2):
        z = zr(FB(t), n)
        dma("g", ap(z), T.NVD[t, :, 0:n], [("NVD", 2 * t, 2 * t + n // K), z], [z], nb(z), True)

    def negate(u):
        act(half(VA, u, 4), half(VA, u, 4), F_.Copy, -1.0)

    def factors(t):
        if t == 1:
            fill(lane("Z", D0 + L3, 0), 0)
        else:
            move("s", zr(D0 + L3 * t, L3), zr(D0 + L3, L3))
        soon("W%d" % t, gcopy, lane("Z", D0 + L3 * t, 2), WW(t))

    dma("s", T.BNI[0:32, :], T.bn[:], [], [U("BNI")], nb(U("BNI")) / 2)
    dma("a", T.ANI[:], T.an[:], [], [("ANI", 0, 192)], nb(("ANI", 0, 192)))
    for out, src in ((TH, T.th), (WW(0), T.wt), (YY(0), T.yt)):
        dma("s", ap(out), src[:], [], [out], nb(out))
    iota(("RI", 0, 4), [[0, 4]], 0, 1, False)
    iota(cs(0, 8), [[0, 2], [1, 4]], 0, 0)
    iota(cs(8, 8), [[K, 2], [L2, 4]], FB(0) + LIFT, 0)
    iota(cs(16, 8), [[L3 - 2, 2], [-W, 4]], QV(0) + LIFT + 2, 0)
    iota(cs(24, 8), [[-2, 2], [0, 4]], 3, 0)
    iota(V2, ROWS, 0, -4)
    iota(("KI", 0, K + LIFT), [[1, K + LIFT]], 0, 0)
    memset(cs(59), float(LIFT))
    ts(("RI", 0, 1), ("RI", 0, 1), 7, None, A_.bitwise_and)
    memset(cs(60), -float(LIFT))
    vcopy(cs(61), ("RI", 0, 1))
    memset(ZERO, 0.0)
    act(cs(64, 4), cs(0, 4), F_.Silu, float(K), cs(59))
    ts(cs(48, 8), cs(0, 8), cs(61), None, A_.subtract)
    ts(("RI", 1, 2), ("RI", 1, 2), 15, None, A_.bitwise_and)
    ts(cs(72, 8), cs(48, 8), -4.5, None, A_.is_lt)
    ts(cs(80, 8), cs(48, 8), -1.0, None, A_.is_equal)
    ts(cs(88, 8), cs(48, 8), -0.5, None, A_.is_gt)

    def e2(t):
        ts(("E2", 144 * t, 144 * t + 144), V2, float(15000 - 4 * t), None, A_.is_equal)
    tt(cs(72, 8), cs(72, 8), cs(80, 8), A_.add)
    tt(cs(16, 8), cs(16, 8), cs(88, 8), A_.mult)
    tt(cs(24, 8), cs(24, 8), cs(88, 8), A_.mult)
    tt(cs(8, 8), cs(8, 8), cs(72, 8), A_.mult)
    e2(1)
    tt(cs(32, 8), cs(24, 8), cs(72, 8), A_.add)
    tt(cs(40, 8), cs(8, 8), cs(16, 8), A_.add)
    e2(0)
    e2(2)
    vcopy(own(0, 0, 4), ("ANI", 0, 192))
    op("v", lambda: g.vector.tensor_scalar(T.BNF[0:32, 0:K], T.BNI[0:32, :], -float(OFF), None, A_.add),
       [U("BNI")], [U("BNF")], K)
    e2(3)

    def share(which):
        n = NE // len(which)
        send([(peer(t), [own(t, s)], names(t, s), "l%d_%d" % (s, t), n * i, n) for i, (t, s) in enumerate(which)])
    DIAG = ("WT", 336, 464)
    iota(DIAG, [[1, 128]], 0, -1)
    share([(1, 0)])
    move("s", half(LOC, 0, 4), ("KI", LIFT, LIFT + K))
    dma("s", ap(VA), T.va[:], [], [VA], nb(VA))
    for u in (1, 2):
        act(half(LOC, u, 4), KK, F_.Identity, 1.0, cs(64 + u))
    ids(0, 0)
    for t in (1, 0, 2, 3):
        wrap([(U("BNF"), ("E2", 144 * t, 144 * t + 144), ALL)], 32, True, 1024 + 48 * t if t > 1 else 48 * t)
    ts(half(LOC, 3, 4), KK, float(3 * K + LIFT), None, A_.add)
    for m, v in ((NIB, -1.0), (IDF, 1.0), (IB, 1.0)):
        ts(m, DIAG, 0.0, v, A_.is_equal, A_.mult)
    ts(own(0, 1, 2), ("PS", 0, 96), float(OFF), None, A_.add)
    ts(WW(0), WW(0), -0.125, None, A_.mult)
    vgat(zr(BS0), TH, names(0, 1))
    ts(own(2, 1, 2), ("PS", 1024 + 96, 1024 + 192), float(OFF), None, A_.add)
    ts(half(IO, 1), KK, cs(36), cs(44), A_.mult, A_.add)
    share([(1, 1)])
    send([(peer(1), [YY(0)], YY(1), "yw1", 0, NE)])
    dma("g", ap(zr(0, W)), T.th[:], [], [zr(0, W)], nb(zr(0, W)))
    ones(E1(ROW_F[3]), ROWS, 1.0, ROW_F[3] - 15000, -1)
    send([(peer(1), [WW(0)], WW(1), "yw4", 0, NE)])
    share([(2, 1), (2, 0), (3, 1), (3, 0)])
    send([(peer(2), [("YW", 0, L2)], ("YW", 2 * L2, 3 * L2), "yw2", 0, NE)])
    hand("yw5", [WW(0)])
    send([(peer(3), [YY(0)], YY(3), "yw3", 0, NE)])
    factors(1)
    now("W1")
    for r in ROW_N:
        ones(E1(r), ROWS, 1.0, r - 15000, -1)
    ones(("EH", 0, 144), ROWS, 1.0, -15000, -1)
    for c in (144, 288):
        ones(("EH", c, c + 144), ROWS, -1.0, -15000, -1)
    select(("EH", 289, 417), ("EH", 289, 417), [[16, 8], [1000, 16]], A_.not_equal, 1.0, -15000, -1)
    soon("K", vcopy, cs(62), ("RI", 1, 2))
    soon("K", ts, ("BNF", 7, 8), cs(60), 0.0, NONE, A_.mult, A_.add)
    soon("K", ts, ("WO", 0, 48), ("KI", 0, 48), 16.0, cs(62), A_.mult, A_.add)
    soon("K", ts, cs(56), cs(62), 7.5, -1.0, A_.is_gt, A_.mult)
    ones(NIF, [[1, 128]], -1.0, 0, -1)
    for rows in ((ROW_F[1], ROW_N[1]), (ROW_F[2], ROW_N[2]), (ROW_F[3], ROW_N[0])):
        for r in rows:
            soon("EG", ones, EG(r), ROWS, 1.0, r - 15000, -1)
        for r in rows:
            soon("EG", select, EG(r), EG(r), ROWS, A_.not_equal, 1.0, r + 8 - 15000, -1)
    soon("EG", ones, E1(ROW_FIN), ROWS, 1.0, ROW_FIN - 15000, -1)
    fill(MVN, int(BIG))
    fill(BN_, -33 * int(BIG) // 2)
    select(MVN, MVN, [[-16, 8], [0, 16]], A_.is_ge, 0.0, 0, 1)
    fill(ONE, 1)
    select(MVN, MVN, [[16, 8], [0, 16]], A_.is_ge, 0.0, 31, -1)
    last16 = (MVN[0], MVN[1] + 112, MVN[2])
    select(last16, last16, [[0, 16]], A_.is_ge, BIG, -16, 1)

    def forward(r, t):
        last = r == RO - 1
        Xy, Xo = EX[t % 2], EX[1 - t % 2]
        zw = TH if r == 0 and t == 0 else ("Z", 0, FB(t))
        fa, fb = fwd(t, 0), fwd(t, 1)
        A, B = AA(t), BB(r, t)
        oa, ob = zr(FB(t)), zr(FB(t) + K)
        P = MM(t) if t > 0 or last else U("D1A", 2)
        pp = pl("PP", r, 0) if r else None
        early_w = r > 0 or t != 1

        def gather(x, win, f):
            for i in range(2):
                agat(pc(x, i), win, pc(f, i))

        def m_before():
            if t > 1 or (t == 1 and last):
                tt(MM(t - 1), Xo, MM(t - 1), A_.add)
        if r == 0 and t == 0:
            ascat(LOC, fa, half(IO, 0))
        elif r == 0:
            if t == 1:
                take_va(0, 0)
            ids(t, 1)
            if t == 2:
                va_part(0)
            if t == 3:
                now("F31")
            marks_a(t, 0)
            now("F%d1" % t)
            marks_a(t, 1)
            tt(half(IO, 1), XU, half(GB, 1), A_.max)
            now("F%d0" % t)
            if t == 2:
                va_part(1)
            if t == 3:
                now("K")
            gather(B, zw, fb)
            if t != 2:
                take_va(t - 1, 1)
            gather(A, zw, fa)
        elif t:
            for i in range(3):
                agat(half(B, i, 3), zw, half(fb, i, 3))
            gather(A, zw, fa)
            m_before()
        for i in range(2):
            place(pc(Xy, i), NIB, pc(YY(t), i), True, False)
        if early_w:
            place(XW, IB, WW(t))
        for i in range(2):
            if r > 0 and t == 0:
                gtt(pc(P, i), zr(BS0), pc(pp, i), pc(A, i), A_.mult)
            elif r > 0 and i == 1:
                for j in (1, 2):
                    gtt(half(P, j, 3), zw, half(fa, j, 3), half(B, j, 3), A_.mult)
            else:
                gtt(pc(P, i), zw, pc(fa, i), pc(B, i), A_.mult)
            place(pc(Xy, i), IDF, pc(P, i), False, True)
            if i == 0 and not early_w:
                place(XW, IB, WW(t))
        if r and t:
            now("N%d" % (t % 3), 1)
        if r == 0 and t == 0:
            vgat(A, zw, fa)
            ascat(LOC, fb, half(IO, 1))
            ids(1, 0)
            lookup(1, 1)
            lookup(1, 0)
        elif r == 0:
            m_before()
            if t == 1:
                now("K", 1)
                factors(2)
                factors(3)
                now("W2")
            if t == 3:
                move("g", zr(FB(2), L2), TMP, True)
                now("W3")
                minus_va(0)
            ascat(LOC, names(t, 1), half(IO, 1))
            if t < 3:
                lookup(t + 1, 1)
                if t == 2:
                    move("s", KEPT[3], half(GB, 1))
                lookup(t + 1, 0)
                ids(t + 1, 0)
                take_va(4 - t, 0)
        elif t == 0:
            ascat(U("D1A"), pp, ("KI", LIFT, LIFT + K))
            vgat(pc(B, 0), zr(BS0), pc(pp, 0))
            agat(pc(B, 1), zr(BS0), pc(pp, 1))
            act(ST, U("D1A"), F_.Identity, 1.0, cs(60))
            soon("PI", ts, pl("PI", r, 0), wrap([(ST, ("EH", 0, 144), ALL)], c0=EX[1][1] - 48), 3.0, 2.25, A_.mult, A_.add)
        if r > 0 and t < 3:
            compose(r, t + 1)
            if t == 1:
                agat(NV3, half(N3, 1), pl("PP", r, 3))
            if t == 2:
                soon("F31", compose, r, 0)
        if r > 0 and t == 3:
            for u in (2, 1, 0):
                minus_va(u)
            if last:
                for i in range(2):
                    soon("TH", move, "g", half(zr(0, W), i), half(VA, i), True)
        if r == 1 and t == 0:
            now("G0", 1)

        def eA(i):
            tt(pc(EA(t), i), pc(Xy, i), pc(A, i), A_.mult)

        def eB(i):
            tt(pc(EB(t), i), pc(Xy, i), pc(B, i), A_.mult)

        def xa(i):
            tt(pc(XW, i), pc(EB(t), i), pc(XW, i), A_.mult)
        if t < 3:
            bout = lane("SB", 0, 2) if r else ob
            ua, ub = (pc(XU, 0), pc(XW, 1)), (pc(XW, 0), pc(XU, 1))

            def xa(i):
                tt(ua[i], pc(EB(t), i), pc(XW, i), A_.mult)

            def xb(i):
                tt(ub[i], pc(EA(t), i), pc(XW, i), A_.mult)

            def na_(i):
                tt(pc(oa, i), ua[i], pc(A, i), A_.add)

            def nb_(i):
                tt(pc(bout, i), ub[i], pc(B, i), A_.add)
            for f, i in ((eB, 0), (eA, 0), (xa, 0), (xb, 0), (na_, 0), (eA, 1), (nb_, 0), (xb, 1), (eB, 1), (nb_, 1),
                         (xa, 1)):
                if r and t == 0 and (f, i) == (nb_, 1):
                    now("PI")
                    spread("pi", r)
                    now("G0")
                    now("EG")
                f(i)
            now("F%d1" % (t + 1) if r else "K", 2 if r else int(t < 2))
            if r:
                agat(ob, ("SB", 0, L3), pl("PI", r, t))
            na_(1)
            return
        da, t2, db = [lane("D1", 0, k) for k in range(3)]
        X = U("SB", 2)
        nva, nvb = half(N3, 0), NV3 if r else half(N3, 1)

        def xb(i):
            tt(pc(X, i), pc(EA(t), i), pc(XW, i), A_.mult)
            place(pc(Xo, i), IDF, pc(B, i), True, False)
            place(pc(Xo, i), IDF, pc(X, i), False, False)
            place(pc(Xo, i), IB, pc(nvb, i), False, True)

        def na_(i):
            tt(pc(XW, i), pc(XW, i), pc(A, i), A_.add)

        def va_(i):
            tt(pc(XW, i), pc(XW, i), pc(nva, i), A_.add)

        def m_(i):
            tt(pc(P, i), pc(Xy, i), pc(P, i), A_.add)
        act(AA3[1], pc(A, 1), F_.Square)
        for f, i in ((eA, 0), (eB, 0), (xb, 0), (xa, 0), (m_, 0), (na_, 0), (eA, 1), (va_, 0), (xb, 1), (eB, 1)):
            f(i)
        act(pc(db, 0), pc(Xo, 0), F_.Copy)
        act(AA3[0], pc(A, 0), F_.Square)
        act(pc(da, 0), pc(XW, 0), F_.Copy)
        if r == 0:
            lookback(2, 0)
        m_(1)
        xa(1)
        tt(pc(t2, 0), AA3[0], pc(db, 0), A_.mult)
        na_(1)
        tt(pc(EA(t), 0), pc(Xo, 0), pc(EA(t), 0), A_.mult)
        va_(1)
        act(pc(db, 1), pc(Xo, 1), F_.Copy)
        if r == 0:
            lookback(2, 1)
            now("W")
        act(pc(da, 1), pc(XW, 1), F_.Copy)
        act(EX[1], B, F_.Square)
        if r == 0:
            keep(2)

    def backward(r, t):
        last = r == RO - 1
        more = t > 1 or (t == 1 and last)
        da, t2, db = [lane("D1", 0, k) for k in range(3)]
        d0 = zr(D0 + L3 * t, L3)
        D1, D1A, SB = ("D1", 0, L3), ("D1A", 0, L3), ("SB", 0, L3)
        zw = ("Z", FB(t), QV(2) if t == 2 else QV(1))
        na, nb_ = half(nxt(t), 0), half(nxt(t), 1)
        Xe = ("PS", 3072, 3072 + K) if last and t == 0 else XU
        Xa = XU if t == 3 else EX[0]
        Xb = XW if t == 1 and not last else EX[1]
        if not last and t == 0:
            for i in (1, 0):
                agat(pc(U("D1A"), i), zw, pc(nb_, i))
            if r == 0:
                split(0)
            else:
                agat(PN, KK, pl("PP", r, 0))
                for u in range(4):
                    negate(u)
            gtt(EB(0), zw, na, EB(0), A_.mult)
            for i in (1, 0):
                tt(pc(XU, i), pc(XU, i), pc(U("D1A"), i), A_.mult)
            for i in (1, 0):
                tt(pc(U("D1A", 1), i), pc(XU, i), pc(EB(0), i), A_.add)
            return

        def side_b(i):
            scan(pc(SB, i), pc(d0, i), pc(D1, i), 0.0, A_.mult, A_.add)

        def home(i, sem, via=None):
            srcs = [pc(EB(t), i), pc(EA(t), i)]
            send([(peer(-t), srcs, pc(CC(t), i), sem, 0, NE)])

        def second(k):
            x = (db, da)[k]
            if LANES.get((r, t), "ga")[k] == "g":
                gcopy(lane("D1A", 0, 2 * k), x)
            else:
                act(lane("D1A", 0, 2 * k), x, F_.Copy)

        def ahead():
            if t == 0:
                for s in (EB(0), EA(0), CC(1)):
                    place(XW, IDF, s, False, s == CC(1))
                return
            x = ("PS", 3072, 3072 + K) if last and t == 1 else XU
            for i in range(2):
                place(pc(x, i), IDF, pc(EA(t - 1), i))
            if t == 1 and last:
                for c in (3, 2):
                    place(XW, IDF, CC(c), c == 3, False)
        if t == 3:
            side_b(0)
            now("N0", 1)
            tt(pc(EA(t), 1), pc(EX[0], 1), pc(EA(t), 1), A_.mult)
            tt(EB(t), XW, EB(t), A_.mult)
            tt(pc(t2, 1), AA3[1], pc(db, 1), A_.mult)
            second(0)
            second(1)
            hand("c%d_3" % r, [EB(t), EA(t)])
            ahead()
            if r == 1:
                fin(0, 0)
        else:
            turn = (1, 0) if t == 1 else (0, 1)
            for i in turn:
                agat(pc(db, i), zw, pc(nb_, i))
            agat(da, zw, na)
            if t != 1:
                second(0)
            if t == 1:
                for i in turn:
                    gtt(pc(EB(t), i), zw, pc(na, i), pc(EB(t), i), A_.mult)
                for i in turn:
                    tt(pc(EA(t), i), pc(Xe, i), pc(db, i), A_.mult)
                    home(i, "c%d_%d" % (r, i))
                second(0)
                tt(t2, Xa, db, A_.mult)
            else:
                gtt(EB(t), zw, na, EB(t), A_.mult)
                for i in turn:
                    tt(pc(t2, i), pc(Xa, i), pc(db, i), A_.mult)
                    tt(pc(EA(t), i), pc(Xe, i), pc(db, i), A_.mult)
            if t == 2:
                home(1, "c%d_2" % r)
                hand("c%d_4" % r, [pc(EB(t), 0), pc(EA(t), 0)])
            second(1)
            if t == 1 and not last:
                place(pc(EX[1], 1), NIF, pc(CC(2), 1), True, False)
            else:
                ahead()
        if r == 0 and t == 1:
            now("N0", 1)
        tt(lane("D1A", 0, 1), Xb, da, A_.mult)
        if t == 1 and not last:
            ahead()
            for i in (1, 0):
                place(pc(EX[1], i), NIF, pc(CC(3), i), i == 0, False)
        if last and t == 3:
            fin(2)
        if r == 0 and t == 2:
            now("N1")
            lookback(0, 0)
            lookback(0, 1)
            now("W")
        if more:
            act(EX[0], AA(t - 1), F_.Square)
        if r == 0 and t == 3:
            lookback(1, 0)
            lookback(1, 1)
            keep(1)
            take_va(1, 0)
            take_va(1, 1)
        if more:
            act(XW if t == 2 and not last else EX[1], BB(r, t - 1), F_.Square)
        if r == 0 and t == 1:
            act(("MB", MVC[1], BC_[2]), ("MB", MVN[1], BN_[2]), F_.Copy, -1.0)
            for u in (3, 1, 2):
                split(u)
            now("G3", 1)
            now("N0", 1)
        if r == 1 and t == 2:
            fin(0, 1)
        if t == 3:
            side_b(1)
        else:
            scan(SB, d0, D1, 0.0, A_.mult, A_.add)
        if r == 0:
            gcopy(zr(QB(t)), lane("SB", 0, 2))
            if t == 1:
                for key, n in (("G1", 1), ("G2", 1), ("G3", 1), ("EG", 4), ("G1", 1), ("G2", 1)):
                    now(key, n)
                now("N0")
            if t == 3:
                move("g", zr(FB(1), L2), TMP, True)
        else:
            agat(zr(QB(t)), SB, pl("PI", r, t))
        if r == 1 and t == 1:
            factors(0)
            now("W0")
        if last and t == 2:
            now("TH")
        if r == 0 and t == 3:
            for i in (1, 0):
                scan(pc(zr(QA(t), L3), i), pc(d0, i), pc(D1A, i), 0.0, A_.mult, A_.add)
                now("N%d" % (t - 1))
                now("W")
        else:
            scan(zr(QA(t), L3), d0, D1A, 0.0, A_.mult, A_.add)
        if r and t == 3:
            now("N0", 1)
        if last and t == 2:
            fin(3)

    def vote(r):
        old = KK if r == 0 else PN
        p0, lo = U("D1A", 1), U("D1A", 2)

        def bias(x, b):
            place(x, b, cut(ONE, (0, size(x)), 512), True, False, 1)
        for x, b in ((pc(EX[0], 0), BN_), (pc(EX[0], 1), BN_), (cut(XW, (0, 512)), BC_)):
            bias(x, b)
        for c, i in ((2, 0), (1, 1), (1, 0)):
            place(pc(EX[1], i), NIF, pc(CC(c), i), False, c == 1)
        bias(cut(XW, (512, K)), BC_)
        place(("PS", 3072, 3072 + 48), IDF, ("WO", 0, 48), True, False)
        for i in (1, 0):
            tt(pc(POS, i), pc(p0, i), pc(EX[1], i), A_.is_lt)
            place(pc(EX[0], i), MVN, pc(POS, i), False, True)
        place(XW, MVC, POS, False, True)
        for i in (1, 0):
            tt(pc(lo, i), pc(EX[0], i), pc(old, i), A_.min)
        scan(ST, XW, lo, NONE, A_.min, A_.max)
        wp = wrap([(ST, ("EH", 288, 432), range(15)), (ST, ("EH", 144, 288), [15]),
                   (("BNF", 7, 7 + K), ("EH", 0, 144), [0])], 128, False, 3072)
        vcopy(cs(57), ("BNF", 7 + K, 8 + K))
        if r == 1:
            fin(1)
        ts(("WT", 672, 720), wp, -BIG, cs(57), A_.mult, A_.min)
        tt(("WO", 0, 48), wp, ("WT", 672, 720), A_.max)
        vcopy(pl("PP", r + 1, 0), ("WO", 0, 48))
        spread("pp", r + 1)

    for r in range(RO):
        for t in range(4):
            forward(r, t)
        for t in (3, 2, 1, 0):
            backward(r, t)
        if r < RO - 1:
            vote(r)

    zw = ("Z", 0, Q0B + K)
    c = 0
    for q, n in LAST:
        if n == 0:
            act(CC(2), XW, F_.Copy, -0.125)
            dma("s", T.yh[:], ap(CC(2)), [CC(2)], [], nb(CC(2)))
            continue
        o = ("AB", c, c + n)
        (vgat if q == "v" else agat)(o, zw, ("FIN", c // 16, (c + n) // 16))
        dma("s", T.yd[:, c:c + n], ap(o), [o], [], nb(o))
        c += n
    issue()
